import numpy as np
import ml_dtypes


def mxq(x, axis, fmt="e4m3"):
    dtype, down = {"e4m3": (ml_dtypes.float8_e4m3fn, 7), "e5m2": (ml_dtypes.float8_e5m2, 14)}[fmt]
    v = np.moveaxis(np.asarray(x, np.float32).astype(ml_dtypes.bfloat16).astype(np.float64), axis, -1)
    blocks = v.reshape(v.shape[:-1] + (-1, 32))
    amax = np.abs(blocks).max(-1, keepdims=True)
    byte = np.maximum(np.where(amax > 0, np.frexp(amax)[1] - 1 + 127, 0) - down, 1)
    scale = np.exp2(byte - 127.0)
    codes = (blocks / scale).astype(np.float32).astype(dtype).astype(np.float64)
    return np.moveaxis((codes * scale).reshape(v.shape), -1, axis)


WIDE = False


def mx_kscale(k):
    if not WIDE:
        return np.ones(k)
    levels = np.array([30, -30])
    if k % 512:
        return np.exp2(np.random.permutation(np.resize(levels, k // 32))).repeat(32)
    a = np.empty((k // 512, 16))
    for p in range(k // 512):
        a[p, :8] = np.random.permutation(np.resize(levels, 8))
        for g in range(8):
            far = levels[np.abs(levels - a[p, g]) >= 10]
            a[p, g + 8] = far[np.random.randint(len(far))]
    return np.exp2(a.ravel()).repeat(32)


def f64(x):
    return np.asarray(x).astype(np.float64)


E2M1 = np.array([0.0, 0.5, 1.0, 1.5, 2.0, 3.0, 4.0, 6.0, -0.0, -0.5, -1.0, -1.5, -2.0, -3.0, -4.0, -6.0])


def pack_weight(w, fmt):
    k, n = w.shape
    w = f64(np.asarray(w, np.float32).astype(ml_dtypes.bfloat16)).reshape(k // 32, 32, n)
    amax = np.abs(w).max(1)
    if fmt == "e4m3":
        byte = np.frexp(amax)[1] - 1 + 127 - 7
    else:
        mant, ex = np.frexp(amax / 6.0)
        byte = np.where(mant > 0.5, ex, ex - 1) + 127
    byte = np.clip(np.where(amax > 0, byte, 1), 1, 254)
    scaled = (w * np.exp2(127.0 - byte)[:, None, :]).reshape(k, n).astype(np.float32)
    by_word = np.ascontiguousarray(scaled.reshape(k // 512, 128, 4, n).transpose(0, 1, 3, 2))
    if fmt == "e4m3":
        words = by_word.astype(ml_dtypes.float8_e4m3fn).view(np.uint8)
    else:
        c = by_word.astype(ml_dtypes.float4_e2m1fn).view(np.uint8) & 0xF
        words = (c[..., 0::2] | (c[..., 1::2] << 4)).reshape(k // 512, 128, 2 * n)
    return np.ascontiguousarray(words), np.ascontiguousarray(byte.astype(np.uint8).reshape(k // 512, 16, n))


def unpack_weight(words, scales, fmt):
    g, _, n = scales.shape
    words = np.ascontiguousarray(words).reshape(g, 128, n, -1)
    if fmt == "e4m3":
        vals = words.view(ml_dtypes.float8_e4m3fn).astype(np.float64)
    else:
        nib = np.empty((g, 128, n, 4), np.uint8)
        nib[..., 0::2] = words & 0xF
        nib[..., 1::2] = words >> 4
        vals = E2M1[nib]
    vals = vals * np.repeat(np.exp2(scales.astype(np.float64) - 127.0), 8, axis=1)[..., None]
    return vals.transpose(0, 1, 3, 2).reshape(g * 512, n)


K, N, T = 1536, 1024, 1024


def setup_inputs():
    n = np.random.standard_normal
    s = mx_kscale(K)[:, None]
    p_w4 = pack_weight(n((K, N)) / np.sqrt(K) / s, "e2m1")
    return {
        "x": (n((K, T)) * s).astype(np.float32),
        "w4_words": p_w4[0],
        "w4_scales": p_w4[1],
    }


def reference(x, w4_words, w4_scales):
    x_q_ = mxq(f64(x), 0, "e4m3")
    x_r_ = mxq(f64(x) - x_q_, 0, "e5m2")
    w4_ = unpack_weight(w4_words, w4_scales, "e2m1")
    y = w4_.T @ x_q_ + w4_.T @ x_r_
    return y

@@ -1,0 +1,202 @@
+from contextlib import ExitStack
+
+import concourse.mybir as mybir
+from concourse.masks import make_identity
+
+K, N, T = 1536, 1024, 1024
+FLOPS = 2 * 2 * K * N * T
+
+F32 = mybir.dt.float32
+BF16 = mybir.dt.bfloat16
+I32 = mybir.dt.int32
+U32 = mybir.dt.uint32
+U8 = mybir.dt.uint8
+E4M3 = mybir.dt.float8_e4m3fn_x4
+E5M2 = mybir.dt.float8_e5m2_x4
+E2M1 = mybir.dt.float4_e2m1fn_x4
+
+P = 128
+PACK = 4
+PASSES = K // (P * PACK)
+T_TILE = 512
+N_TILES = N // P
+HALVES = T // T_TILE
+PIECE = 128
+PIECES = T_TILE // PIECE
+CHUNKS = HALVES * PASSES
+SUM_BANKS = 6
+BACK_BANKS = 2
+LINE = 4
+
+
+def slab_widths(chunk):
+    return [128, 128, 128, 128] if chunk == 0 else [256, 256]
+
+
+def piece_position(chunk, s):
+    if chunk == 0:
+        return 0
+    if chunk == 1:
+        return 7 + 2 * s
+    return 12 * chunk - 8 + 3 * s
+
+
+def tile_mix_tierx_none_kernel(tc, x, w4_words, w4_scales, out):
+    nc = tc.nc
+    with ExitStack() as ctx:
+        keep = ctx.enter_context(tc.tile_pool(name="keep", bufs=1))
+        stage = ctx.enter_context(tc.tile_pool(name="stage", bufs=6))
+        sums = ctx.enter_context(tc.psum_pool(name="sums", bufs=SUM_BANKS))
+        backs = ctx.enter_context(tc.psum_pool(name="backs", bufs=BACK_BANKS))
+        ctx.enter_context(tc.manual_schedule())
+
+        slabs = []
+        for chunk in range(CHUNKS):
+            col = 0
+            for width in slab_widths(chunk):
+                slabs.append((chunk, col, width))
+                col = col + width
+
+        w_scale = keep.tile([P, PASSES, N], U8, align_bytes=64)
+        nc.vector.memset(w_scale[:].bitcast(U32), 0)
+        w_code = [keep.tile([P, 2 * N], U8, align_bytes=64, name="w_code%d" % a) for a in range(PASSES)]
+        raw = [keep.tile([P, PACK, width], F32, align_bytes=64, name="raw%d" % i) for i, (chunk, col, width) in enumerate(slabs)]
+        rounded = [keep.tile([P, width, PACK], BF16, align_bytes=64, name="rounded%d" % i) for i, (chunk, col, width) in enumerate(slabs)]
+        rest = [keep.tile([P, width, PACK], BF16, align_bytes=64, name="rest%d" % i) for i, (chunk, col, width) in enumerate(slabs)]
+        q_code = [keep.tile([P, T_TILE], U32, align_bytes=64, name="q_code%d" % c) for c in range(CHUNKS)]
+        q_scale = [keep.tile([P, T_TILE], U8, align_bytes=64, name="q_scale%d" % c) for c in range(CHUNKS)]
+        r_code = [keep.tile([P, T_TILE], U32, align_bytes=64, name="r_code%d" % c) for c in range(CHUNKS)]
+        r_scale = [keep.tile([P, T_TILE], U8, align_bytes=64, name="r_scale%d" % c) for c in range(CHUNKS)]
+
+        scale_rows = w4_scales.bitcast(I32).rearrange("a (q r) n -> r q a n", r=4)
+
+        def load_scales(a0, a1):
+            for r in range(4):
+                nc.sync.dma_start(out=w_scale[:].bitcast(I32)[r:P:32, a0:a1, :], in_=scale_rows[r, :, a0:a1, :])
+
+        for i, (chunk, col, width) in enumerate(slabs):
+            half, a = divmod(chunk, PASSES)
+            t0 = half * T_TILE + col
+            rows = x[a * P * PACK : (a + 1) * P * PACK, t0 : t0 + width]
+            nc.sync.dma_start(out=raw[i][:], in_=rows.rearrange("(p j) t -> p j t", j=PACK))
+            if col + width == T_TILE and half == 0:
+                if a == 0:
+                    load_scales(0, 1)
+                nc.sync.dma_start(out=w_code[a][:].bitcast(I32), in_=w4_words[a].bitcast(I32))
+                if a == 1:
+                    load_scales(1, PASSES)
+
+        eye = keep.tile([P, P], BF16)
+        make_identity(nc, eye[:])
+        eye_rows = keep.tile([P, PACK, P, PACK], BF16, align_bytes=64)
+        nc.vector.memset(eye_rows[:].rearrange("p j m i -> p (j m i)").bitcast(U32), 0)
+        for j in range(PACK):
+            nc.vector.tensor_copy(out=eye_rows[:, j, :, j], in_=eye[:])
+        eye_code = keep.tile([P, PACK * P], U32, align_bytes=64)
+        eye_scale = keep.tile([P, PACK * P], U8, align_bytes=64)
+        nc.vector.quantize_mx(
+            out=eye_code[:].bitcast(E4M3), scales=eye_scale[:], in_=eye_rows[:].rearrange("p j m i -> p (j m i)")
+        )
+
+        for i in range(len(slabs)):
+            nc.scalar.copy(
+                out=rounded[i][:].rearrange("p (c i) j -> p c j i", i=LINE),
+                in_=raw[i][:].rearrange("p j (c i) -> p c j i", i=LINE),
+            )
+
+        def quantise_first(i):
+            chunk, col, width = slabs[i]
+            nc.vector.quantize_mx(
+                out=q_code[chunk][:, col : col + width].bitcast(E4M3),
+                scales=q_scale[chunk][:, col : col + width],
+                in_=rounded[i][:].rearrange("p t j -> p (t j)"),
+            )
+
+        def quantise_rest(i):
+            chunk, col, width = slabs[i]
+            nc.vector.quantize_mx(
+                out=r_code[chunk][:, col : col + width].bitcast(E5M2),
+                scales=r_scale[chunk][:, col : col + width],
+                in_=rest[i][:].rearrange("p t j -> p (t j)"),
+            )
+
+        state = {"q": 0, "r": 0}
+
+        def slab_of(chunk, s):
+            for i, (c, col, width) in enumerate(slabs):
+                if c == chunk and col <= s * PIECE < col + width:
+                    return i
+
+        def piece(chunk, s):
+            i = slab_of(chunk, s)
+            col, width = slabs[i][1], slabs[i][2]
+            while state["q"] <= i:
+                quantise_first(state["q"])
+                state["q"] = state["q"] + 1
+            cols = slice(s * PIECE, (s + 1) * PIECE)
+            back = backs.tile([P, PACK, PIECE], F32)
+            for j in range(PACK):
+                nc.tensor.matmul_mx(
+                    out=back[:, j, :],
+                    lhsT=eye_code[:, j * P : (j + 1) * P].bitcast(E4M3),
+                    lhsT_scale=eye_scale[:, j * P : (j + 1) * P],
+                    rhs=q_code[chunk][:, cols].bitcast(E4M3),
+                    rhs_scale=q_scale[chunk][:, cols],
+                    start=True,
+                    stop=True,
+                )
+            last_of_slab = (s + 1) * PIECE == col + width
+            last_of_chunk = s == PIECES - 1
+            if last_of_slab and i + 1 < len(slabs) and not (last_of_chunk and chunk == 0):
+                quantise_first(i + 1)
+                state["q"] = i + 2
+            local = slice(s * PIECE - col, (s + 1) * PIECE - col)
+            nc.vector.tensor_tensor(
+                out=rest[i][:, local, :].rearrange("p (c i) j -> p c j i", i=LINE),
+                in0=raw[i][:, :, local].rearrange("p j (c i) -> p c j i", i=LINE),
+                in1=back[:].rearrange("p j (c i) -> p c j i", i=LINE),
+                op=mybir.AluOpType.subtract,
+            )
+            upto = i + 1 if last_of_chunk else i
+            while state["r"] < upto:
+                quantise_rest(state["r"])
+                state["r"] = state["r"] + 1
+
+        waves = [[(0, n) for n in range(SUM_BANKS)], [(0, n) for n in range(SUM_BANKS, N_TILES)]]
+        waves.append([(1, n) for n in range(4)])
+        waves.extend([[(1, n)] for n in range(4, N_TILES)])
+        placed = {}
+        for chunk in range(CHUNKS):
+            for s in range(PIECES):
+                placed.setdefault(piece_position(chunk, s), []).append((chunk, s))
+
+        step = 0
+        for wave in waves:
+            acc = {}
+            for a in range(PASSES):
+                for tier in range(2):
+                    for half, n in wave:
+                        for chunk, s in placed.get(step, []):
+                            piece(chunk, s)
+                        step = step + 1
+                        chunk = half * PASSES + a
+                        if a == 0 and tier == 0:
+                            acc[n] = sums.tile([P, T_TILE], F32, name="acc")
+                        last = a == PASSES - 1 and tier == 1
+                        nc.tensor.matmul_mx(
+                            out=acc[n][:],
+                            lhsT=w_code[a][:, 2 * n * P : 2 * (n + 1) * P].bitcast(E2M1),
+                            lhsT_scale=w_scale[:, a, n * P : (n + 1) * P],
+                            rhs=q_code[chunk][:].bitcast(E4M3) if tier == 0 else r_code[chunk][:].bitcast(E5M2),
+                            rhs_scale=q_scale[chunk][:] if tier == 0 else r_scale[chunk][:],
+                            start=(a == 0 and tier == 0),
+                            stop=last,
+                        )
+                        if last:
+                            parts = 2 if (half, n) == (HALVES - 1, N_TILES - 1) else 1
+                            width = T_TILE // parts
+                            for part in range(parts):
+                                result = stage.tile([P, width], F32, name="result")
+                                nc.scalar.copy(out=result[:], in_=acc[n][:, part * width : (part + 1) * width])
+                                t0 = half * T_TILE + part * width
+                                nc.sync.dma_start(out=out[n * P : (n + 1) * P, t0 : t0 + width], in_=result[:])

@@ -1,7 +1,6 @@
 from contextlib import ExitStack
 
 import concourse.mybir as mybir
-from concourse.masks import make_identity
 
 K, N, T = 1536, 1024, 1024
 FLOPS = 2 * 2 * K * N * T
@@ -26,7 +25,12 @@ PIECES = T_TILE // PIECE
 CHUNKS = HALVES * PASSES
 SUM_BANKS = 6
 BACK_BANKS = 2
-LINE = 4
+RUN = 2
+WARM = 0
+
+
+def load_widths(chunk):
+    return [256, 256] if chunk < PASSES else [512]
 
 
 def slab_widths(chunk):
@@ -34,33 +38,38 @@ def slab_widths(chunk):
 
 
 def piece_position(chunk, s):
-    if chunk == 0:
-        return 0
-    if chunk == 1:
-        return 7 + 2 * s
-    return 12 * chunk - 8 + 3 * s
+    half, a = divmod(chunk, PASSES)
+    first = half * N_TILES * PASSES * 2 + a * SUM_BANKS * 2
+    lead = 5 if chunk == 1 else 6
+    return max(0, first - lead + 2 * s) if chunk > 0 else 0
+
+
+def cut(widths_of):
+    parts = []
+    for chunk in range(CHUNKS):
+        col = 0
+        for width in widths_of(chunk):
+            parts.append((chunk, col, width))
+            col = col + width
+    return parts
 
 
 def tile_mix_tierx_none_kernel(tc, x, w4_words, w4_scales, out):
     nc = tc.nc
     with ExitStack() as ctx:
         keep = ctx.enter_context(tc.tile_pool(name="keep", bufs=1))
-        stage = ctx.enter_context(tc.tile_pool(name="stage", bufs=6))
+        stage = ctx.enter_context(tc.tile_pool(name="stage", bufs=17))
         sums = ctx.enter_context(tc.psum_pool(name="sums", bufs=SUM_BANKS))
         backs = ctx.enter_context(tc.psum_pool(name="backs", bufs=BACK_BANKS))
         ctx.enter_context(tc.manual_schedule())
 
-        slabs = []
-        for chunk in range(CHUNKS):
-            col = 0
-            for width in slab_widths(chunk):
-                slabs.append((chunk, col, width))
-                col = col + width
+        loads = cut(load_widths)
+        slabs = cut(slab_widths)
 
         w_scale = keep.tile([P, PASSES, N], U8, align_bytes=64)
         nc.vector.memset(w_scale[:].bitcast(U32), 0)
         w_code = [keep.tile([P, 2 * N], U8, align_bytes=64, name="w_code%d" % a) for a in range(PASSES)]
-        raw = [keep.tile([P, PACK, width], F32, align_bytes=64, name="raw%d" % i) for i, (chunk, col, width) in enumerate(slabs)]
+        raw = [keep.tile([P, PACK, width], F32, align_bytes=64, name="raw%d" % i) for i, (chunk, col, width) in enumerate(loads)]
         rounded = [keep.tile([P, width, PACK], BF16, align_bytes=64, name="rounded%d" % i) for i, (chunk, col, width) in enumerate(slabs)]
         rest = [keep.tile([P, width, PACK], BF16, align_bytes=64, name="rest%d" % i) for i, (chunk, col, width) in enumerate(slabs)]
         q_code = [keep.tile([P, T_TILE], U32, align_bytes=64, name="q_code%d" % c) for c in range(CHUNKS)]
@@ -74,7 +83,7 @@ def tile_mix_tierx_none_kernel(tc, x, w4_words, w4_scales, out):
             for r in range(4):
                 nc.sync.dma_start(out=w_scale[:].bitcast(I32)[r:P:32, a0:a1, :], in_=scale_rows[r, :, a0:a1, :])
 
-        for i, (chunk, col, width) in enumerate(slabs):
+        for i, (chunk, col, width) in enumerate(loads):
             half, a = divmod(chunk, PASSES)
             t0 = half * T_TILE + col
             rows = x[a * P * PACK : (a + 1) * P * PACK, t0 : t0 + width]
@@ -86,23 +95,49 @@ def tile_mix_tierx_none_kernel(tc, x, w4_words, w4_scales, out):
                 if a == 1:
                     load_scales(1, PASSES)
 
-        eye = keep.tile([P, P], BF16)
-        make_identity(nc, eye[:])
-        eye_rows = keep.tile([P, PACK, P, PACK], BF16, align_bytes=64)
-        nc.vector.memset(eye_rows[:].rearrange("p j m i -> p (j m i)").bitcast(U32), 0)
+        def raw_columns(chunk, col, width):
+            for i, (c, first, loaded) in enumerate(loads):
+                if c == chunk and first <= col < first + loaded:
+                    return raw[i][:, :, col - first : col - first + width].rearrange("p j (c i) -> p c j i", i=RUN)
+
+        marks = keep.tile([P, PACK * P + PACK], BF16)
+        nc.gpsimd.memset(marks[:].bitcast(U32), 0)
+        nc.gpsimd.affine_select(
+            out=marks[:],
+            in_=marks[:],
+            compare_op=mybir.AluOpType.not_equal,
+            fill=1.0,
+            base=PACK - 1,
+            pattern=[[-1, PACK * P + PACK]],
+            channel_multiplier=PACK,
+        )
+        eye_rows = keep.tile([P, PACK, PACK * P], BF16, align_bytes=64)
         for j in range(PACK):
-            nc.vector.tensor_copy(out=eye_rows[:, j, :, j], in_=eye[:])
+            nc.vector.tensor_copy(out=eye_rows[:, j, :], in_=marks[:, PACK - 1 - j : PACK - 1 - j + PACK * P])
         eye_code = keep.tile([P, PACK * P], U32, align_bytes=64)
         eye_scale = keep.tile([P, PACK * P], U8, align_bytes=64)
         nc.vector.quantize_mx(
-            out=eye_code[:].bitcast(E4M3), scales=eye_scale[:], in_=eye_rows[:].rearrange("p j m i -> p (j m i)")
+            out=eye_code[:].bitcast(E4M3), scales=eye_scale[:], in_=eye_rows[:].rearrange("p j f -> p (j f)")
         )
-
-        for i in range(len(slabs)):
-            nc.scalar.copy(
-                out=rounded[i][:].rearrange("p (c i) j -> p c j i", i=LINE),
-                in_=raw[i][:].rearrange("p j (c i) -> p c j i", i=LINE),
+        for i in range(WARM):
+            warm = sums.tile([P, T_TILE], F32, name="acc")
+            nc.tensor.matmul_mx(
+                out=warm[:],
+                lhsT=eye_code[:, 0:P].bitcast(E4M3),
+                lhsT_scale=eye_scale[:, 0:P],
+                rhs=eye_code[:].bitcast(E4M3),
+                rhs_scale=eye_scale[:],
+                start=True,
+                stop=True,
             )
+
+        def round_chunk(chunk):
+            for i, (c, col, width) in enumerate(slabs):
+                if c == chunk:
+                    nc.scalar.copy(
+                        out=rounded[i][:].rearrange("p (c i) j -> p c j i", i=RUN),
+                        in_=raw_columns(chunk, col, width),
+                    )
 
         def quantise_first(i):
             chunk, col, width = slabs[i]
@@ -127,12 +162,15 @@ def tile_mix_tierx_none_kernel(tc, x, w4_words, w4_scales, out):
                 if c == chunk and col <= s * PIECE < col + width:
                     return i
 
+        def first_upto(i):
+            while state["q"] <= min(i, len(slabs) - 1):
+                quantise_first(state["q"])
+                state["q"] = state["q"] + 1
+
         def piece(chunk, s):
             i = slab_of(chunk, s)
             col, width = slabs[i][1], slabs[i][2]
-            while state["q"] <= i:
-                quantise_first(state["q"])
-                state["q"] = state["q"] + 1
+            first_upto(i)
             cols = slice(s * PIECE, (s + 1) * PIECE)
             back = backs.tile([P, PACK, PIECE], F32)
             for j in range(PACK):
@@ -147,28 +185,31 @@ def tile_mix_tierx_none_kernel(tc, x, w4_words, w4_scales, out):
                 )
             last_of_slab = (s + 1) * PIECE == col + width
             last_of_chunk = s == PIECES - 1
-            if last_of_slab and i + 1 < len(slabs) and not (last_of_chunk and chunk == 0):
-                quantise_first(i + 1)
-                state["q"] = i + 2
+            if last_of_slab and not last_of_chunk:
+                first_upto(i + 1)
             local = slice(s * PIECE - col, (s + 1) * PIECE - col)
             nc.vector.tensor_tensor(
-                out=rest[i][:, local, :].rearrange("p (c i) j -> p c j i", i=LINE),
-                in0=raw[i][:, :, local].rearrange("p j (c i) -> p c j i", i=LINE),
-                in1=back[:].rearrange("p j (c i) -> p c j i", i=LINE),
+                out=rest[i][:, local, :].rearrange("p (c i) j -> p c j i", i=RUN),
+                in0=raw_columns(chunk, s * PIECE, PIECE),
+                in1=back[:].rearrange("p j (c i) -> p c j i", i=RUN),
                 op=mybir.AluOpType.subtract,
             )
+            if last_of_chunk and chunk >= 3:
+                first_upto(i + 1)
             upto = i + 1 if last_of_chunk else i
             while state["r"] < upto:
                 quantise_rest(state["r"])
                 state["r"] = state["r"] + 1
 
-        waves = [[(0, n) for n in range(SUM_BANKS)], [(0, n) for n in range(SUM_BANKS, N_TILES)]]
-        waves.append([(1, n) for n in range(4)])
-        waves.extend([[(1, n)] for n in range(4, N_TILES)])
+        waves = []
+        for half in range(HALVES):
+            waves.append([(half, n) for n in range(SUM_BANKS)])
+            waves.extend([[(half, n)] for n in range(SUM_BANKS, N_TILES)])
         placed = {}
         for chunk in range(CHUNKS):
             for s in range(PIECES):
                 placed.setdefault(piece_position(chunk, s), []).append((chunk, s))
+        rounding = {0: [0, 1, 2, 3], 36: [4], 48: [5]}
 
         step = 0
         for wave in waves:
@@ -176,6 +217,8 @@ def tile_mix_tierx_none_kernel(tc, x, w4_words, w4_scales, out):
             for a in range(PASSES):
                 for tier in range(2):
                     for half, n in wave:
+                        for chunk in rounding.get(step, []):
+                            round_chunk(chunk)
                         for chunk, s in placed.get(step, []):
                             piece(chunk, s)
                         step = step + 1
@@ -197,6 +240,10 @@ def tile_mix_tierx_none_kernel(tc, x, w4_words, w4_scales, out):
                             width = T_TILE // parts
                             for part in range(parts):
                                 result = stage.tile([P, width], F32, name="result")
-                                nc.scalar.copy(out=result[:], in_=acc[n][:, part * width : (part + 1) * width])
+                                source = acc[n][:, part * width : (part + 1) * width]
+                                if len(wave) > 1 and n % 2 == 0:
+                                    nc.vector.tensor_copy(out=result[:], in_=source)
+                                else:
+                                    nc.scalar.copy(out=result[:], in_=source)
                                 t0 = half * T_TILE + part * width
                                 nc.sync.dma_start(out=out[n * P : (n + 1) * P, t0 : t0 + width], in_=result[:])

@@ -40,8 +40,15 @@ def slab_widths(chunk):
 def piece_position(chunk, s):
     half, a = divmod(chunk, PASSES)
     first = half * N_TILES * PASSES * 2 + a * SUM_BANKS * 2
-    lead = 5 if chunk == 1 else 6
-    return max(0, first - lead + 2 * s) if chunk > 0 else 0
+    return first - 6 + 2 * s if half == 0 else first - 12 + 3 * s
+
+
+def quantise_position(chunk):
+    return piece_position(chunk, 0) - (0 if chunk < PASSES else 4)
+
+
+def round_position(chunk):
+    return piece_position(chunk - 1, 0)
 
 
 def cut(widths_of):
@@ -155,22 +162,10 @@ def tile_mix_tierx_none_kernel(tc, x, w4_words, w4_scales, out):
                 in_=rest[i][:].rearrange("p t j -> p (t j)"),
             )
 
-        state = {"q": 0, "r": 0}
+        def slabs_of(chunk):
+            return [i for i, slab in enumerate(slabs) if slab[0] == chunk]
 
-        def slab_of(chunk, s):
-            for i, (c, col, width) in enumerate(slabs):
-                if c == chunk and col <= s * PIECE < col + width:
-                    return i
-
-        def first_upto(i):
-            while state["q"] <= min(i, len(slabs) - 1):
-                quantise_first(state["q"])
-                state["q"] = state["q"] + 1
-
-        def piece(chunk, s):
-            i = slab_of(chunk, s)
-            col, width = slabs[i][1], slabs[i][2]
-            first_upto(i)
+        def read_back(chunk, s):
             cols = slice(s * PIECE, (s + 1) * PIECE)
             back = backs.tile([P, PACK, PIECE], F32)
             for j in range(PACK):
@@ -183,33 +178,49 @@ def tile_mix_tierx_none_kernel(tc, x, w4_words, w4_scales, out):
                     start=True,
                     stop=True,
                 )
-            last_of_slab = (s + 1) * PIECE == col + width
-            last_of_chunk = s == PIECES - 1
-            if last_of_slab and not last_of_chunk:
-                first_upto(i + 1)
-            local = slice(s * PIECE - col, (s + 1) * PIECE - col)
+            return back
+
+        def subtract(chunk, s, back):
+            i = [i for i in slabs_of(chunk) if slabs[i][1] <= s * PIECE][-1]
+            local = slice(s * PIECE - slabs[i][1], (s + 1) * PIECE - slabs[i][1])
             nc.vector.tensor_tensor(
                 out=rest[i][:, local, :].rearrange("p (c i) j -> p c j i", i=RUN),
                 in0=raw_columns(chunk, s * PIECE, PIECE),
                 in1=back[:].rearrange("p j (c i) -> p c j i", i=RUN),
                 op=mybir.AluOpType.subtract,
             )
-            if last_of_chunk and chunk >= 3:
-                first_upto(i + 1)
-            upto = i + 1 if last_of_chunk else i
-            while state["r"] < upto:
-                quantise_rest(state["r"])
-                state["r"] = state["r"] + 1
+
+        for chunk in range(PASSES + 1):
+            round_chunk(chunk)
+        quantise_first(0)
+        for s in range(PIECES):
+            back = read_back(0, s)
+            if s + 1 < PIECES:
+                quantise_first(s + 1)
+            subtract(0, s, back)
+            if s > 0:
+                quantise_rest(s - 1)
+        quantise_rest(PIECES - 1)
+
+        def side_work(step):
+            for chunk in range(1, CHUNKS):
+                if chunk > PASSES and step == round_position(chunk):
+                    round_chunk(chunk)
+                if step == quantise_position(chunk):
+                    for i in slabs_of(chunk):
+                        quantise_first(i)
+            for chunk in range(1, CHUNKS):
+                for s in range(PIECES):
+                    if step == piece_position(chunk, s):
+                        subtract(chunk, s, read_back(chunk, s))
+                        if s == PIECES - 1:
+                            for i in slabs_of(chunk):
+                                quantise_rest(i)
 
         waves = []
         for half in range(HALVES):
             waves.append([(half, n) for n in range(SUM_BANKS)])
             waves.extend([[(half, n)] for n in range(SUM_BANKS, N_TILES)])
-        placed = {}
-        for chunk in range(CHUNKS):
-            for s in range(PIECES):
-                placed.setdefault(piece_position(chunk, s), []).append((chunk, s))
-        rounding = {0: [0, 1, 2, 3], 36: [4], 48: [5]}
 
         step = 0
         for wave in waves:
@@ -217,10 +228,7 @@ def tile_mix_tierx_none_kernel(tc, x, w4_words, w4_scales, out):
             for a in range(PASSES):
                 for tier in range(2):
                     for half, n in wave:
-                        for chunk in rounding.get(step, []):
-                            round_chunk(chunk)
-                        for chunk, s in placed.get(step, []):
-                            piece(chunk, s)
+                        side_work(step)
                         step = step + 1
                         chunk = half * PASSES + a
                         if a == 0 and tier == 0:

@@ -24,6 +24,7 @@ PIECE = 128
 PIECES = T_TILE // PIECE
 CHUNKS = HALVES * PASSES
 SUM_BANKS = 6
+WAVE = (6, 5)
 BACK_BANKS = 2
 RUN = 2
 WARM = 0
@@ -39,16 +40,16 @@ def slab_widths(chunk):
 
 def piece_position(chunk, s):
     half, a = divmod(chunk, PASSES)
-    first = half * N_TILES * PASSES * 2 + a * SUM_BANKS * 2
+    first = half * N_TILES * PASSES * 2 + a * WAVE[half] * 2
     return first - 6 + 2 * s if half == 0 else first - 12 + 3 * s
 
 
 def quantise_position(chunk):
-    return piece_position(chunk, 0) - (0 if chunk < PASSES else 4)
+    return piece_position(chunk, 0) - (0 if chunk < PASSES else 6)
 
 
 def round_position(chunk):
-    return piece_position(chunk - 1, 0)
+    return WAVE[0] * PASSES * 2
 
 
 def cut(widths_of):
@@ -96,11 +97,8 @@ def tile_mix_tierx_none_kernel(tc, x, w4_words, w4_scales, out):
             rows = x[a * P * PACK : (a + 1) * P * PACK, t0 : t0 + width]
             nc.sync.dma_start(out=raw[i][:], in_=rows.rearrange("(p j) t -> p j t", j=PACK))
             if col + width == T_TILE and half == 0:
-                if a == 0:
-                    load_scales(0, 1)
+                load_scales(a, a + 1)
                 nc.sync.dma_start(out=w_code[a][:].bitcast(I32), in_=w4_words[a].bitcast(I32))
-                if a == 1:
-                    load_scales(1, PASSES)
 
         def raw_columns(chunk, col, width):
             for i, (c, first, loaded) in enumerate(loads):
@@ -190,21 +188,21 @@ def tile_mix_tierx_none_kernel(tc, x, w4_words, w4_scales, out):
                 op=mybir.AluOpType.subtract,
             )
 
-        for chunk in range(PASSES + 1):
+        for chunk in range(CHUNKS - 1):
             round_chunk(chunk)
         quantise_first(0)
+        quantise_first(1)
         for s in range(PIECES):
-            back = read_back(0, s)
-            if s + 1 < PIECES:
-                quantise_first(s + 1)
-            subtract(0, s, back)
+            subtract(0, s, read_back(0, s))
+            if s + 2 < PIECES:
+                quantise_first(s + 2)
             if s > 0:
                 quantise_rest(s - 1)
         quantise_rest(PIECES - 1)
 
         def side_work(step):
             for chunk in range(1, CHUNKS):
-                if chunk > PASSES and step == round_position(chunk):
+                if chunk == CHUNKS - 1 and step == round_position(chunk):
                     round_chunk(chunk)
                 if step == quantise_position(chunk):
                     for i in slabs_of(chunk):
@@ -219,8 +217,8 @@ def tile_mix_tierx_none_kernel(tc, x, w4_words, w4_scales, out):
 
         waves = []
         for half in range(HALVES):
-            waves.append([(half, n) for n in range(SUM_BANKS)])
-            waves.extend([[(half, n)] for n in range(SUM_BANKS, N_TILES)])
+            waves.append([(half, n) for n in range(WAVE[half])])
+            waves.extend([[(half, n)] for n in range(WAVE[half], N_TILES)])
 
         step = 0
         for wave in waves:

@@ -27,7 +27,7 @@ SUM_BANKS = 6
 WAVE = (6, 5)
 BACK_BANKS = 2
 RUN = 2
-WARM = 0
+WARM = 2
 
 
 def load_widths(chunk):
@@ -124,7 +124,8 @@ def tile_mix_tierx_none_kernel(tc, x, w4_words, w4_scales, out):
         nc.vector.quantize_mx(
             out=eye_code[:].bitcast(E4M3), scales=eye_scale[:], in_=eye_rows[:].rearrange("p j f -> p (j f)")
         )
-        for i in range(WARM):
+
+        def warm_up():
             warm = sums.tile([P, T_TILE], F32, name="acc")
             nc.tensor.matmul_mx(
                 out=warm[:],
@@ -135,6 +136,9 @@ def tile_mix_tierx_none_kernel(tc, x, w4_words, w4_scales, out):
                 start=True,
                 stop=True,
             )
+
+        for i in range(WARM):
+            warm_up()
 
         def round_chunk(chunk):
             for i, (c, col, width) in enumerate(slabs):
@@ -194,6 +198,8 @@ def tile_mix_tierx_none_kernel(tc, x, w4_words, w4_scales, out):
         quantise_first(1)
         for s in range(PIECES):
             subtract(0, s, read_back(0, s))
+            if s == 1:
+                warm_up()
             if s + 2 < PIECES:
                 quantise_first(s + 2)
             if s > 0:

@@ -23,11 +23,9 @@ HALVES = T // T_TILE
 PIECE = 128
 PIECES = T_TILE // PIECE
 CHUNKS = HALVES * PASSES
-SUM_BANKS = 6
-WAVE = (6, 5)
-BACK_BANKS = 2
+WAVE = 6
 RUN = 2
-WARM = 2
+BACK_PACE = 3
 
 
 def load_widths(chunk):
@@ -35,21 +33,13 @@ def load_widths(chunk):
 
 
 def slab_widths(chunk):
+    if chunk == 0:
+        return [128, 128, 128, 128]
+    return [256, 128, 128] if chunk < PASSES else [256, 256]
+
+
+def rest_widths(chunk):
     return [128, 128, 128, 128] if chunk == 0 else [256, 256]
-
-
-def piece_position(chunk, s):
-    half, a = divmod(chunk, PASSES)
-    first = half * N_TILES * PASSES * 2 + a * WAVE[half] * 2
-    return first - 6 + 2 * s if half == 0 else first - 12 + 3 * s
-
-
-def quantise_position(chunk):
-    return piece_position(chunk, 0) - (0 if chunk < PASSES else 6)
-
-
-def round_position(chunk):
-    return WAVE[0] * PASSES * 2
 
 
 def cut(widths_of):
@@ -67,19 +57,19 @@ def tile_mix_tierx_none_kernel(tc, x, w4_words, w4_scales, out):
     with ExitStack() as ctx:
         keep = ctx.enter_context(tc.tile_pool(name="keep", bufs=1))
         stage = ctx.enter_context(tc.tile_pool(name="stage", bufs=17))
-        sums = ctx.enter_context(tc.psum_pool(name="sums", bufs=SUM_BANKS))
-        backs = ctx.enter_context(tc.psum_pool(name="backs", bufs=BACK_BANKS))
+        psum = ctx.enter_context(tc.psum_pool(name="psum", bufs=1))
         ctx.enter_context(tc.manual_schedule())
 
         loads = cut(load_widths)
         slabs = cut(slab_widths)
+        rests = cut(rest_widths)
 
         w_scale = keep.tile([P, PASSES, N], U8, align_bytes=64)
         nc.vector.memset(w_scale[:].bitcast(U32), 0)
         w_code = [keep.tile([P, 2 * N], U8, align_bytes=64, name="w_code%d" % a) for a in range(PASSES)]
         raw = [keep.tile([P, PACK, width], F32, align_bytes=64, name="raw%d" % i) for i, (chunk, col, width) in enumerate(loads)]
         rounded = [keep.tile([P, width, PACK], BF16, align_bytes=64, name="rounded%d" % i) for i, (chunk, col, width) in enumerate(slabs)]
-        rest = [keep.tile([P, width, PACK], BF16, align_bytes=64, name="rest%d" % i) for i, (chunk, col, width) in enumerate(slabs)]
+        rest = [keep.tile([P, width, PACK], BF16, align_bytes=64, name="rest%d" % i) for i, (chunk, col, width) in enumerate(rests)]
         q_code = [keep.tile([P, T_TILE], U32, align_bytes=64, name="q_code%d" % c) for c in range(CHUNKS)]
         q_scale = [keep.tile([P, T_TILE], U8, align_bytes=64, name="q_scale%d" % c) for c in range(CHUNKS)]
         r_code = [keep.tile([P, T_TILE], U32, align_bytes=64, name="r_code%d" % c) for c in range(CHUNKS)]
@@ -125,30 +115,18 @@ def tile_mix_tierx_none_kernel(tc, x, w4_words, w4_scales, out):
             out=eye_code[:].bitcast(E4M3), scales=eye_scale[:], in_=eye_rows[:].rearrange("p j f -> p (j f)")
         )
 
-        def warm_up():
-            warm = sums.tile([P, T_TILE], F32, name="acc")
-            nc.tensor.matmul_mx(
-                out=warm[:],
-                lhsT=eye_code[:, 0:P].bitcast(E4M3),
-                lhsT_scale=eye_scale[:, 0:P],
-                rhs=eye_code[:].bitcast(E4M3),
-                rhs_scale=eye_scale[:],
-                start=True,
-                stop=True,
+        def parts_of(parts, chunk):
+            return [i for i, part in enumerate(parts) if part[0] == chunk]
+
+        def round_slab(i):
+            chunk, col, width = slabs[i]
+            nc.scalar.copy(
+                out=rounded[i][:].rearrange("p (c i) j -> p c j i", i=RUN),
+                in_=raw_columns(chunk, col, width),
             )
 
-        for i in range(WARM):
-            warm_up()
-
-        def round_chunk(chunk):
-            for i, (c, col, width) in enumerate(slabs):
-                if c == chunk:
-                    nc.scalar.copy(
-                        out=rounded[i][:].rearrange("p (c i) j -> p c j i", i=RUN),
-                        in_=raw_columns(chunk, col, width),
-                    )
-
-        def quantise_first(i):
+        def quantise_first(chunk, part):
+            i = parts_of(slabs, chunk)[part]
             chunk, col, width = slabs[i]
             nc.vector.quantize_mx(
                 out=q_code[chunk][:, col : col + width].bitcast(E4M3),
@@ -156,23 +134,21 @@ def tile_mix_tierx_none_kernel(tc, x, w4_words, w4_scales, out):
                 in_=rounded[i][:].rearrange("p t j -> p (t j)"),
             )
 
-        def quantise_rest(i):
-            chunk, col, width = slabs[i]
+        def quantise_rest(chunk, part):
+            i = parts_of(rests, chunk)[part]
+            chunk, col, width = rests[i]
             nc.vector.quantize_mx(
                 out=r_code[chunk][:, col : col + width].bitcast(E5M2),
                 scales=r_scale[chunk][:, col : col + width],
                 in_=rest[i][:].rearrange("p t j -> p (t j)"),
             )
 
-        def slabs_of(chunk):
-            return [i for i, slab in enumerate(slabs) if slab[0] == chunk]
-
-        def read_back(chunk, s):
+        def leftover(chunk, s, bank):
             cols = slice(s * PIECE, (s + 1) * PIECE)
-            back = backs.tile([P, PACK, PIECE], F32)
+            back = psum.tile([P, T_TILE], F32, name="bank%d" % bank)
             for j in range(PACK):
                 nc.tensor.matmul_mx(
-                    out=back[:, j, :],
+                    out=back[:, j * PIECE : (j + 1) * PIECE],
                     lhsT=eye_code[:, j * P : (j + 1) * P].bitcast(E4M3),
                     lhsT_scale=eye_scale[:, j * P : (j + 1) * P],
                     rhs=q_code[chunk][:, cols].bitcast(E4M3),
@@ -180,82 +156,118 @@ def tile_mix_tierx_none_kernel(tc, x, w4_words, w4_scales, out):
                     start=True,
                     stop=True,
                 )
-            return back
-
-        def subtract(chunk, s, back):
-            i = [i for i in slabs_of(chunk) if slabs[i][1] <= s * PIECE][-1]
-            local = slice(s * PIECE - slabs[i][1], (s + 1) * PIECE - slabs[i][1])
+            i = [i for i in parts_of(rests, chunk) if rests[i][1] <= s * PIECE][-1]
+            local = slice(s * PIECE - rests[i][1], (s + 1) * PIECE - rests[i][1])
             nc.vector.tensor_tensor(
                 out=rest[i][:, local, :].rearrange("p (c i) j -> p c j i", i=RUN),
                 in0=raw_columns(chunk, s * PIECE, PIECE),
-                in1=back[:].rearrange("p j (c i) -> p c j i", i=RUN),
+                in1=back[:].rearrange("p (j c i) -> p c j i", j=PACK, i=RUN),
                 op=mybir.AluOpType.subtract,
             )
 
-        for chunk in range(CHUNKS - 1):
-            round_chunk(chunk)
-        quantise_first(0)
-        quantise_first(1)
+        last_slab = len(slabs) - 1
+        for i in range(last_slab):
+            round_slab(i)
+
+        quantise_first(0, 0)
+        quantise_first(0, 1)
         for s in range(PIECES):
-            subtract(0, s, read_back(0, s))
-            if s == 1:
-                warm_up()
+            leftover(0, s, WAVE + s % 2)
             if s + 2 < PIECES:
-                quantise_first(s + 2)
+                quantise_first(0, s + 2)
             if s > 0:
-                quantise_rest(s - 1)
-        quantise_rest(PIECES - 1)
+                quantise_rest(0, s - 1)
+        quantise_rest(0, PIECES - 1)
 
-        def side_work(step):
-            for chunk in range(1, CHUNKS):
-                if chunk == CHUNKS - 1 and step == round_position(chunk):
-                    round_chunk(chunk)
-                if step == quantise_position(chunk):
-                    for i in slabs_of(chunk):
-                        quantise_first(i)
-            for chunk in range(1, CHUNKS):
-                for s in range(PIECES):
-                    if step == piece_position(chunk, s):
-                        subtract(chunk, s, read_back(chunk, s))
-                        if s == PIECES - 1:
-                            for i in slabs_of(chunk):
-                                quantise_rest(i)
+        order = []
+        for a in range(PASSES):
+            for tier in range(2):
+                if (a, tier) == (PASSES - 1, 1):
+                    order.extend([(0, WAVE, b, other) for b in range(PASSES) for other in range(2)][:-1])
+                    order.extend([(0, n, a, tier) for n in range(WAVE + 1)])
+                else:
+                    order.extend([(0, n, a, tier) for n in range(WAVE)])
+        order.extend([(0, WAVE + 1, a, tier) for a in range(PASSES) for tier in range(2)])
+        for tier in range(2):
+            order.extend([(1, n, 0, tier) for n in range(WAVE - 1)])
+        order.extend([(1, WAVE - 1, 0, tier) for tier in range(2)])
+        for a in range(1, PASSES):
+            for tier in range(2):
+                order.extend([(1, n, a, tier) for n in range(WAVE)])
+        for n in range(WAVE, N_TILES):
+            order.extend([(1, n, a, tier) for a in range(PASSES) for tier in range(2)])
 
-        waves = []
-        for half in range(HALVES):
-            waves.append([(half, n) for n in range(WAVE[half])])
-            waves.extend([[(half, n)] for n in range(WAVE[half], N_TILES)])
+        bank_of = {}
+        for n in range(WAVE + 1):
+            bank_of[(0, n)] = n
+        bank_of[(0, WAVE + 1)] = 0
+        for n in range(WAVE - 1):
+            bank_of[(1, n)] = n + 2
+        bank_of[(1, WAVE - 1)] = 0
+        bank_of[(1, WAVE)] = 1
+        bank_of[(1, WAVE + 1)] = WAVE + 1
 
-        step = 0
-        for wave in waves:
-            acc = {}
-            for a in range(PASSES):
-                for tier in range(2):
-                    for half, n in wave:
-                        side_work(step)
-                        step = step + 1
-                        chunk = half * PASSES + a
-                        if a == 0 and tier == 0:
-                            acc[n] = sums.tile([P, T_TILE], F32, name="acc")
-                        last = a == PASSES - 1 and tier == 1
-                        nc.tensor.matmul_mx(
-                            out=acc[n][:],
-                            lhsT=w_code[a][:, 2 * n * P : 2 * (n + 1) * P].bitcast(E2M1),
-                            lhsT_scale=w_scale[:, a, n * P : (n + 1) * P],
-                            rhs=q_code[chunk][:].bitcast(E4M3) if tier == 0 else r_code[chunk][:].bitcast(E5M2),
-                            rhs_scale=q_scale[chunk][:] if tier == 0 else r_scale[chunk][:],
-                            start=(a == 0 and tier == 0),
-                            stop=last,
-                        )
-                        if last:
-                            parts = 2 if (half, n) == (HALVES - 1, N_TILES - 1) else 1
-                            width = T_TILE // parts
-                            for part in range(parts):
-                                result = stage.tile([P, width], F32, name="result")
-                                source = acc[n][:, part * width : (part + 1) * width]
-                                if len(wave) > 1 and n % 2 == 0:
-                                    nc.vector.tensor_copy(out=result[:], in_=source)
-                                else:
-                                    nc.scalar.copy(out=result[:], in_=source)
-                                t0 = half * T_TILE + part * width
-                                nc.sync.dma_start(out=out[n * P : (n + 1) * P, t0 : t0 + width], in_=result[:])
+        side = {}
+
+        def at(step, work, *args):
+            side.setdefault(step, []).append((work, args))
+
+        for chunk in range(1, PASSES):
+            first = order.index((0, 0, chunk, 0))
+            at(first - 5, quantise_first, chunk, 0)
+            at(first - 5, leftover, chunk, 0, WAVE)
+            at(first - 5, quantise_first, chunk, 1)
+            at(first - 3, leftover, chunk, 1, WAVE + 1)
+            at(first - 3, quantise_first, chunk, 2)
+            at(first - 1, leftover, chunk, 2, WAVE)
+            at(first, leftover, chunk, 3, WAVE + 1)
+            at(first, quantise_rest, chunk, 0)
+            at(first, quantise_rest, chunk, 1)
+
+        start = order.index((0, WAVE, 0, 0)) + 4
+        at(start, quantise_first, PASSES, 0)
+        for k in range(PASSES * PIECES):
+            chunk, s = PASSES + k // PIECES, k % PIECES
+            step = start + BACK_PACE * k + (1 if k > 0 else 0)
+            at(step, leftover, chunk, s, WAVE + 1 if k < 2 or k % 2 == 1 else 1)
+            if s == 0:
+                if chunk == PASSES:
+                    at(step, quantise_first, chunk, 1)
+                else:
+                    at(step, quantise_rest, chunk - 1, 1)
+            if s == 2:
+                at(step, quantise_rest, chunk, 0)
+            if s % 2 == 1 and chunk + 1 < CHUNKS:
+                at(step, quantise_first, chunk + 1, s // 2)
+        at(step, quantise_rest, CHUNKS - 1, 1)
+        at(order.index((1, 0, 0, 0)), round_slab, last_slab)
+
+        acc = {}
+        for step, (half, n, a, tier) in enumerate(order):
+            for work, args in side.get(step, []):
+                work(*args)
+            chunk = half * PASSES + a
+            if a == 0 and tier == 0:
+                acc[n] = psum.tile([P, T_TILE], F32, name="bank%d" % bank_of[(half, n)])
+            last = a == PASSES - 1 and tier == 1
+            nc.tensor.matmul_mx(
+                out=acc[n][:],
+                lhsT=w_code[a][:, 2 * n * P : 2 * (n + 1) * P].bitcast(E2M1),
+                lhsT_scale=w_scale[:, a, n * P : (n + 1) * P],
+                rhs=q_code[chunk][:].bitcast(E4M3) if tier == 0 else r_code[chunk][:].bitcast(E5M2),
+                rhs_scale=q_scale[chunk][:] if tier == 0 else r_scale[chunk][:],
+                start=(a == 0 and tier == 0),
+                stop=last,
+            )
+            if last:
+                parts = 2 if (half, n) == (HALVES - 1, N_TILES - 1) else 1
+                width = T_TILE // parts
+                for part in range(parts):
+                    result = stage.tile([P, width], F32, name="result")
+                    source = acc[n][:, part * width : (part + 1) * width]
+                    if half == 1 and n < WAVE and n % 2 == 0:
+                        nc.vector.tensor_copy(out=result[:], in_=source)
+                    else:
+                        nc.scalar.copy(out=result[:], in_=source)
+                    t0 = half * T_TILE + part * width
+                    nc.sync.dma_start(out=out[n * P : (n + 1) * P, t0 : t0 + width], in_=result[:])

@@ -29,17 +29,15 @@ BACK_PACE = 3
 
 
 def load_widths(chunk):
-    return [256, 256] if chunk < PASSES else [512]
+    return [256, 256] if chunk == 0 else [512]
 
 
 def slab_widths(chunk):
-    if chunk == 0:
-        return [128, 128, 128, 128]
-    return [256, 128, 128] if chunk < PASSES else [256, 256]
+    return [128, 128, 128, 128] if chunk < PASSES else [256, 256]
 
 
 def rest_widths(chunk):
-    return [128, 128, 128, 128] if chunk == 0 else [256, 256]
+    return [256, 128, 128] if chunk < PASSES else [256, 256]
 
 
 def cut(widths_of):
@@ -64,9 +62,11 @@ def tile_mix_tierx_none_kernel(tc, x, w4_words, w4_scales, out):
         slabs = cut(slab_widths)
         rests = cut(rest_widths)
 
-        w_scale = keep.tile([P, PASSES, N], U8, align_bytes=64)
-        nc.vector.memset(w_scale[:].bitcast(U32), 0)
-        w_code = [keep.tile([P, 2 * N], U8, align_bytes=64, name="w_code%d" % a) for a in range(PASSES)]
+        w_scale = [keep.tile([P, N], U8, align_bytes=64, name="w_scale%d" % a) for a in range(PASSES)]
+        for a in range(PASSES):
+            nc.vector.memset(w_scale[a][:].bitcast(U32), 0)
+        w_code = [keep.tile([P, 2 * WAVE * P], U8, align_bytes=64, name="w_code%d" % a) for a in range(PASSES)]
+        w_late = keep.tile([P, PASSES, 2 * (N - WAVE * P)], U8, align_bytes=64)
         raw = [keep.tile([P, PACK, width], F32, align_bytes=64, name="raw%d" % i) for i, (chunk, col, width) in enumerate(loads)]
         rounded = [keep.tile([P, width, PACK], BF16, align_bytes=64, name="rounded%d" % i) for i, (chunk, col, width) in enumerate(slabs)]
         rest = [keep.tile([P, width, PACK], BF16, align_bytes=64, name="rest%d" % i) for i, (chunk, col, width) in enumerate(rests)]
@@ -75,11 +75,35 @@ def tile_mix_tierx_none_kernel(tc, x, w4_words, w4_scales, out):
         r_code = [keep.tile([P, T_TILE], U32, align_bytes=64, name="r_code%d" % c) for c in range(CHUNKS)]
         r_scale = [keep.tile([P, T_TILE], U8, align_bytes=64, name="r_scale%d" % c) for c in range(CHUNKS)]
 
+        marks = keep.tile([P, PACK * P + PACK], BF16)
+        nc.gpsimd.iota(
+            marks[:],
+            pattern=[[-1, PACK * P + PACK]],
+            base=PACK - 1,
+            channel_multiplier=PACK,
+            allow_small_or_imprecise_dtypes=True,
+        )
+        eye_rows = [keep.tile([P, PACK * P], BF16, align_bytes=64, name="eye_rows%d" % j) for j in range(PACK)]
+        eye_code = keep.tile([P, PACK * P], U32, align_bytes=64)
+        eye_scale = keep.tile([P, PACK * P], U8, align_bytes=64)
+        for j in range(PACK + 2):
+            if j < PACK:
+                nc.vector.tensor_scalar(
+                    out=eye_rows[j][:],
+                    in0=marks[:, PACK - 1 - j : PACK - 1 - j + PACK * P],
+                    scalar1=0.0,
+                    scalar2=None,
+                    op0=mybir.AluOpType.is_equal,
+                )
+            if j >= 2:
+                cols = slice((j - 2) * P, (j - 1) * P)
+                nc.vector.quantize_mx(out=eye_code[:, cols].bitcast(E4M3), scales=eye_scale[:, cols], in_=eye_rows[j - 2][:])
+
         scale_rows = w4_scales.bitcast(I32).rearrange("a (q r) n -> r q a n", r=4)
 
-        def load_scales(a0, a1):
+        def load_scales(a):
             for r in range(4):
-                nc.sync.dma_start(out=w_scale[:].bitcast(I32)[r:P:32, a0:a1, :], in_=scale_rows[r, :, a0:a1, :])
+                nc.sync.dma_start(out=w_scale[a][:].bitcast(I32)[r:P:32, :], in_=scale_rows[r, :, a, :])
 
         for i, (chunk, col, width) in enumerate(loads):
             half, a = divmod(chunk, PASSES)
@@ -87,33 +111,21 @@ def tile_mix_tierx_none_kernel(tc, x, w4_words, w4_scales, out):
             rows = x[a * P * PACK : (a + 1) * P * PACK, t0 : t0 + width]
             nc.sync.dma_start(out=raw[i][:], in_=rows.rearrange("(p j) t -> p j t", j=PACK))
             if col + width == T_TILE and half == 0:
-                load_scales(a, a + 1)
-                nc.sync.dma_start(out=w_code[a][:].bitcast(I32), in_=w4_words[a].bitcast(I32))
+                load_scales(a)
+                nc.sync.dma_start(out=w_code[a][:].bitcast(I32), in_=w4_words[a, :, : 2 * WAVE * P].bitcast(I32))
+                if a == PASSES - 1:
+                    late = w4_words[:, :, 2 * WAVE * P :].bitcast(I32).rearrange("a p n -> p a n")
+                    nc.sync.dma_start(out=w_late[:].bitcast(I32), in_=late)
+
+        def weight_words(a, n):
+            if n < WAVE:
+                return w_code[a][:, 2 * n * P : 2 * (n + 1) * P]
+            return w_late[:, a, 2 * (n - WAVE) * P : 2 * (n - WAVE + 1) * P]
 
         def raw_columns(chunk, col, width):
             for i, (c, first, loaded) in enumerate(loads):
                 if c == chunk and first <= col < first + loaded:
                     return raw[i][:, :, col - first : col - first + width].rearrange("p j (c i) -> p c j i", i=RUN)
-
-        marks = keep.tile([P, PACK * P + PACK], BF16)
-        nc.gpsimd.memset(marks[:].bitcast(U32), 0)
-        nc.gpsimd.affine_select(
-            out=marks[:],
-            in_=marks[:],
-            compare_op=mybir.AluOpType.not_equal,
-            fill=1.0,
-            base=PACK - 1,
-            pattern=[[-1, PACK * P + PACK]],
-            channel_multiplier=PACK,
-        )
-        eye_rows = keep.tile([P, PACK, PACK * P], BF16, align_bytes=64)
-        for j in range(PACK):
-            nc.vector.tensor_copy(out=eye_rows[:, j, :], in_=marks[:, PACK - 1 - j : PACK - 1 - j + PACK * P])
-        eye_code = keep.tile([P, PACK * P], U32, align_bytes=64)
-        eye_scale = keep.tile([P, PACK * P], U8, align_bytes=64)
-        nc.vector.quantize_mx(
-            out=eye_code[:].bitcast(E4M3), scales=eye_scale[:], in_=eye_rows[:].rearrange("p j f -> p (j f)")
-        )
 
         def parts_of(parts, chunk):
             return [i for i, part in enumerate(parts) if part[0] == chunk]
@@ -175,9 +187,10 @@ def tile_mix_tierx_none_kernel(tc, x, w4_words, w4_scales, out):
             leftover(0, s, WAVE + s % 2)
             if s + 2 < PIECES:
                 quantise_first(0, s + 2)
-            if s > 0:
-                quantise_rest(0, s - 1)
-        quantise_rest(0, PIECES - 1)
+            if s == 2:
+                quantise_rest(0, 0)
+        quantise_rest(0, 1)
+        quantise_rest(0, 2)
 
         order = []
         for a in range(PASSES):
@@ -215,14 +228,16 @@ def tile_mix_tierx_none_kernel(tc, x, w4_words, w4_scales, out):
         for chunk in range(1, PASSES):
             first = order.index((0, 0, chunk, 0))
             at(first - 5, quantise_first, chunk, 0)
-            at(first - 5, leftover, chunk, 0, WAVE)
             at(first - 5, quantise_first, chunk, 1)
+            at(first - 5, leftover, chunk, 0, WAVE)
+            at(first - 5, quantise_first, chunk, 2)
             at(first - 3, leftover, chunk, 1, WAVE + 1)
-            at(first - 3, quantise_first, chunk, 2)
+            at(first - 3, quantise_first, chunk, 3)
             at(first - 1, leftover, chunk, 2, WAVE)
+            at(first - 1, quantise_rest, chunk, 0)
             at(first, leftover, chunk, 3, WAVE + 1)
-            at(first, quantise_rest, chunk, 0)
             at(first, quantise_rest, chunk, 1)
+            at(first, quantise_rest, chunk, 2)
 
         start = order.index((0, WAVE, 0, 0)) + 4
         at(start, quantise_first, PASSES, 0)
@@ -252,8 +267,8 @@ def tile_mix_tierx_none_kernel(tc, x, w4_words, w4_scales, out):
             last = a == PASSES - 1 and tier == 1
             nc.tensor.matmul_mx(
                 out=acc[n][:],
-                lhsT=w_code[a][:, 2 * n * P : 2 * (n + 1) * P].bitcast(E2M1),
-                lhsT_scale=w_scale[:, a, n * P : (n + 1) * P],
+                lhsT=weight_words(a, n).bitcast(E2M1),
+                lhsT_scale=w_scale[a][:, n * P : (n + 1) * P],
                 rhs=q_code[chunk][:].bitcast(E4M3) if tier == 0 else r_code[chunk][:].bitcast(E5M2),
                 rhs_scale=q_scale[chunk][:] if tier == 0 else r_scale[chunk][:],
                 start=(a == 0 and tier == 0),

@@ -177,6 +177,38 @@ def tile_mix_tierx_none_kernel(tc, x, w4_words, w4_scales, out):
                 op=mybir.AluOpType.subtract,
             )
 
+        pairs = {}
+
+        def leftover_wide(chunk, part, u, bank):
+            cols = slice(part * 2 * PIECE, (part + 1) * 2 * PIECE)
+            back = psum.tile([P, T_TILE], F32, name="bank%d" % bank)
+            for e in range(2):
+                j = 2 * u + e
+                nc.tensor.matmul_mx(
+                    out=back[:, e * 2 * PIECE : (e + 1) * 2 * PIECE],
+                    lhsT=eye_code[:, j * P : (j + 1) * P].bitcast(E4M3),
+                    lhsT_scale=eye_scale[:, j * P : (j + 1) * P],
+                    rhs=q_code[chunk][:, cols].bitcast(E4M3),
+                    rhs_scale=q_scale[chunk][:, cols],
+                    start=True,
+                    stop=True,
+                )
+            if u == 0:
+                pairs[(chunk, part)] = stage.tile([P, 2, 2 * PIECE, 2], BF16, name="pairs", bufs=2)
+            source = raw[parts_of(loads, chunk)[0]][:, 2 * u : 2 * u + 2, cols]
+            nc.vector.tensor_tensor(
+                out=pairs[(chunk, part)][:, u, :, :].rearrange("p (c i) e -> p c e i", i=4),
+                in0=source.rearrange("p e (c i) -> p c e i", i=4),
+                in1=back[:].rearrange("p (e c i) -> p c e i", e=2, i=4),
+                op=mybir.AluOpType.subtract,
+            )
+            if u == 1:
+                words = pairs[(chunk, part)][:].rearrange("p u t e -> p (u t e)").bitcast(U32)
+                target = rest[parts_of(rests, chunk)[part]][:].rearrange("p t j -> p (t j)").bitcast(U32)
+                nc.scalar.copy(
+                    out=target.rearrange("p (t u) -> p t u", u=2), in_=words.rearrange("p (u t) -> p t u", u=2)
+                )
+
         last_slab = len(slabs) - 1
         for i in range(last_slab):
             round_slab(i)
@@ -207,8 +239,8 @@ def tile_mix_tierx_none_kernel(tc, x, w4_words, w4_scales, out):
         for a in range(1, PASSES):
             for tier in range(2):
                 order.extend([(1, n, a, tier) for n in range(WAVE)])
-        for n in range(WAVE, N_TILES):
-            order.extend([(1, n, a, tier) for a in range(PASSES) for tier in range(2)])
+        order.extend([(1, WAVE, a, tier) for a in range(PASSES) for tier in range(2)])
+        order.extend([(1, WAVE + 1, a, 1) for a in range(PASSES)])
 
         bank_of = {}
         for n in range(WAVE + 1):
@@ -244,7 +276,7 @@ def tile_mix_tierx_none_kernel(tc, x, w4_words, w4_scales, out):
         for k in range(PASSES * PIECES):
             chunk, s = PASSES + k // PIECES, k % PIECES
             step = start + BACK_PACE * k + (1 if k > 0 else 0)
-            at(step, leftover, chunk, s, WAVE + 1 if k < 2 or k % 2 == 1 else 1)
+            at(step, leftover_wide, chunk, s // 2, s % 2, WAVE + 1 if k < 2 or k % 2 == 1 else 1)
             if s == 0:
                 if chunk == PASSES:
                     at(step, quantise_first, chunk, 1)
@@ -262,7 +294,9 @@ def tile_mix_tierx_none_kernel(tc, x, w4_words, w4_scales, out):
             for work, args in side.get(step, []):
                 work(*args)
             chunk = half * PASSES + a
-            if a == 0 and tier == 0:
+            split = (half, n) == (HALVES - 1, N_TILES - 1)
+            opens = a == 0 and (tier == 0 or split)
+            if opens:
                 acc[n] = psum.tile([P, T_TILE], F32, name="bank%d" % bank_of[(half, n)])
             last = a == PASSES - 1 and tier == 1
             nc.tensor.matmul_mx(
@@ -271,18 +305,44 @@ def tile_mix_tierx_none_kernel(tc, x, w4_words, w4_scales, out):
                 lhsT_scale=w_scale[a][:, n * P : (n + 1) * P],
                 rhs=q_code[chunk][:].bitcast(E4M3) if tier == 0 else r_code[chunk][:].bitcast(E5M2),
                 rhs_scale=q_scale[chunk][:] if tier == 0 else r_scale[chunk][:],
-                start=(a == 0 and tier == 0),
+                start=opens,
                 stop=last,
             )
-            if last:
-                parts = 2 if (half, n) == (HALVES - 1, N_TILES - 1) else 1
-                width = T_TILE // parts
-                for part in range(parts):
-                    result = stage.tile([P, width], F32, name="result")
-                    source = acc[n][:, part * width : (part + 1) * width]
-                    if half == 1 and n < WAVE and n % 2 == 0:
-                        nc.vector.tensor_copy(out=result[:], in_=source)
-                    else:
-                        nc.scalar.copy(out=result[:], in_=source)
-                    t0 = half * T_TILE + part * width
-                    nc.sync.dma_start(out=out[n * P : (n + 1) * P, t0 : t0 + width], in_=result[:])
+            if last and split:
+                second_tier = keep.tile([P, T_TILE], F32)
+                for s in range(PIECES):
+                    nc.scalar.copy(out=second_tier[:, s * PIECE : (s + 1) * PIECE], in_=acc[n][:, s * PIECE : (s + 1) * PIECE])
+            elif last:
+                result = stage.tile([P, T_TILE], F32, name="result")
+                if half == 1 and n < WAVE and n % 2 == 0:
+                    nc.vector.tensor_copy(out=result[:], in_=acc[n][:])
+                else:
+                    nc.scalar.copy(out=result[:], in_=acc[n][:])
+                t0 = half * T_TILE
+                nc.sync.dma_start(out=out[n * P : (n + 1) * P, t0 : t0 + T_TILE], in_=result[:])
+
+        half, n = HALVES - 1, N_TILES - 1
+        total = keep.tile([P, T_TILE], F32)
+        for s in range(PIECES):
+            cols = slice(s * PIECE, (s + 1) * PIECE)
+            small = psum.tile([P, T_TILE], F32, name="bank%d" % bank_of[(half, s)])
+            for a in range(PASSES):
+                chunk = half * PASSES + a
+                nc.tensor.matmul_mx(
+                    out=small[:, :PIECE],
+                    lhsT=weight_words(a, n).bitcast(E2M1),
+                    lhsT_scale=w_scale[a][:, n * P : (n + 1) * P],
+                    rhs=q_code[chunk][:, cols].bitcast(E4M3),
+                    rhs_scale=q_scale[chunk][:, cols],
+                    start=(a == 0),
+                    stop=(a == PASSES - 1),
+                )
+            nc.vector.tensor_tensor(
+                out=total[:, cols], in0=small[:, :PIECE], in1=second_tier[:, cols], op=mybir.AluOpType.add
+            )
+            if s % 2 == 1:
+                stored = slice((s - 1) * PIECE, (s + 1) * PIECE)
+                t0 = half * T_TILE
+                nc.sync.dma_start(
+                    out=out[n * P : (n + 1) * P, t0 + stored.start : t0 + stored.stop], in_=total[:, stored]
+                )

@@ -20,24 +20,29 @@ PASSES = K // (P * PACK)
 T_TILE = 512
 N_TILES = N // P
 HALVES = T // T_TILE
-PIECE = 128
-PIECES = T_TILE // PIECE
 CHUNKS = HALVES * PASSES
+TIERS = 2
+PIECE = T_TILE // PACK
+PIECES = T_TILE // PIECE
+WIDE = 2 * PIECE
 WAVE = 6
 RUN = 2
+WIDE_RUN = 4
+BACK_LEADS = (5, 3, 1, 0)
+BACK_DELAY = 4
 BACK_PACE = 3
 
 
 def load_widths(chunk):
-    return [256, 256] if chunk == 0 else [512]
+    return [WIDE, WIDE] if chunk == 0 else [T_TILE]
 
 
-def slab_widths(chunk):
-    return [128, 128, 128, 128] if chunk < PASSES else [256, 256]
+def first_widths(chunk):
+    return [PIECE] * PIECES if chunk < PASSES else [WIDE, WIDE]
 
 
 def rest_widths(chunk):
-    return [256, 128, 128] if chunk < PASSES else [256, 256]
+    return [WIDE, PIECE, PIECE] if chunk < PASSES else [WIDE, WIDE]
 
 
 def cut(widths_of):
@@ -50,30 +55,73 @@ def cut(widths_of):
     return parts
 
 
+def parts_of(parts, chunk):
+    return [i for i, part in enumerate(parts) if part[0] == chunk]
+
+
+def pass_order():
+    def together(half, group, a, tiers):
+        return [(half, n, a, tier) for tier in tiers for n in group]
+
+    def alone(half, n):
+        return [(half, n, a, tier) for a in range(PASSES) for tier in range(TIERS)]
+
+    final = PASSES - 1
+    order = []
+    for a in range(final):
+        order.extend(together(0, range(WAVE), a, range(TIERS)))
+    order.extend(together(0, range(WAVE), final, [0]))
+    order.extend(alone(0, WAVE)[:-1])
+    order.extend(together(0, range(WAVE + 1), final, [1]))
+    order.extend(alone(0, WAVE + 1))
+    order.extend(together(1, range(WAVE - 1), 0, range(TIERS)))
+    order.extend(together(1, [WAVE - 1], 0, range(TIERS)))
+    order.extend(together(1, range(WAVE), 1, range(TIERS)))
+    order.extend(together(1, range(WAVE - 2), final, range(TIERS)))
+    order.extend(together(1, range(WAVE - 2, WAVE), final, range(TIERS)))
+    order.extend(alone(1, WAVE))
+    order.extend([(1, WAVE + 1, a, 1) for a in range(PASSES)])
+    return order
+
+
+def sum_bank(half, n):
+    if half == 0:
+        return n if n <= WAVE else 0
+    if n < WAVE - 1:
+        return n + 2
+    return {WAVE - 1: 0, WAVE: 1, WAVE + 1: WAVE + 1}[n]
+
+
 def tile_mix_tierx_none_kernel(tc, x, w4_words, w4_scales, out):
     nc = tc.nc
     with ExitStack() as ctx:
         keep = ctx.enter_context(tc.tile_pool(name="keep", bufs=1))
-        stage = ctx.enter_context(tc.tile_pool(name="stage", bufs=17))
+        stage = ctx.enter_context(tc.tile_pool(name="stage", bufs=HALVES * N_TILES - 1))
         psum = ctx.enter_context(tc.psum_pool(name="psum", bufs=1))
         ctx.enter_context(tc.manual_schedule())
 
+        def bank_tile(bank):
+            return psum.tile([P, T_TILE], F32, name="bank%d" % bank)
+
+        def kept(name, count, shape_of, dtype):
+            return [keep.tile(shape_of(i), dtype, align_bytes=64, name="%s%d" % (name, i)) for i in range(count)]
+
         loads = cut(load_widths)
-        slabs = cut(slab_widths)
+        firsts = cut(first_widths)
         rests = cut(rest_widths)
 
-        w_scale = [keep.tile([P, N], U8, align_bytes=64, name="w_scale%d" % a) for a in range(PASSES)]
+        w_scale = kept("w_scale", PASSES, lambda a: [P, N], U8)
         for a in range(PASSES):
             nc.vector.memset(w_scale[a][:].bitcast(U32), 0)
-        w_code = [keep.tile([P, 2 * WAVE * P], U8, align_bytes=64, name="w_code%d" % a) for a in range(PASSES)]
+        w_code = kept("w_code", PASSES, lambda a: [P, 2 * WAVE * P], U8)
         w_late = keep.tile([P, PASSES, 2 * (N - WAVE * P)], U8, align_bytes=64)
-        raw = [keep.tile([P, PACK, width], F32, align_bytes=64, name="raw%d" % i) for i, (chunk, col, width) in enumerate(loads)]
-        rounded = [keep.tile([P, width, PACK], BF16, align_bytes=64, name="rounded%d" % i) for i, (chunk, col, width) in enumerate(slabs)]
-        rest = [keep.tile([P, width, PACK], BF16, align_bytes=64, name="rest%d" % i) for i, (chunk, col, width) in enumerate(rests)]
-        q_code = [keep.tile([P, T_TILE], U32, align_bytes=64, name="q_code%d" % c) for c in range(CHUNKS)]
-        q_scale = [keep.tile([P, T_TILE], U8, align_bytes=64, name="q_scale%d" % c) for c in range(CHUNKS)]
-        r_code = [keep.tile([P, T_TILE], U32, align_bytes=64, name="r_code%d" % c) for c in range(CHUNKS)]
-        r_scale = [keep.tile([P, T_TILE], U8, align_bytes=64, name="r_scale%d" % c) for c in range(CHUNKS)]
+        raw = kept("raw", len(loads), lambda i: [P, PACK, loads[i][2]], F32)
+        rounded = kept("rounded", len(firsts), lambda i: [P, firsts[i][2], PACK], BF16)
+        rest = kept("rest", len(rests), lambda i: [P, rests[i][2], PACK], BF16)
+        q_code = kept("q_code", CHUNKS, lambda c: [P, T_TILE], U32)
+        q_scale = kept("q_scale", CHUNKS, lambda c: [P, T_TILE], U8)
+        r_code = kept("r_code", CHUNKS, lambda c: [P, T_TILE], U32)
+        r_scale = kept("r_scale", CHUNKS, lambda c: [P, T_TILE], U8)
 
         marks = keep.tile([P, PACK * P + PACK], BF16)
         nc.gpsimd.iota(
@@ -83,10 +131,11 @@ def tile_mix_tierx_none_kernel(tc, x, w4_words, w4_scales, out):
             channel_multiplier=PACK,
             allow_small_or_imprecise_dtypes=True,
         )
-        eye_rows = [keep.tile([P, PACK * P], BF16, align_bytes=64, name="eye_rows%d" % j) for j in range(PACK)]
+        eye_rows = kept("eye_rows", PACK, lambda j: [P, PACK * P], BF16)
         eye_code = keep.tile([P, PACK * P], U32, align_bytes=64)
         eye_scale = keep.tile([P, PACK * P], U8, align_bytes=64)
-        for j in range(PACK + 2):
+        trail = 2
+        for j in range(PACK + trail):
             if j < PACK:
                 nc.vector.tensor_scalar(
                     out=eye_rows[j][:],
@@ -95,23 +144,21 @@ def tile_mix_tierx_none_kernel(tc, x, w4_words, w4_scales, out):
                     scalar2=None,
                     op0=mybir.AluOpType.is_equal,
                 )
-            if j >= 2:
-                cols = slice((j - 2) * P, (j - 1) * P)
-                nc.vector.quantize_mx(out=eye_code[:, cols].bitcast(E4M3), scales=eye_scale[:, cols], in_=eye_rows[j - 2][:])
+            if j >= trail:
+                block = slice((j - trail) * P, (j - trail + 1) * P)
+                nc.vector.quantize_mx(
+                    out=eye_code[:, block].bitcast(E4M3), scales=eye_scale[:, block], in_=eye_rows[j - trail][:]
+                )
 
         scale_rows = w4_scales.bitcast(I32).rearrange("a (q r) n -> r q a n", r=4)
-
-        def load_scales(a):
-            for r in range(4):
-                nc.sync.dma_start(out=w_scale[a][:].bitcast(I32)[r:P:32, :], in_=scale_rows[r, :, a, :])
-
         for i, (chunk, col, width) in enumerate(loads):
             half, a = divmod(chunk, PASSES)
             t0 = half * T_TILE + col
             rows = x[a * P * PACK : (a + 1) * P * PACK, t0 : t0 + width]
             nc.sync.dma_start(out=raw[i][:], in_=rows.rearrange("(p j) t -> p j t", j=PACK))
             if col + width == T_TILE and half == 0:
-                load_scales(a)
+                for r in range(4):
+                    nc.sync.dma_start(out=w_scale[a][:].bitcast(I32)[r:P:32, :], in_=scale_rows[r, :, a, :])
                 nc.sync.dma_start(out=w_code[a][:].bitcast(I32), in_=w4_words[a, :, : 2 * WAVE * P].bitcast(I32))
                 if a == PASSES - 1:
                     late = w4_words[:, :, 2 * WAVE * P :].bitcast(I32).rearrange("a p n -> p a n")
@@ -123,100 +170,91 @@ def tile_mix_tierx_none_kernel(tc, x, w4_words, w4_scales, out):
             return w_late[:, a, 2 * (n - WAVE) * P : 2 * (n - WAVE + 1) * P]
 
         def raw_columns(chunk, col, width):
-            for i, (c, first, loaded) in enumerate(loads):
-                if c == chunk and first <= col < first + loaded:
-                    return raw[i][:, :, col - first : col - first + width].rearrange("p j (c i) -> p c j i", i=RUN)
+            i = [i for i in parts_of(loads, chunk) if loads[i][1] <= col][-1]
+            return raw[i][:, :, col - loads[i][1] : col - loads[i][1] + width]
 
-        def parts_of(parts, chunk):
-            return [i for i, part in enumerate(parts) if part[0] == chunk]
-
-        def round_slab(i):
-            chunk, col, width = slabs[i]
+        def round_part(i):
+            chunk, col, width = firsts[i]
             nc.scalar.copy(
                 out=rounded[i][:].rearrange("p (c i) j -> p c j i", i=RUN),
-                in_=raw_columns(chunk, col, width),
+                in_=raw_columns(chunk, col, width).rearrange("p j (c i) -> p c j i", i=RUN),
             )
 
         def quantise_first(chunk, part):
-            i = parts_of(slabs, chunk)[part]
-            chunk, col, width = slabs[i]
+            i = parts_of(firsts, chunk)[part]
+            cols = slice(firsts[i][1], firsts[i][1] + firsts[i][2])
             nc.vector.quantize_mx(
-                out=q_code[chunk][:, col : col + width].bitcast(E4M3),
-                scales=q_scale[chunk][:, col : col + width],
+                out=q_code[chunk][:, cols].bitcast(E4M3),
+                scales=q_scale[chunk][:, cols],
                 in_=rounded[i][:].rearrange("p t j -> p (t j)"),
             )
 
         def quantise_rest(chunk, part):
             i = parts_of(rests, chunk)[part]
-            chunk, col, width = rests[i]
+            cols = slice(rests[i][1], rests[i][1] + rests[i][2])
             nc.vector.quantize_mx(
-                out=r_code[chunk][:, col : col + width].bitcast(E5M2),
-                scales=r_scale[chunk][:, col : col + width],
+                out=r_code[chunk][:, cols].bitcast(E5M2),
+                scales=r_scale[chunk][:, cols],
                 in_=rest[i][:].rearrange("p t j -> p (t j)"),
             )
 
-        def leftover(chunk, s, bank):
-            cols = slice(s * PIECE, (s + 1) * PIECE)
-            back = psum.tile([P, T_TILE], F32, name="bank%d" % bank)
-            for j in range(PACK):
+        def read_back(chunk, col, width, rows, bank):
+            back = bank_tile(bank)
+            for place, j in enumerate(rows):
                 nc.tensor.matmul_mx(
-                    out=back[:, j * PIECE : (j + 1) * PIECE],
+                    out=back[:, place * width : (place + 1) * width],
                     lhsT=eye_code[:, j * P : (j + 1) * P].bitcast(E4M3),
                     lhsT_scale=eye_scale[:, j * P : (j + 1) * P],
-                    rhs=q_code[chunk][:, cols].bitcast(E4M3),
-                    rhs_scale=q_scale[chunk][:, cols],
+                    rhs=q_code[chunk][:, col : col + width].bitcast(E4M3),
+                    rhs_scale=q_scale[chunk][:, col : col + width],
                     start=True,
                     stop=True,
                 )
-            i = [i for i in parts_of(rests, chunk) if rests[i][1] <= s * PIECE][-1]
-            local = slice(s * PIECE - rests[i][1], (s + 1) * PIECE - rests[i][1])
+            return back
+
+        def leftover_narrow(chunk, s, bank):
+            col = s * PIECE
+            back = read_back(chunk, col, PIECE, range(PACK), bank)
+            i = [i for i in parts_of(rests, chunk) if rests[i][1] <= col][-1]
+            local = slice(col - rests[i][1], col - rests[i][1] + PIECE)
             nc.vector.tensor_tensor(
                 out=rest[i][:, local, :].rearrange("p (c i) j -> p c j i", i=RUN),
-                in0=raw_columns(chunk, s * PIECE, PIECE),
+                in0=raw_columns(chunk, col, PIECE).rearrange("p j (c i) -> p c j i", i=RUN),
                 in1=back[:].rearrange("p (j c i) -> p c j i", j=PACK, i=RUN),
                 op=mybir.AluOpType.subtract,
             )
 
         pairs = {}
 
-        def leftover_wide(chunk, part, u, bank):
-            cols = slice(part * 2 * PIECE, (part + 1) * 2 * PIECE)
-            back = psum.tile([P, T_TILE], F32, name="bank%d" % bank)
-            for e in range(2):
-                j = 2 * u + e
-                nc.tensor.matmul_mx(
-                    out=back[:, e * 2 * PIECE : (e + 1) * 2 * PIECE],
-                    lhsT=eye_code[:, j * P : (j + 1) * P].bitcast(E4M3),
-                    lhsT_scale=eye_scale[:, j * P : (j + 1) * P],
-                    rhs=q_code[chunk][:, cols].bitcast(E4M3),
-                    rhs_scale=q_scale[chunk][:, cols],
-                    start=True,
-                    stop=True,
-                )
+        def leftover_wide(chunk, s, bank):
+            part, u = divmod(s, 2)
+            col = part * WIDE
+            back = read_back(chunk, col, WIDE, range(2 * u, 2 * u + 2), bank)
             if u == 0:
-                pairs[(chunk, part)] = stage.tile([P, 2, 2 * PIECE, 2], BF16, name="pairs", bufs=2)
-            source = raw[parts_of(loads, chunk)[0]][:, 2 * u : 2 * u + 2, cols]
+                pairs[part] = stage.tile([P, 2, WIDE, 2], BF16, name="pairs", bufs=2)
             nc.vector.tensor_tensor(
-                out=pairs[(chunk, part)][:, u, :, :].rearrange("p (c i) e -> p c e i", i=4),
-                in0=source.rearrange("p e (c i) -> p c e i", i=4),
-                in1=back[:].rearrange("p (e c i) -> p c e i", e=2, i=4),
+                out=pairs[part][:, u, :, :].rearrange("p (c i) e -> p c e i", i=WIDE_RUN),
+                in0=raw_columns(chunk, col, WIDE)[:, 2 * u : 2 * u + 2, :].rearrange(
+                    "p e (c i) -> p c e i", i=WIDE_RUN
+                ),
+                in1=back[:].rearrange("p (e c i) -> p c e i", e=2, i=WIDE_RUN),
                 op=mybir.AluOpType.subtract,
             )
             if u == 1:
-                words = pairs[(chunk, part)][:].rearrange("p u t e -> p (u t e)").bitcast(U32)
+                source = pairs[part][:].rearrange("p u t e -> p (u t e)").bitcast(U32)
                 target = rest[parts_of(rests, chunk)[part]][:].rearrange("p t j -> p (t j)").bitcast(U32)
                 nc.scalar.copy(
-                    out=target.rearrange("p (t u) -> p t u", u=2), in_=words.rearrange("p (u t) -> p t u", u=2)
+                    out=target.rearrange("p (t u) -> p t u", u=2), in_=source.rearrange("p (u t) -> p t u", u=2)
                 )
 
-        last_slab = len(slabs) - 1
-        for i in range(last_slab):
-            round_slab(i)
+        last_part = len(firsts) - 1
+        for i in range(last_part):
+            round_part(i)
 
         quantise_first(0, 0)
         quantise_first(0, 1)
         for s in range(PIECES):
-            leftover(0, s, WAVE + s % 2)
+            leftover_narrow(0, s, WAVE + s % 2)
             if s + 2 < PIECES:
                 quantise_first(0, s + 2)
             if s == 2:
@@ -224,59 +262,33 @@ def tile_mix_tierx_none_kernel(tc, x, w4_words, w4_scales, out):
         quantise_rest(0, 1)
         quantise_rest(0, 2)
 
-        order = []
-        for a in range(PASSES):
-            for tier in range(2):
-                if (a, tier) == (PASSES - 1, 1):
-                    order.extend([(0, WAVE, b, other) for b in range(PASSES) for other in range(2)][:-1])
-                    order.extend([(0, n, a, tier) for n in range(WAVE + 1)])
-                else:
-                    order.extend([(0, n, a, tier) for n in range(WAVE)])
-        order.extend([(0, WAVE + 1, a, tier) for a in range(PASSES) for tier in range(2)])
-        for tier in range(2):
-            order.extend([(1, n, 0, tier) for n in range(WAVE - 1)])
-        order.extend([(1, WAVE - 1, 0, tier) for tier in range(2)])
-        for a in range(1, PASSES):
-            for tier in range(2):
-                order.extend([(1, n, a, tier) for n in range(WAVE)])
-        order.extend([(1, WAVE, a, tier) for a in range(PASSES) for tier in range(2)])
-        order.extend([(1, WAVE + 1, a, 1) for a in range(PASSES)])
-
-        bank_of = {}
-        for n in range(WAVE + 1):
-            bank_of[(0, n)] = n
-        bank_of[(0, WAVE + 1)] = 0
-        for n in range(WAVE - 1):
-            bank_of[(1, n)] = n + 2
-        bank_of[(1, WAVE - 1)] = 0
-        bank_of[(1, WAVE)] = 1
-        bank_of[(1, WAVE + 1)] = WAVE + 1
-
+        order = pass_order()
         side = {}
 
         def at(step, work, *args):
             side.setdefault(step, []).append((work, args))
 
         for chunk in range(1, PASSES):
-            first = order.index((0, 0, chunk, 0))
-            at(first - 5, quantise_first, chunk, 0)
-            at(first - 5, quantise_first, chunk, 1)
-            at(first - 5, leftover, chunk, 0, WAVE)
-            at(first - 5, quantise_first, chunk, 2)
-            at(first - 3, leftover, chunk, 1, WAVE + 1)
-            at(first - 3, quantise_first, chunk, 3)
-            at(first - 1, leftover, chunk, 2, WAVE)
-            at(first - 1, quantise_rest, chunk, 0)
-            at(first, leftover, chunk, 3, WAVE + 1)
-            at(first, quantise_rest, chunk, 1)
-            at(first, quantise_rest, chunk, 2)
+            steps = [order.index((0, 0, chunk, 0)) - lead for lead in BACK_LEADS]
+            at(steps[0], quantise_first, chunk, 0)
+            at(steps[0], quantise_first, chunk, 1)
+            for s in range(PIECES):
+                at(steps[s], leftover_narrow, chunk, s, WAVE + s % 2)
+                if s + 2 < PIECES:
+                    at(steps[s], quantise_first, chunk, s + 2)
+                if s == 2:
+                    at(steps[s], quantise_rest, chunk, 0)
+            at(steps[-1], quantise_rest, chunk, 1)
+            at(steps[-1], quantise_rest, chunk, 2)
 
-        start = order.index((0, WAVE, 0, 0)) + 4
-        at(start, quantise_first, PASSES, 0)
-        for k in range(PASSES * PIECES):
-            chunk, s = PASSES + k // PIECES, k % PIECES
-            step = start + BACK_PACE * k + (1 if k > 0 else 0)
-            at(step, leftover_wide, chunk, s // 2, s % 2, WAVE + 1 if k < 2 or k % 2 == 1 else 1)
+        begin = order.index((0, WAVE, 0, 0)) + BACK_DELAY
+        at(begin, quantise_first, PASSES, 0)
+        for count in range(PASSES * PIECES):
+            chunk, s = PASSES + count // PIECES, count % PIECES
+            step = begin + BACK_PACE * count + (1 if count > 0 else 0)
+            bank = WAVE + 1 if count == 0 or count % 2 == 1 else 1
+            narrow = chunk == CHUNKS - 1 and s >= 2
+            at(step, leftover_narrow if narrow else leftover_wide, chunk, s, bank)
             if s == 0:
                 if chunk == PASSES:
                     at(step, quantise_first, chunk, 1)
@@ -284,21 +296,22 @@ def tile_mix_tierx_none_kernel(tc, x, w4_words, w4_scales, out):
                     at(step, quantise_rest, chunk - 1, 1)
             if s == 2:
                 at(step, quantise_rest, chunk, 0)
+            if (chunk, s) == (CHUNKS - 2, 1):
+                at(step, round_part, last_part)
             if s % 2 == 1 and chunk + 1 < CHUNKS:
                 at(step, quantise_first, chunk + 1, s // 2)
         at(step, quantise_rest, CHUNKS - 1, 1)
-        at(order.index((1, 0, 0, 0)), round_slab, last_slab)
 
+        last_tile = (HALVES - 1, N_TILES - 1)
         acc = {}
         for step, (half, n, a, tier) in enumerate(order):
             for work, args in side.get(step, []):
                 work(*args)
             chunk = half * PASSES + a
-            split = (half, n) == (HALVES - 1, N_TILES - 1)
-            opens = a == 0 and (tier == 0 or split)
+            opens = a == 0 and (tier == 0 or (half, n) == last_tile)
+            closes = a == PASSES - 1 and tier == 1
             if opens:
-                acc[n] = psum.tile([P, T_TILE], F32, name="bank%d" % bank_of[(half, n)])
-            last = a == PASSES - 1 and tier == 1
+                acc[n] = bank_tile(sum_bank(half, n))
             nc.tensor.matmul_mx(
                 out=acc[n][:],
                 lhsT=weight_words(a, n).bitcast(E2M1),
@@ -306,13 +319,14 @@ def tile_mix_tierx_none_kernel(tc, x, w4_words, w4_scales, out):
                 rhs=q_code[chunk][:].bitcast(E4M3) if tier == 0 else r_code[chunk][:].bitcast(E5M2),
                 rhs_scale=q_scale[chunk][:] if tier == 0 else r_scale[chunk][:],
                 start=opens,
-                stop=last,
+                stop=closes,
             )
-            if last and split:
+            if closes and (half, n) == last_tile:
                 second_tier = keep.tile([P, T_TILE], F32)
                 for s in range(PIECES):
-                    nc.scalar.copy(out=second_tier[:, s * PIECE : (s + 1) * PIECE], in_=acc[n][:, s * PIECE : (s + 1) * PIECE])
-            elif last:
+                    cols = slice(s * PIECE, (s + 1) * PIECE)
+                    nc.scalar.copy(out=second_tier[:, cols], in_=acc[n][:, cols])
+            elif closes:
                 result = stage.tile([P, T_TILE], F32, name="result")
                 if half == 1 and n < WAVE and n % 2 == 0:
                     nc.vector.tensor_copy(out=result[:], in_=acc[n][:])
@@ -321,11 +335,11 @@ def tile_mix_tierx_none_kernel(tc, x, w4_words, w4_scales, out):
                 t0 = half * T_TILE
                 nc.sync.dma_start(out=out[n * P : (n + 1) * P, t0 : t0 + T_TILE], in_=result[:])
 
-        half, n = HALVES - 1, N_TILES - 1
+        half, n = last_tile
         total = keep.tile([P, T_TILE], F32)
         for s in range(PIECES):
             cols = slice(s * PIECE, (s + 1) * PIECE)
-            small = psum.tile([P, T_TILE], F32, name="bank%d" % bank_of[(half, s)])
+            small = bank_tile(sum_bank(half, s))
             for a in range(PASSES):
                 chunk = half * PASSES + a
                 nc.tensor.matmul_mx(
@@ -341,8 +355,6 @@ def tile_mix_tierx_none_kernel(tc, x, w4_words, w4_scales, out):
                 out=total[:, cols], in0=small[:, :PIECE], in1=second_tier[:, cols], op=mybir.AluOpType.add
             )
             if s % 2 == 1:
-                stored = slice((s - 1) * PIECE, (s + 1) * PIECE)
-                t0 = half * T_TILE
-                nc.sync.dma_start(
-                    out=out[n * P : (n + 1) * P, t0 + stored.start : t0 + stored.stop], in_=total[:, stored]
-                )
+                first = (s - 1) * PIECE
+                t0 = half * T_TILE + first
+                nc.sync.dma_start(out=out[n * P : (n + 1) * P, t0 : t0 + WIDE], in_=total[:, first : first + WIDE])

@@ -26,15 +26,17 @@ PIECE = T_TILE // PACK
 PIECES = T_TILE // PIECE
 WIDE = 2 * PIECE
 WAVE = 6
+SECOND_WAVE = 5
 RUN = 2
 WIDE_RUN = 4
-BACK_LEADS = (5, 3, 1, 0)
-BACK_DELAY = 4
+BACK_LEADS = {1: (7, 5, 3, 0), 2: (8, 5, 3, 0)}
+BACK_BEGIN = 33
 BACK_PACE = 3
+WIDE_CHUNKS = ()
 
 
 def load_widths(chunk):
-    return [WIDE, WIDE] if chunk == 0 else [T_TILE]
+    return [WIDE, WIDE] if chunk < 3 else [T_TILE]
 
 
 def first_widths(chunk):
@@ -43,6 +45,14 @@ def first_widths(chunk):
 
 def rest_widths(chunk):
     return [WIDE, PIECE, PIECE] if chunk < PASSES else [WIDE, WIDE]
+
+
+def is_wide(chunk, s):
+    return chunk in WIDE_CHUNKS and (chunk, s // 2) != (CHUNKS - 1, 1)
+
+
+def back_bank(chunk, s):
+    return WAVE - 2 + s if chunk == 0 else WAVE + s % 2
 
 
 def cut(widths_of):
@@ -66,30 +76,63 @@ def pass_order():
     def alone(half, n):
         return [(half, n, a, tier) for a in range(PASSES) for tier in range(TIERS)]
 
-    final = PASSES - 1
     order = []
-    for a in range(final):
-        order.extend(together(0, range(WAVE), a, range(TIERS)))
-    order.extend(together(0, range(WAVE), final, [0]))
-    order.extend(alone(0, WAVE)[:-1])
-    order.extend(together(0, range(WAVE + 1), final, [1]))
-    order.extend(alone(0, WAVE + 1))
-    order.extend(together(1, range(WAVE - 1), 0, range(TIERS)))
-    order.extend(together(1, [WAVE - 1], 0, range(TIERS)))
-    order.extend(together(1, range(WAVE), 1, range(TIERS)))
-    order.extend(together(1, range(WAVE - 2), final, range(TIERS)))
-    order.extend(together(1, range(WAVE - 2, WAVE), final, range(TIERS)))
-    order.extend(alone(1, WAVE))
-    order.extend([(1, WAVE + 1, a, 1) for a in range(PASSES)])
-    return order
+    for half, wave in enumerate((WAVE, SECOND_WAVE)):
+        for a in range(PASSES):
+            order.extend(together(half, range(wave), a, range(TIERS)))
+        for n in range(wave, N_TILES):
+            order.extend(alone(half, n))
+    return [step for step in order if step[:2] != (HALVES - 1, N_TILES - 1) or step[3] == 1]
 
 
 def sum_bank(half, n):
-    if half == 0:
-        return n if n <= WAVE else 0
-    if n < WAVE - 1:
-        return n + 2
-    return {WAVE - 1: 0, WAVE: 1, WAVE + 1: WAVE + 1}[n]
+    return (half * N_TILES + n) % WAVE
+
+
+def tensor_order():
+    order = pass_order()
+    before = {}
+    for chunk in range(CHUNKS):
+        for s in range(PIECES):
+            if chunk == 0:
+                step = 0
+            elif chunk < PASSES:
+                step = order.index((0, 0, chunk, 0)) - BACK_LEADS[chunk][s]
+            else:
+                step = BACK_BEGIN + BACK_PACE * (PIECES * (chunk - PASSES) + s)
+            before.setdefault(step, []).append(("back", chunk, s))
+    queue = []
+    for step, work in enumerate(order):
+        queue.extend(before.get(step, []))
+        queue.append(("pass",) + work)
+    return queue
+
+
+def vector_order():
+    queue = [("round", 0, 0), ("first", 0, 0), ("first", 0, 1), ("round", 0, 3), ("first", 0, 2), ("first", 0, 3), ("sub", 0, 0), ("sub", 0, 1), ("sub", 0, 2), ("rest", 0, 0), ("first", 1, 0), ("sub", 0, 3), ("rest", 0, 1), ("rest", 0, 2)]
+    queue.extend([("first", 1, 1), ("sub", 1, 0), ("first", 1, 2), ("first", 1, 3), ("sub", 1, 1), ("sub", 1, 2), ("rest", 1, 0), ("first", 2, 0), ("sub", 1, 3), ("rest", 1, 1), ("rest", 1, 2)])
+    queue.extend([("first", 2, 1), ("sub", 2, 0), ("first", 2, 2), ("first", 2, 3), ("sub", 2, 1), ("sub", 2, 2), ("rest", 2, 0), ("sub", 2, 3), ("rest", 2, 1), ("rest", 2, 2), ("first", 3, 0)])
+    for chunk in range(PASSES, CHUNKS):
+        queue.extend([("sub", chunk, 0), ("first", chunk, 1)])
+        if chunk > PASSES:
+            queue.append(("rest", chunk - 1, 1))
+        queue.extend([("sub", chunk, 1), ("sub", chunk, 2), ("rest", chunk, 0)])
+        if chunk + 1 < CHUNKS:
+            queue.append(("first", chunk + 1, 0))
+        queue.append(("sub", chunk, 3))
+    queue.append(("rest", CHUNKS - 1, 1))
+    queue.extend([("empty", 1, n) for n in range(0, SECOND_WAVE, 2)])
+    return queue
+
+
+def scalar_order():
+    queue = [("round", 0, 1), ("round", 0, 2)]
+    queue.extend([("round", c, s) for c in (1, 2) for s in range(PIECES)])
+    queue.extend([("round", 3, 0), ("round", 3, 1), ("empty", 0, 0), ("empty", 0, 1), ("round", 4, 0)])
+    queue.extend([("empty", 0, 2), ("empty", 0, 3), ("round", 4, 1), ("empty", 0, 4), ("empty", 0, 5), ("empty", 0, 6)])
+    queue.extend([("round", 5, 0), ("empty", 0, 7), ("round", 5, 1)])
+    queue.extend([("empty", 1, n) for n in range(N_TILES) if n >= SECOND_WAVE or n % 2 == 1])
+    return queue
 
 
 def tile_mix_tierx_none_kernel(tc, x, w4_words, w4_scales, out):
@@ -160,9 +203,9 @@ def tile_mix_tierx_none_kernel(tc, x, w4_words, w4_scales, out):
                 for r in range(4):
                     nc.sync.dma_start(out=w_scale[a][:].bitcast(I32)[r:P:32, :], in_=scale_rows[r, :, a, :])
                 nc.sync.dma_start(out=w_code[a][:].bitcast(I32), in_=w4_words[a, :, : 2 * WAVE * P].bitcast(I32))
-                if a == PASSES - 1:
-                    late = w4_words[:, :, 2 * WAVE * P :].bitcast(I32).rearrange("a p n -> p a n")
-                    nc.sync.dma_start(out=w_late[:].bitcast(I32), in_=late)
+            if col + width == T_TILE and chunk == PASSES:
+                late = w4_words[:, :, 2 * WAVE * P :].bitcast(I32).rearrange("a p n -> p a n")
+                nc.sync.dma_start(out=w_late[:].bitcast(I32), in_=late)
 
         def weight_words(a, n):
             if n < WAVE:
@@ -173,9 +216,9 @@ def tile_mix_tierx_none_kernel(tc, x, w4_words, w4_scales, out):
             i = [i for i in parts_of(loads, chunk) if loads[i][1] <= col][-1]
             return raw[i][:, :, col - loads[i][1] : col - loads[i][1] + width]
 
-        def round_part(i):
+        def round_part(i, copy):
             chunk, col, width = firsts[i]
-            nc.scalar.copy(
+            copy(
                 out=rounded[i][:].rearrange("p (c i) j -> p c j i", i=RUN),
                 in_=raw_columns(chunk, col, width).rearrange("p j (c i) -> p c j i", i=RUN),
             )
@@ -198,8 +241,12 @@ def tile_mix_tierx_none_kernel(tc, x, w4_words, w4_scales, out):
                 in_=rest[i][:].rearrange("p t j -> p (t j)"),
             )
 
-        def read_back(chunk, col, width, rows, bank):
-            back = bank_tile(bank)
+        def read_back(chunk, s):
+            if is_wide(chunk, s):
+                col, width, rows = s // 2 * WIDE, WIDE, range(s % 2 * 2, s % 2 * 2 + 2)
+            else:
+                col, width, rows = s * PIECE, PIECE, range(PACK)
+            back = bank_tile(back_bank(chunk, s))
             for place, j in enumerate(rows):
                 nc.tensor.matmul_mx(
                     out=back[:, place * width : (place + 1) * width],
@@ -212,134 +259,144 @@ def tile_mix_tierx_none_kernel(tc, x, w4_words, w4_scales, out):
                 )
             return back
 
-        def leftover_narrow(chunk, s, bank):
-            col = s * PIECE
-            back = read_back(chunk, col, PIECE, range(PACK), bank)
-            i = [i for i in parts_of(rests, chunk) if rests[i][1] <= col][-1]
-            local = slice(col - rests[i][1], col - rests[i][1] + PIECE)
-            nc.vector.tensor_tensor(
-                out=rest[i][:, local, :].rearrange("p (c i) j -> p c j i", i=RUN),
-                in0=raw_columns(chunk, col, PIECE).rearrange("p j (c i) -> p c j i", i=RUN),
-                in1=back[:].rearrange("p (j c i) -> p c j i", j=PACK, i=RUN),
-                op=mybir.AluOpType.subtract,
-            )
-
         pairs = {}
 
-        def leftover_wide(chunk, s, bank):
-            part, u = divmod(s, 2)
-            col = part * WIDE
-            back = read_back(chunk, col, WIDE, range(2 * u, 2 * u + 2), bank)
-            if u == 0:
-                pairs[part] = stage.tile([P, 2, WIDE, 2], BF16, name="pairs", bufs=2)
-            nc.vector.tensor_tensor(
-                out=pairs[part][:, u, :, :].rearrange("p (c i) e -> p c e i", i=WIDE_RUN),
-                in0=raw_columns(chunk, col, WIDE)[:, 2 * u : 2 * u + 2, :].rearrange(
-                    "p e (c i) -> p c e i", i=WIDE_RUN
-                ),
-                in1=back[:].rearrange("p (e c i) -> p c e i", e=2, i=WIDE_RUN),
-                op=mybir.AluOpType.subtract,
-            )
-            if u == 1:
-                source = pairs[part][:].rearrange("p u t e -> p (u t e)").bitcast(U32)
-                target = rest[parts_of(rests, chunk)[part]][:].rearrange("p t j -> p (t j)").bitcast(U32)
-                nc.scalar.copy(
-                    out=target.rearrange("p (t u) -> p t u", u=2), in_=source.rearrange("p (u t) -> p t u", u=2)
+        def subtract(back, chunk, s):
+            if is_wide(chunk, s):
+                part, u = divmod(s, 2)
+                if u == 0:
+                    pairs[chunk, part] = keep.tile([P, 2, WIDE, 2], BF16, name="pairs%d_%d" % (chunk, part))
+                nc.vector.tensor_tensor(
+                    out=pairs[chunk, part][:, u, :, :].rearrange("p (c i) e -> p c e i", i=WIDE_RUN),
+                    in0=raw_columns(chunk, part * WIDE, WIDE)[:, 2 * u : 2 * u + 2, :].rearrange(
+                        "p e (c i) -> p c e i", i=WIDE_RUN
+                    ),
+                    in1=back[:].rearrange("p (e c i) -> p c e i", e=2, i=WIDE_RUN),
+                    op=mybir.AluOpType.subtract,
+                )
+            else:
+                col = s * PIECE
+                i = [i for i in parts_of(rests, chunk) if rests[i][1] <= col][-1]
+                local = slice(col - rests[i][1], col - rests[i][1] + PIECE)
+                nc.vector.tensor_tensor(
+                    out=rest[i][:, local, :].rearrange("p (c i) j -> p c j i", i=RUN),
+                    in0=raw_columns(chunk, col, PIECE).rearrange("p j (c i) -> p c j i", i=RUN),
+                    in1=back[:].rearrange("p (j c i) -> p c j i", j=PACK, i=RUN),
+                    op=mybir.AluOpType.subtract,
                 )
 
-        last_part = len(firsts) - 1
-        for i in range(last_part):
-            round_part(i)
-
-        quantise_first(0, 0)
-        quantise_first(0, 1)
-        for s in range(PIECES):
-            leftover_narrow(0, s, WAVE + s % 2)
-            if s + 2 < PIECES:
-                quantise_first(0, s + 2)
-            if s == 2:
-                quantise_rest(0, 0)
-        quantise_rest(0, 1)
-        quantise_rest(0, 2)
-
-        order = pass_order()
-        side = {}
-
-        def at(step, work, *args):
-            side.setdefault(step, []).append((work, args))
-
-        for chunk in range(1, PASSES):
-            steps = [order.index((0, 0, chunk, 0)) - lead for lead in BACK_LEADS]
-            at(steps[0], quantise_first, chunk, 0)
-            at(steps[0], quantise_first, chunk, 1)
-            for s in range(PIECES):
-                at(steps[s], leftover_narrow, chunk, s, WAVE + s % 2)
-                if s + 2 < PIECES:
-                    at(steps[s], quantise_first, chunk, s + 2)
-                if s == 2:
-                    at(steps[s], quantise_rest, chunk, 0)
-            at(steps[-1], quantise_rest, chunk, 1)
-            at(steps[-1], quantise_rest, chunk, 2)
-
-        begin = order.index((0, WAVE, 0, 0)) + BACK_DELAY
-        at(begin, quantise_first, PASSES, 0)
-        for count in range(PASSES * PIECES):
-            chunk, s = PASSES + count // PIECES, count % PIECES
-            step = begin + BACK_PACE * count + (1 if count > 0 else 0)
-            bank = WAVE + 1 if count == 0 or count % 2 == 1 else 1
-            narrow = chunk == CHUNKS - 1 and s >= 2
-            at(step, leftover_narrow if narrow else leftover_wide, chunk, s, bank)
-            if s == 0:
-                if chunk == PASSES:
-                    at(step, quantise_first, chunk, 1)
-                else:
-                    at(step, quantise_rest, chunk - 1, 1)
-            if s == 2:
-                at(step, quantise_rest, chunk, 0)
-            if (chunk, s) == (CHUNKS - 2, 1):
-                at(step, round_part, last_part)
-            if s % 2 == 1 and chunk + 1 < CHUNKS:
-                at(step, quantise_first, chunk + 1, s // 2)
-        at(step, quantise_rest, CHUNKS - 1, 1)
+        def join(chunk, part):
+            source = pairs[chunk, part][:].rearrange("p u t e -> p (u t e)").bitcast(U32)
+            target = rest[parts_of(rests, chunk)[part]][:].rearrange("p t j -> p (t j)").bitcast(U32)
+            nc.scalar.copy(
+                out=target.rearrange("p (t u) -> p t u", u=2), in_=source.rearrange("p (u t) -> p t u", u=2)
+            )
 
         last_tile = (HALVES - 1, N_TILES - 1)
         acc = {}
-        for step, (half, n, a, tier) in enumerate(order):
-            for work, args in side.get(step, []):
-                work(*args)
+        second_tier = keep.tile([P, T_TILE], F32)
+
+        def main_pass(half, n, a, tier):
             chunk = half * PASSES + a
             opens = a == 0 and (tier == 0 or (half, n) == last_tile)
-            closes = a == PASSES - 1 and tier == 1
             if opens:
-                acc[n] = bank_tile(sum_bank(half, n))
+                acc[half, n] = bank_tile(sum_bank(half, n))
             nc.tensor.matmul_mx(
-                out=acc[n][:],
+                out=acc[half, n][:],
                 lhsT=weight_words(a, n).bitcast(E2M1),
                 lhsT_scale=w_scale[a][:, n * P : (n + 1) * P],
                 rhs=q_code[chunk][:].bitcast(E4M3) if tier == 0 else r_code[chunk][:].bitcast(E5M2),
                 rhs_scale=q_scale[chunk][:] if tier == 0 else r_scale[chunk][:],
                 start=opens,
-                stop=closes,
+                stop=a == PASSES - 1 and tier == 1,
             )
-            if closes and (half, n) == last_tile:
-                second_tier = keep.tile([P, T_TILE], F32)
+
+        def empty(half, n, copy):
+            if (half, n) == last_tile:
                 for s in range(PIECES):
                     cols = slice(s * PIECE, (s + 1) * PIECE)
-                    nc.scalar.copy(out=second_tier[:, cols], in_=acc[n][:, cols])
-            elif closes:
+                    copy(out=second_tier[:, cols], in_=acc[half, n][:, cols])
+            else:
                 result = stage.tile([P, T_TILE], F32, name="result")
-                if half == 1 and n < WAVE and n % 2 == 0:
-                    nc.vector.tensor_copy(out=result[:], in_=acc[n][:])
-                else:
-                    nc.scalar.copy(out=result[:], in_=acc[n][:])
+                copy(out=result[:], in_=acc[half, n][:])
                 t0 = half * T_TILE
                 nc.sync.dma_start(out=out[n * P : (n + 1) * P, t0 : t0 + T_TILE], in_=result[:])
+
+        def covering(kind, parts, chunk, col, width):
+            mine = [parts[i] for i in parts_of(parts, chunk)]
+            return [(kind, chunk, k) for k, part in enumerate(mine) if part[1] < col + width and col < part[1] + part[2]]
+
+        def needs(task, bank_user):
+            kind = task[0]
+            if kind == "first":
+                return [("round",) + task[1:]]
+            if kind == "back":
+                chunk, s = task[1:]
+                col, width = (s // 2 * WIDE, WIDE) if is_wide(chunk, s) else (s * PIECE, PIECE)
+                return covering("first", firsts, chunk, col, width) + bank_user.get(back_bank(chunk, s), [])
+            if kind == "sub":
+                return [("back",) + task[1:]]
+            if kind == "join":
+                return [("sub", task[1], 2 * task[2]), ("sub", task[1], 2 * task[2] + 1)]
+            if kind == "rest":
+                chunk, col, width = rests[parts_of(rests, task[1])[task[2]]]
+                pieces = range(col // PIECE, (col + width) // PIECE)
+                return [("join", chunk, s // 2) if is_wide(chunk, s) else ("sub", chunk, s) for s in pieces]
+            if kind == "pass":
+                half, n, a, tier = task[1:]
+                parts = firsts if tier == 0 else rests
+                wanted = covering("first" if tier == 0 else "rest", parts, half * PASSES + a, 0, T_TILE)
+                user = bank_user.get(sum_bank(half, n), [])
+                return wanted + [u for u in user if u != ("empty", half, n)]
+            if kind == "empty":
+                return [("pass", task[1], task[2], PASSES - 1, 1)]
+            return []
+
+        queues = {"vector": vector_order(), "scalar": scalar_order(), "tensor": tensor_order()}
+        issued = set()
+        bank_user = {}
+        backs = {}
+
+        def issue(engine, task):
+            kind, args = task[0], task[1:]
+            copy = nc.vector.tensor_copy if engine == "vector" else nc.scalar.copy
+            if kind == "round":
+                round_part(parts_of(firsts, args[0])[args[1]], copy)
+            elif kind == "first":
+                quantise_first(*args)
+            elif kind == "rest":
+                quantise_rest(*args)
+            elif kind == "back":
+                backs[args] = read_back(*args)
+                bank_user[back_bank(*args)] = [("sub",) + args]
+            elif kind == "sub":
+                subtract(backs[args], *args)
+            elif kind == "join":
+                join(*args)
+            elif kind == "pass":
+                main_pass(*args)
+                bank_user[sum_bank(args[0], args[1])] = [("empty", args[0], args[1])]
+            else:
+                empty(args[0], args[1], copy)
+            issued.add(task)
+
+        place = {engine: 0 for engine in queues}
+        while any(place[engine] < len(queue) for engine, queue in queues.items()):
+            moved = False
+            for engine, queue in queues.items():
+                while place[engine] < len(queue) and all(t in issued for t in needs(queue[place[engine]], bank_user)):
+                    issue(engine, queue[place[engine]])
+                    place[engine] = place[engine] + 1
+                    moved = True
+                    if engine == "tensor":
+                        break
+            assert moved
 
         half, n = last_tile
         total = keep.tile([P, T_TILE], F32)
         for s in range(PIECES):
             cols = slice(s * PIECE, (s + 1) * PIECE)
-            small = bank_tile(sum_bank(half, s))
+            small = bank_tile((sum_bank(half, n) + 1 + s) % N_TILES)
             for a in range(PASSES):
                 chunk = half * PASSES + a
                 nc.tensor.matmul_mx(

@@ -48,7 +48,7 @@ def rest_widths(chunk):
 
 
 def is_wide(chunk, s):
-    return chunk in WIDE_CHUNKS and (chunk, s // 2) != (CHUNKS - 1, 1)
+    return (chunk, s // 2) in ((3, 0), (3, 1), (4, 0), (4, 1), (5, 0))
 
 
 def back_bank(chunk, s):
@@ -109,28 +109,13 @@ def tensor_order():
 
 
 def vector_order():
-    queue = [("round", 0, 0), ("first", 0, 0), ("first", 0, 1), ("round", 0, 3), ("first", 0, 2), ("first", 0, 3), ("sub", 0, 0), ("sub", 0, 1), ("sub", 0, 2), ("rest", 0, 0), ("first", 1, 0), ("sub", 0, 3), ("rest", 0, 1), ("rest", 0, 2)]
-    queue.extend([("first", 1, 1), ("sub", 1, 0), ("first", 1, 2), ("first", 1, 3), ("sub", 1, 1), ("sub", 1, 2), ("rest", 1, 0), ("first", 2, 0), ("sub", 1, 3), ("rest", 1, 1), ("rest", 1, 2)])
-    queue.extend([("first", 2, 1), ("sub", 2, 0), ("first", 2, 2), ("first", 2, 3), ("sub", 2, 1), ("sub", 2, 2), ("rest", 2, 0), ("sub", 2, 3), ("rest", 2, 1), ("rest", 2, 2), ("first", 3, 0)])
-    for chunk in range(PASSES, CHUNKS):
-        queue.extend([("sub", chunk, 0), ("first", chunk, 1)])
-        if chunk > PASSES:
-            queue.append(("rest", chunk - 1, 1))
-        queue.extend([("sub", chunk, 1), ("sub", chunk, 2), ("rest", chunk, 0)])
-        if chunk + 1 < CHUNKS:
-            queue.append(("first", chunk + 1, 0))
-        queue.append(("sub", chunk, 3))
-    queue.append(("rest", CHUNKS - 1, 1))
+    queue = [("round", 0, 0), ("first", 0, 0), ("first", 0, 1), ("round", 0, 3), ("first", 0, 2), ("first", 0, 3), ("sub", 0, 0), ("sub", 0, 1), ("sub", 0, 2), ("rest", 0, 0), ("first", 1, 0), ("sub", 0, 3), ("rest", 0, 1), ("rest", 0, 2), ("first", 1, 1), ("sub", 1, 0), ("first", 1, 2), ("first", 1, 3), ("sub", 1, 1), ("sub", 1, 2), ("rest", 1, 0), ("first", 2, 0), ("sub", 1, 3), ("rest", 1, 1), ("rest", 1, 2), ("first", 2, 1), ("sub", 2, 0), ("first", 2, 2), ("first", 2, 3), ("sub", 2, 1), ("sub", 2, 2), ("rest", 2, 0), ("sub", 2, 3), ("rest", 2, 1), ("rest", 2, 2), ("first", 3, 0), ("empty", 0, 0), ("empty", 0, 2), ("sub", 3, 0), ("first", 3, 1), ("sub", 3, 1), ("sub", 3, 2), ("first", 4, 0), ("sub", 3, 3), ("rest", 3, 0), ("sub", 4, 0), ("first", 4, 1), ("rest", 3, 1), ("sub", 4, 1), ("sub", 4, 2), ("first", 5, 0), ("sub", 4, 3), ("rest", 4, 0), ("sub", 5, 0), ("first", 5, 1), ("rest", 4, 1), ("sub", 5, 1), ("sub", 5, 2), ("sub", 5, 3), ("rest", 5, 0), ("rest", 5, 1)]
     queue.extend([("empty", 1, n) for n in range(0, SECOND_WAVE, 2)])
     return queue
 
 
 def scalar_order():
-    queue = [("round", 0, 1), ("round", 0, 2)]
-    queue.extend([("round", c, s) for c in (1, 2) for s in range(PIECES)])
-    queue.extend([("round", 3, 0), ("round", 3, 1), ("empty", 0, 0), ("empty", 0, 1), ("round", 4, 0)])
-    queue.extend([("empty", 0, 2), ("empty", 0, 3), ("round", 4, 1), ("empty", 0, 4), ("empty", 0, 5), ("empty", 0, 6)])
-    queue.extend([("round", 5, 0), ("empty", 0, 7), ("round", 5, 1)])
+    queue = [("round", 0, 1), ("round", 0, 2), ("round", 1, 0), ("round", 1, 1), ("round", 1, 2), ("round", 1, 3), ("round", 2, 0), ("round", 2, 1), ("round", 2, 2), ("round", 2, 3), ("round", 3, 0), ("round", 3, 1), ("empty", 0, 1), ("empty", 0, 3), ("round", 4, 0), ("empty", 0, 4), ("empty", 0, 5), ("join", 3, 0), ("round", 4, 1), ("join", 3, 1), ("empty", 0, 6), ("round", 5, 0), ("join", 4, 0), ("round", 5, 1), ("join", 4, 1), ("join", 5, 0), ("empty", 0, 7)]
     queue.extend([("empty", 1, n) for n in range(N_TILES) if n >= SECOND_WAVE or n % 2 == 1])
     return queue
 

@@ -29,7 +29,7 @@ WAVE = 6
 SECOND_WAVE = 5
 RUN = 2
 WIDE_RUN = 4
-BACK_LEADS = {1: (7, 5, 3, 0), 2: (8, 5, 3, 0)}
+BACK_LEADS = {1: (6, 4, 2, 0), 2: (7, 5, 3, 0)}
 BACK_BEGIN = 33
 BACK_PACE = 3
 WIDE_CHUNKS = ()
@@ -44,7 +44,7 @@ def first_widths(chunk):
 
 
 def rest_widths(chunk):
-    return [WIDE, PIECE, PIECE] if chunk < PASSES else [WIDE, WIDE]
+    return [PIECE] * PIECES if chunk == 0 else [WIDE, PIECE, PIECE] if chunk < PASSES else [WIDE, WIDE]
 
 
 def is_wide(chunk, s):
@@ -109,7 +109,7 @@ def tensor_order():
 
 
 def vector_order():
-    queue = [("round", 0, 0), ("first", 0, 0), ("first", 0, 1), ("round", 0, 3), ("first", 0, 2), ("first", 0, 3), ("sub", 0, 0), ("sub", 0, 1), ("sub", 0, 2), ("rest", 0, 0), ("first", 1, 0), ("sub", 0, 3), ("rest", 0, 1), ("rest", 0, 2), ("first", 1, 1), ("sub", 1, 0), ("first", 1, 2), ("first", 1, 3), ("sub", 1, 1), ("sub", 1, 2), ("rest", 1, 0), ("first", 2, 0), ("sub", 1, 3), ("rest", 1, 1), ("rest", 1, 2), ("first", 2, 1), ("sub", 2, 0), ("first", 2, 2), ("first", 2, 3), ("sub", 2, 1), ("sub", 2, 2), ("rest", 2, 0), ("sub", 2, 3), ("rest", 2, 1), ("rest", 2, 2), ("first", 3, 0), ("empty", 0, 0), ("empty", 0, 2), ("sub", 3, 0), ("first", 3, 1), ("sub", 3, 1), ("sub", 3, 2), ("first", 4, 0), ("sub", 3, 3), ("rest", 3, 0), ("sub", 4, 0), ("first", 4, 1), ("rest", 3, 1), ("sub", 4, 1), ("sub", 4, 2), ("first", 5, 0), ("sub", 4, 3), ("rest", 4, 0), ("sub", 5, 0), ("first", 5, 1), ("rest", 4, 1), ("sub", 5, 1), ("sub", 5, 2), ("sub", 5, 3), ("rest", 5, 0), ("rest", 5, 1)]
+    queue = [("round", 0, 0), ("first", 0, 0), ("first", 0, 1), ("round", 0, 3), ("sub", 0, 0), ("first", 0, 2), ("first", 0, 3), ("sub", 0, 1), ("rest", 0, 0), ("sub", 0, 2), ("rest", 0, 1), ("sub", 0, 3), ("rest", 0, 2), ("first", 1, 0), ("rest", 0, 3), ("first", 1, 1), ("first", 1, 2), ("sub", 1, 0), ("first", 1, 3), ("sub", 1, 1), ("sub", 1, 2), ("rest", 1, 0), ("first", 2, 0), ("sub", 1, 3), ("rest", 1, 1), ("rest", 1, 2), ("first", 2, 1), ("sub", 2, 0), ("first", 2, 2), ("first", 2, 3), ("sub", 2, 1), ("sub", 2, 2), ("rest", 2, 0), ("sub", 2, 3), ("rest", 2, 1), ("rest", 2, 2), ("first", 3, 0), ("empty", 0, 0), ("empty", 0, 2), ("sub", 3, 0), ("first", 3, 1), ("sub", 3, 1), ("sub", 3, 2), ("first", 4, 0), ("sub", 3, 3), ("rest", 3, 0), ("sub", 4, 0), ("first", 4, 1), ("rest", 3, 1), ("sub", 4, 1), ("sub", 4, 2), ("first", 5, 0), ("sub", 4, 3), ("rest", 4, 0), ("sub", 5, 0), ("first", 5, 1), ("rest", 4, 1), ("sub", 5, 1), ("sub", 5, 2), ("sub", 5, 3), ("rest", 5, 0), ("rest", 5, 1)]
     queue.extend([("empty", 1, n) for n in range(0, SECOND_WAVE, 2)])
     return queue
 
@@ -138,9 +138,26 @@ def tile_mix_tierx_none_kernel(tc, x, w4_words, w4_scales, out):
         firsts = cut(first_widths)
         rests = cut(rest_widths)
 
-        w_scale = kept("w_scale", PASSES, lambda a: [P, N], U8)
-        for a in range(PASSES):
-            nc.vector.memset(w_scale[a][:].bitcast(U32), 0)
+        planes = keep.tile([P, PASSES * N], U8, align_bytes=64)
+        nc.vector.memset(planes[:].bitcast(U32), 0)
+        w_scale = [planes[:, a * N : (a + 1) * N] for a in range(PASSES)]
+
+        warm_code = keep.tile([P, WIDE], U32, align_bytes=64)
+        warm_scale = keep.tile([P, WIDE], U8, align_bytes=64)
+        nc.vector.quantize_mx(
+            out=warm_code[:].bitcast(E4M3), scales=warm_scale[:], in_=planes[:, : 2 * PACK * WIDE].bitcast(BF16)
+        )
+        warm = bank_tile(0)
+        for count in range(6):
+            nc.tensor.matmul_mx(
+                out=warm[:, :WIDE],
+                lhsT=warm_code[:, :P].bitcast(E4M3),
+                lhsT_scale=warm_scale[:, :P],
+                rhs=warm_code[:].bitcast(E4M3),
+                rhs_scale=warm_scale[:],
+                start=True,
+                stop=True,
+            )
         w_code = kept("w_code", PASSES, lambda a: [P, 2 * WAVE * P], U8)
         w_late = keep.tile([P, PASSES, 2 * (N - WAVE * P)], U8, align_bytes=64)
         raw = kept("raw", len(loads), lambda i: [P, PACK, loads[i][2]], F32)
@@ -186,7 +203,7 @@ def tile_mix_tierx_none_kernel(tc, x, w4_words, w4_scales, out):
             nc.sync.dma_start(out=raw[i][:], in_=rows.rearrange("(p j) t -> p j t", j=PACK))
             if col + width == T_TILE and half == 0:
                 for r in range(4):
-                    nc.sync.dma_start(out=w_scale[a][:].bitcast(I32)[r:P:32, :], in_=scale_rows[r, :, a, :])
+                    nc.sync.dma_start(out=w_scale[a].bitcast(I32)[r:P:32, :], in_=scale_rows[r, :, a, :])
                 nc.sync.dma_start(out=w_code[a][:].bitcast(I32), in_=w4_words[a, :, : 2 * WAVE * P].bitcast(I32))
             if col + width == T_TILE and chunk == PASSES:
                 late = w4_words[:, :, 2 * WAVE * P :].bitcast(I32).rearrange("a p n -> p a n")

@@ -22,37 +22,27 @@ N_TILES = N // P
 HALVES = T // T_TILE
 CHUNKS = HALVES * PASSES
 TIERS = 2
+LAST_TILE = (HALVES - 1, N_TILES - 1)
 PIECE = T_TILE // PACK
 PIECES = T_TILE // PIECE
-WIDE = 2 * PIECE
-WAVE = 6
-SECOND_WAVE = 5
+PAIR = 2 * PIECE
+BANKS = 8
+SUM_BANKS = 6
+WAVES = (SUM_BANKS, SUM_BANKS - 1)
 RUN = 2
-WIDE_RUN = 4
-BACK_LEADS = {1: (6, 4, 2, 0), 2: (7, 5, 3, 0)}
-BACK_BEGIN = 33
-BACK_PACE = 3
-WIDE_CHUNKS = ()
+FIRST_PACE = 2
+SECOND_PACE = 3
+SECOND_LEAD = 3
+WARM_ZEROS = 4
+WARM_EYE = 2
 
 
 def load_widths(chunk):
-    return [WIDE, WIDE] if chunk < 3 else [T_TILE]
+    return [PAIR, PAIR] if chunk < PASSES else [T_TILE]
 
 
-def first_widths(chunk):
-    return [PIECE] * PIECES if chunk < PASSES else [WIDE, WIDE]
-
-
-def rest_widths(chunk):
-    return [PIECE] * PIECES if chunk == 0 else [WIDE, PIECE, PIECE] if chunk < PASSES else [WIDE, WIDE]
-
-
-def is_wide(chunk, s):
-    return (chunk, s // 2) in ((3, 0), (3, 1), (4, 0), (4, 1), (5, 0))
-
-
-def back_bank(chunk, s):
-    return WAVE - 2 + s if chunk == 0 else WAVE + s % 2
+def step_widths(chunk):
+    return [PIECE] * PIECES if chunk < PASSES else [PAIR, PAIR]
 
 
 def cut(widths_of):
@@ -70,53 +60,71 @@ def parts_of(parts, chunk):
 
 
 def pass_order():
-    def together(half, group, a, tiers):
-        return [(half, n, a, tier) for tier in tiers for n in group]
-
-    def alone(half, n):
-        return [(half, n, a, tier) for a in range(PASSES) for tier in range(TIERS)]
-
     order = []
-    for half, wave in enumerate((WAVE, SECOND_WAVE)):
-        for a in range(PASSES):
-            order.extend(together(half, range(wave), a, range(TIERS)))
-        for n in range(wave, N_TILES):
-            order.extend(alone(half, n))
-    return [step for step in order if step[:2] != (HALVES - 1, N_TILES - 1) or step[3] == 1]
+    for half, wave in enumerate(WAVES):
+        order.extend([(half, n, a, tier) for a in range(PASSES) for tier in range(TIERS) for n in range(wave)])
+        order.extend([(half, n, a, tier) for n in range(wave, N_TILES) for a in range(PASSES) for tier in range(TIERS)])
+    return [step for step in order if step[:2] != LAST_TILE or step[3] == 1]
 
 
 def sum_bank(half, n):
-    return (half * N_TILES + n) % WAVE
+    return (half * N_TILES + n) % SUM_BANKS
+
+
+def back_bank(chunk, s):
+    return BANKS - PIECES + s if chunk == 0 else SUM_BANKS + s % 2
 
 
 def tensor_order():
     order = pass_order()
-    before = {}
+    second = order.index((0, WAVES[0], 0, 0)) - SECOND_LEAD
+    ahead_of = {}
     for chunk in range(CHUNKS):
         for s in range(PIECES):
-            if chunk == 0:
-                step = 0
-            elif chunk < PASSES:
-                step = order.index((0, 0, chunk, 0)) - BACK_LEADS[chunk][s]
+            if chunk < PASSES:
+                step = max(0, order.index((0, 0, chunk, 0)) - FIRST_PACE * (PIECES - 1 - s))
             else:
-                step = BACK_BEGIN + BACK_PACE * (PIECES * (chunk - PASSES) + s)
-            before.setdefault(step, []).append(("back", chunk, s))
+                step = second + SECOND_PACE * (PIECES * (chunk - PASSES) + s)
+            ahead_of.setdefault(step, []).append(("back", chunk, s))
     queue = []
     for step, work in enumerate(order):
-        queue.extend(before.get(step, []))
+        queue.extend(ahead_of.get(step, []))
         queue.append(("pass",) + work)
     return queue
 
 
 def vector_order():
-    queue = [("round", 0, 0), ("first", 0, 0), ("first", 0, 1), ("round", 0, 3), ("sub", 0, 0), ("first", 0, 2), ("first", 0, 3), ("sub", 0, 1), ("rest", 0, 0), ("sub", 0, 2), ("rest", 0, 1), ("sub", 0, 3), ("rest", 0, 2), ("first", 1, 0), ("rest", 0, 3), ("first", 1, 1), ("first", 1, 2), ("sub", 1, 0), ("first", 1, 3), ("sub", 1, 1), ("sub", 1, 2), ("rest", 1, 0), ("first", 2, 0), ("sub", 1, 3), ("rest", 1, 1), ("rest", 1, 2), ("first", 2, 1), ("sub", 2, 0), ("first", 2, 2), ("first", 2, 3), ("sub", 2, 1), ("sub", 2, 2), ("rest", 2, 0), ("sub", 2, 3), ("rest", 2, 1), ("rest", 2, 2), ("first", 3, 0), ("empty", 0, 0), ("empty", 0, 2), ("sub", 3, 0), ("first", 3, 1), ("sub", 3, 1), ("sub", 3, 2), ("first", 4, 0), ("sub", 3, 3), ("rest", 3, 0), ("sub", 4, 0), ("first", 4, 1), ("rest", 3, 1), ("sub", 4, 1), ("sub", 4, 2), ("first", 5, 0), ("sub", 4, 3), ("rest", 4, 0), ("sub", 5, 0), ("first", 5, 1), ("rest", 4, 1), ("sub", 5, 1), ("sub", 5, 2), ("sub", 5, 3), ("rest", 5, 0), ("rest", 5, 1)]
-    queue.extend([("empty", 1, n) for n in range(0, SECOND_WAVE, 2)])
+    queue = [("round", 0, 0), ("first", 0, 0), ("first", 0, 1), ("round", 0, 3)]
+    for chunk in range(PASSES):
+        queue.extend([("sub", chunk, 0), ("first", chunk, 2), ("first", chunk, 3)])
+        for s in range(1, PIECES):
+            queue.extend([("sub", chunk, s), ("second", chunk, s - 1)])
+        if chunk + 1 < PASSES:
+            queue.extend([("first", chunk + 1, 0), ("second", chunk, PIECES - 1), ("first", chunk + 1, 1)])
+        else:
+            queue.extend([("second", chunk, PIECES - 1), ("first", chunk + 1, 0)])
+    for chunk in range(PASSES, CHUNKS):
+        queue.extend([("sub", chunk, 0), ("first", chunk, 1)])
+        if chunk > PASSES:
+            queue.append(("second", chunk - 1, 1))
+        queue.extend([("sub", chunk, 1), ("sub", chunk, 2), ("second", chunk, 0)])
+        if chunk + 1 < CHUNKS:
+            queue.append(("first", chunk + 1, 0))
+        queue.append(("sub", chunk, 3))
+    queue.append(("second", CHUNKS - 1, 1))
+    queue.extend([("empty", 1, n) for n in range(0, WAVES[1], 2)])
     return queue
 
 
 def scalar_order():
-    queue = [("round", 0, 1), ("round", 0, 2), ("round", 1, 0), ("round", 1, 1), ("round", 1, 2), ("round", 1, 3), ("round", 2, 0), ("round", 2, 1), ("round", 2, 2), ("round", 2, 3), ("round", 3, 0), ("round", 3, 1), ("empty", 0, 1), ("empty", 0, 3), ("round", 4, 0), ("empty", 0, 4), ("empty", 0, 5), ("join", 3, 0), ("round", 4, 1), ("join", 3, 1), ("empty", 0, 6), ("round", 5, 0), ("join", 4, 0), ("round", 5, 1), ("join", 4, 1), ("join", 5, 0), ("empty", 0, 7)]
-    queue.extend([("empty", 1, n) for n in range(N_TILES) if n >= SECOND_WAVE or n % 2 == 1])
+    queue = [("round", 0, 1), ("round", 0, 2)]
+    queue.extend([("round", chunk, k) for chunk in range(1, PASSES + 1) for k in range(len(step_widths(chunk)))])
+    for k in range(2):
+        queue.extend([("empty", 0, 2 * k), ("empty", 0, 2 * k + 1), ("round", CHUNKS - 2, k)])
+    queue.extend([("empty", 0, n) for n in range(4, WAVES[0])])
+    for k in range(2):
+        queue.extend([("empty", 0, WAVES[0] + k), ("round", CHUNKS - 1, k)])
+    queue.extend([("empty", 1, n) for n in range(N_TILES) if n >= WAVES[1] or n % 2 == 1])
     return queue
 
 
@@ -135,47 +143,48 @@ def tile_mix_tierx_none_kernel(tc, x, w4_words, w4_scales, out):
             return [keep.tile(shape_of(i), dtype, align_bytes=64, name="%s%d" % (name, i)) for i in range(count)]
 
         loads = cut(load_widths)
-        firsts = cut(first_widths)
-        rests = cut(rest_widths)
+        steps = cut(step_widths)
 
         planes = keep.tile([P, PASSES * N], U8, align_bytes=64)
         nc.vector.memset(planes[:].bitcast(U32), 0)
         w_scale = [planes[:, a * N : (a + 1) * N] for a in range(PASSES)]
 
-        warm_code = keep.tile([P, WIDE], U32, align_bytes=64)
-        warm_scale = keep.tile([P, WIDE], U8, align_bytes=64)
+        def warm_up(count, code, scale, width):
+            unread = bank_tile(0)
+            for turn in range(count):
+                nc.tensor.matmul_mx(
+                    out=unread[:, :width],
+                    lhsT=code[:, :P].bitcast(E4M3),
+                    lhsT_scale=scale[:, :P],
+                    rhs=code[:, :width].bitcast(E4M3),
+                    rhs_scale=scale[:, :width],
+                    start=True,
+                    stop=True,
+                )
+
+        zero_code = keep.tile([P, PAIR], U32, align_bytes=64)
+        zero_scale = keep.tile([P, PAIR], U8, align_bytes=64)
         nc.vector.quantize_mx(
-            out=warm_code[:].bitcast(E4M3), scales=warm_scale[:], in_=planes[:, : 2 * PACK * WIDE].bitcast(BF16)
+            out=zero_code[:].bitcast(E4M3), scales=zero_scale[:], in_=planes[:, : 2 * PACK * PAIR].bitcast(BF16)
         )
-        warm = bank_tile(0)
-        for count in range(6):
-            nc.tensor.matmul_mx(
-                out=warm[:, :WIDE],
-                lhsT=warm_code[:, :P].bitcast(E4M3),
-                lhsT_scale=warm_scale[:, :P],
-                rhs=warm_code[:].bitcast(E4M3),
-                rhs_scale=warm_scale[:],
-                start=True,
-                stop=True,
-            )
-        w_code = kept("w_code", PASSES, lambda a: [P, 2 * WAVE * P], U8)
-        w_late = keep.tile([P, PASSES, 2 * (N - WAVE * P)], U8, align_bytes=64)
+        warm_up(WARM_ZEROS, zero_code, zero_scale, PAIR)
+
+        early = WAVES[0] * P
+        w_code = kept("w_code", PASSES, lambda a: [P, 2 * early], U8)
+        w_late = keep.tile([P, PASSES, 2 * (N - early)], U8, align_bytes=64)
         raw = kept("raw", len(loads), lambda i: [P, PACK, loads[i][2]], F32)
-        rounded = kept("rounded", len(firsts), lambda i: [P, firsts[i][2], PACK], BF16)
-        rest = kept("rest", len(rests), lambda i: [P, rests[i][2], PACK], BF16)
+        rounded = kept("rounded", len(steps), lambda i: [P, steps[i][2], PACK], BF16)
+        rest = kept("rest", len(steps), lambda i: [P, steps[i][2], PACK], BF16)
         q_code = kept("q_code", CHUNKS, lambda c: [P, T_TILE], U32)
         q_scale = kept("q_scale", CHUNKS, lambda c: [P, T_TILE], U8)
         r_code = kept("r_code", CHUNKS, lambda c: [P, T_TILE], U32)
         r_scale = kept("r_scale", CHUNKS, lambda c: [P, T_TILE], U8)
 
-        marks = keep.tile([P, PACK * P + PACK], BF16)
+        ramp = keep.tile([P, 2 * P + 2], F32)
         nc.gpsimd.iota(
-            marks[:],
-            pattern=[[-1, PACK * P + PACK]],
-            base=PACK - 1,
-            channel_multiplier=PACK,
-            allow_small_or_imprecise_dtypes=True,
+            ramp[:], pattern=[[-1, 2 * P + 2]], base=2, channel_multiplier=2, allow_small_or_imprecise_dtypes=True
         )
+        marks = ramp[:].bitcast(BF16)
         eye_rows = kept("eye_rows", PACK, lambda j: [P, PACK * P], BF16)
         eye_code = keep.tile([P, PACK * P], U32, align_bytes=64)
         eye_scale = keep.tile([P, PACK * P], U8, align_bytes=64)
@@ -185,7 +194,7 @@ def tile_mix_tierx_none_kernel(tc, x, w4_words, w4_scales, out):
                 nc.vector.tensor_scalar(
                     out=eye_rows[j][:],
                     in0=marks[:, PACK - 1 - j : PACK - 1 - j + PACK * P],
-                    scalar1=0.0,
+                    scalar1=1.0,
                     scalar2=None,
                     op0=mybir.AluOpType.is_equal,
                 )
@@ -194,6 +203,8 @@ def tile_mix_tierx_none_kernel(tc, x, w4_words, w4_scales, out):
                 nc.vector.quantize_mx(
                     out=eye_code[:, block].bitcast(E4M3), scales=eye_scale[:, block], in_=eye_rows[j - trail][:]
                 )
+
+        warm_up(WARM_EYE, eye_code, eye_scale, T_TILE)
 
         scale_rows = w4_scales.bitcast(I32).rearrange("a (q r) n -> r q a n", r=4)
         for i, (chunk, col, width) in enumerate(loads):
@@ -204,103 +215,68 @@ def tile_mix_tierx_none_kernel(tc, x, w4_words, w4_scales, out):
             if col + width == T_TILE and half == 0:
                 for r in range(4):
                     nc.sync.dma_start(out=w_scale[a].bitcast(I32)[r:P:32, :], in_=scale_rows[r, :, a, :])
-                nc.sync.dma_start(out=w_code[a][:].bitcast(I32), in_=w4_words[a, :, : 2 * WAVE * P].bitcast(I32))
+                nc.sync.dma_start(out=w_code[a][:].bitcast(I32), in_=w4_words[a, :, : 2 * early].bitcast(I32))
             if col + width == T_TILE and chunk == PASSES:
-                late = w4_words[:, :, 2 * WAVE * P :].bitcast(I32).rearrange("a p n -> p a n")
+                late = w4_words[:, :, 2 * early :].bitcast(I32).rearrange("a p n -> p a n")
                 nc.sync.dma_start(out=w_late[:].bitcast(I32), in_=late)
 
         def weight_words(a, n):
-            if n < WAVE:
+            if n * P < early:
                 return w_code[a][:, 2 * n * P : 2 * (n + 1) * P]
-            return w_late[:, a, 2 * (n - WAVE) * P : 2 * (n - WAVE + 1) * P]
+            return w_late[:, a, 2 * (n * P - early) : 2 * ((n + 1) * P - early)]
 
         def raw_columns(chunk, col, width):
             i = [i for i in parts_of(loads, chunk) if loads[i][1] <= col][-1]
             return raw[i][:, :, col - loads[i][1] : col - loads[i][1] + width]
 
-        def round_part(i, copy):
-            chunk, col, width = firsts[i]
+        def round_part(chunk, k, copy):
+            i = parts_of(steps, chunk)[k]
             copy(
                 out=rounded[i][:].rearrange("p (c i) j -> p c j i", i=RUN),
-                in_=raw_columns(chunk, col, width).rearrange("p j (c i) -> p c j i", i=RUN),
+                in_=raw_columns(*steps[i]).rearrange("p j (c i) -> p c j i", i=RUN),
             )
 
-        def quantise_first(chunk, part):
-            i = parts_of(firsts, chunk)[part]
-            cols = slice(firsts[i][1], firsts[i][1] + firsts[i][2])
+        def quantise(chunk, k, source, code, scale, dtype):
+            i = parts_of(steps, chunk)[k]
+            cols = slice(steps[i][1], steps[i][1] + steps[i][2])
             nc.vector.quantize_mx(
-                out=q_code[chunk][:, cols].bitcast(E4M3),
-                scales=q_scale[chunk][:, cols],
-                in_=rounded[i][:].rearrange("p t j -> p (t j)"),
-            )
-
-        def quantise_rest(chunk, part):
-            i = parts_of(rests, chunk)[part]
-            cols = slice(rests[i][1], rests[i][1] + rests[i][2])
-            nc.vector.quantize_mx(
-                out=r_code[chunk][:, cols].bitcast(E5M2),
-                scales=r_scale[chunk][:, cols],
-                in_=rest[i][:].rearrange("p t j -> p (t j)"),
+                out=code[chunk][:, cols].bitcast(dtype),
+                scales=scale[chunk][:, cols],
+                in_=source[i][:].rearrange("p t j -> p (t j)"),
             )
 
         def read_back(chunk, s):
-            if is_wide(chunk, s):
-                col, width, rows = s // 2 * WIDE, WIDE, range(s % 2 * 2, s % 2 * 2 + 2)
-            else:
-                col, width, rows = s * PIECE, PIECE, range(PACK)
             back = bank_tile(back_bank(chunk, s))
-            for place, j in enumerate(rows):
+            cols = slice(s * PIECE, (s + 1) * PIECE)
+            for j in range(PACK):
                 nc.tensor.matmul_mx(
-                    out=back[:, place * width : (place + 1) * width],
+                    out=back[:, j * PIECE : (j + 1) * PIECE],
                     lhsT=eye_code[:, j * P : (j + 1) * P].bitcast(E4M3),
                     lhsT_scale=eye_scale[:, j * P : (j + 1) * P],
-                    rhs=q_code[chunk][:, col : col + width].bitcast(E4M3),
-                    rhs_scale=q_scale[chunk][:, col : col + width],
+                    rhs=q_code[chunk][:, cols].bitcast(E4M3),
+                    rhs_scale=q_scale[chunk][:, cols],
                     start=True,
                     stop=True,
                 )
             return back
 
-        pairs = {}
-
         def subtract(back, chunk, s):
-            if is_wide(chunk, s):
-                part, u = divmod(s, 2)
-                if u == 0:
-                    pairs[chunk, part] = keep.tile([P, 2, WIDE, 2], BF16, name="pairs%d_%d" % (chunk, part))
-                nc.vector.tensor_tensor(
-                    out=pairs[chunk, part][:, u, :, :].rearrange("p (c i) e -> p c e i", i=WIDE_RUN),
-                    in0=raw_columns(chunk, part * WIDE, WIDE)[:, 2 * u : 2 * u + 2, :].rearrange(
-                        "p e (c i) -> p c e i", i=WIDE_RUN
-                    ),
-                    in1=back[:].rearrange("p (e c i) -> p c e i", e=2, i=WIDE_RUN),
-                    op=mybir.AluOpType.subtract,
-                )
-            else:
-                col = s * PIECE
-                i = [i for i in parts_of(rests, chunk) if rests[i][1] <= col][-1]
-                local = slice(col - rests[i][1], col - rests[i][1] + PIECE)
-                nc.vector.tensor_tensor(
-                    out=rest[i][:, local, :].rearrange("p (c i) j -> p c j i", i=RUN),
-                    in0=raw_columns(chunk, col, PIECE).rearrange("p j (c i) -> p c j i", i=RUN),
-                    in1=back[:].rearrange("p (j c i) -> p c j i", j=PACK, i=RUN),
-                    op=mybir.AluOpType.subtract,
-                )
-
-        def join(chunk, part):
-            source = pairs[chunk, part][:].rearrange("p u t e -> p (u t e)").bitcast(U32)
-            target = rest[parts_of(rests, chunk)[part]][:].rearrange("p t j -> p (t j)").bitcast(U32)
-            nc.scalar.copy(
-                out=target.rearrange("p (t u) -> p t u", u=2), in_=source.rearrange("p (u t) -> p t u", u=2)
+            col = s * PIECE
+            i = [i for i in parts_of(steps, chunk) if steps[i][1] <= col][-1]
+            local = slice(col - steps[i][1], col - steps[i][1] + PIECE)
+            nc.vector.tensor_tensor(
+                out=rest[i][:, local, :].rearrange("p (c i) j -> p c j i", i=RUN),
+                in0=raw_columns(chunk, col, PIECE).rearrange("p j (c i) -> p c j i", i=RUN),
+                in1=back[:].rearrange("p (j c i) -> p c j i", j=PACK, i=RUN),
+                op=mybir.AluOpType.subtract,
             )
 
-        last_tile = (HALVES - 1, N_TILES - 1)
         acc = {}
         second_tier = keep.tile([P, T_TILE], F32)
 
         def main_pass(half, n, a, tier):
             chunk = half * PASSES + a
-            opens = a == 0 and (tier == 0 or (half, n) == last_tile)
+            opens = a == 0 and (tier == 0 or (half, n) == LAST_TILE)
             if opens:
                 acc[half, n] = bank_tile(sum_bank(half, n))
             nc.tensor.matmul_mx(
@@ -314,7 +290,7 @@ def tile_mix_tierx_none_kernel(tc, x, w4_words, w4_scales, out):
             )
 
         def empty(half, n, copy):
-            if (half, n) == last_tile:
+            if (half, n) == LAST_TILE:
                 for s in range(PIECES):
                     cols = slice(s * PIECE, (s + 1) * PIECE)
                     copy(out=second_tier[:, cols], in_=acc[half, n][:, cols])
@@ -324,81 +300,68 @@ def tile_mix_tierx_none_kernel(tc, x, w4_words, w4_scales, out):
                 t0 = half * T_TILE
                 nc.sync.dma_start(out=out[n * P : (n + 1) * P, t0 : t0 + T_TILE], in_=result[:])
 
-        def covering(kind, parts, chunk, col, width):
-            mine = [parts[i] for i in parts_of(parts, chunk)]
-            return [(kind, chunk, k) for k, part in enumerate(mine) if part[1] < col + width and col < part[1] + part[2]]
+        frees = {}
 
-        def needs(task, bank_user):
-            kind = task[0]
+        def needs(task):
+            kind, args = task[0], task[1:]
             if kind == "first":
-                return [("round",) + task[1:]]
+                return [("round",) + args]
             if kind == "back":
-                chunk, s = task[1:]
-                col, width = (s // 2 * WIDE, WIDE) if is_wide(chunk, s) else (s * PIECE, PIECE)
-                return covering("first", firsts, chunk, col, width) + bank_user.get(back_bank(chunk, s), [])
+                chunk, s = args
+                return [("first", chunk, s * PIECE // step_widths(chunk)[0])] + frees.get(back_bank(chunk, s), [])
             if kind == "sub":
-                return [("back",) + task[1:]]
-            if kind == "join":
-                return [("sub", task[1], 2 * task[2]), ("sub", task[1], 2 * task[2] + 1)]
-            if kind == "rest":
-                chunk, col, width = rests[parts_of(rests, task[1])[task[2]]]
-                pieces = range(col // PIECE, (col + width) // PIECE)
-                return [("join", chunk, s // 2) if is_wide(chunk, s) else ("sub", chunk, s) for s in pieces]
+                return [("back",) + args]
+            if kind == "second":
+                chunk, col, width = steps[parts_of(steps, args[0])[args[1]]]
+                return [("sub", chunk, s) for s in range(col // PIECE, (col + width) // PIECE)]
             if kind == "pass":
-                half, n, a, tier = task[1:]
-                parts = firsts if tier == 0 else rests
-                wanted = covering("first" if tier == 0 else "rest", parts, half * PASSES + a, 0, T_TILE)
-                user = bank_user.get(sum_bank(half, n), [])
-                return wanted + [u for u in user if u != ("empty", half, n)]
+                half, n, a, tier = args
+                chunk = half * PASSES + a
+                operand = [("second" if tier else "first", chunk, k) for k in range(len(step_widths(chunk)))]
+                return operand + ([] if (half, n) in acc else frees.get(sum_bank(half, n), []))
             if kind == "empty":
-                return [("pass", task[1], task[2], PASSES - 1, 1)]
+                return [("pass",) + args + (PASSES - 1, 1)]
             return []
 
-        queues = {"vector": vector_order(), "scalar": scalar_order(), "tensor": tensor_order()}
-        issued = set()
-        bank_user = {}
         backs = {}
 
         def issue(engine, task):
             kind, args = task[0], task[1:]
             copy = nc.vector.tensor_copy if engine == "vector" else nc.scalar.copy
             if kind == "round":
-                round_part(parts_of(firsts, args[0])[args[1]], copy)
+                round_part(*args, copy)
             elif kind == "first":
-                quantise_first(*args)
-            elif kind == "rest":
-                quantise_rest(*args)
+                quantise(*args, rounded, q_code, q_scale, E4M3)
+            elif kind == "second":
+                quantise(*args, rest, r_code, r_scale, E5M2)
             elif kind == "back":
                 backs[args] = read_back(*args)
-                bank_user[back_bank(*args)] = [("sub",) + args]
+                frees[back_bank(*args)] = [("sub",) + args]
             elif kind == "sub":
                 subtract(backs[args], *args)
-            elif kind == "join":
-                join(*args)
             elif kind == "pass":
                 main_pass(*args)
-                bank_user[sum_bank(args[0], args[1])] = [("empty", args[0], args[1])]
+                frees[sum_bank(*args[:2])] = [("empty",) + args[:2]]
             else:
-                empty(args[0], args[1], copy)
-            issued.add(task)
+                empty(*args, copy)
 
-        place = {engine: 0 for engine in queues}
-        while any(place[engine] < len(queue) for engine, queue in queues.items()):
-            moved = False
+        queues = {"vector": vector_order(), "scalar": scalar_order(), "tensor": tensor_order()}
+        issued = set()
+        while any(queues.values()):
+            before = len(issued)
             for engine, queue in queues.items():
-                while place[engine] < len(queue) and all(t in issued for t in needs(queue[place[engine]], bank_user)):
-                    issue(engine, queue[place[engine]])
-                    place[engine] = place[engine] + 1
-                    moved = True
-                    if engine == "tensor":
-                        break
-            assert moved
+                if queue and all(step in issued for step in needs(queue[0])):
+                    task = queue[0]
+                    issue(engine, task)
+                    issued.add(task)
+                    queue.remove(task)
+            assert len(issued) > before
 
-        half, n = last_tile
+        half, n = LAST_TILE
         total = keep.tile([P, T_TILE], F32)
         for s in range(PIECES):
             cols = slice(s * PIECE, (s + 1) * PIECE)
-            small = bank_tile((sum_bank(half, n) + 1 + s) % N_TILES)
+            small = bank_tile(sum_bank(half, n) + 1 + s)
             for a in range(PASSES):
                 chunk = half * PASSES + a
                 nc.tensor.matmul_mx(
@@ -416,4 +379,4 @@ def tile_mix_tierx_none_kernel(tc, x, w4_words, w4_scales, out):
             if s % 2 == 1:
                 first = (s - 1) * PIECE
                 t0 = half * T_TILE + first
-                nc.sync.dma_start(out=out[n * P : (n + 1) * P, t0 : t0 + WIDE], in_=total[:, first : first + WIDE])
+                nc.sync.dma_start(out=out[n * P : (n + 1) * P, t0 : t0 + PAIR], in_=total[:, first : first + PAIR])

@@ -30,11 +30,12 @@ BANKS = 8
 SUM_BANKS = 6
 WAVES = (SUM_BANKS, SUM_BANKS - 1)
 RUN = 2
+WIDE_RUN = 4
 FIRST_PACE = 2
 SECOND_PACE = 3
 SECOND_LEAD = 3
-WARM_ZEROS = 4
-WARM_EYE = 2
+VECTOR_EMPTIES = (0, 2)
+WARM_PASSES = 6
 
 
 def load_widths(chunk):
@@ -43,6 +44,10 @@ def load_widths(chunk):
 
 def step_widths(chunk):
     return [PIECE] * PIECES if chunk < PASSES else [PAIR, PAIR]
+
+
+def is_wide(chunk, s):
+    return chunk >= PASSES and (chunk, s // 2) != (CHUNKS - 1, 1)
 
 
 def cut(widths_of):
@@ -97,20 +102,23 @@ def vector_order():
     queue = [("round", 0, 0), ("first", 0, 0), ("first", 0, 1), ("round", 0, 3)]
     for chunk in range(PASSES):
         queue.extend([("sub", chunk, 0), ("first", chunk, 2), ("first", chunk, 3)])
-        for s in range(1, PIECES):
+        for s in range(1, PIECES - 1):
             queue.extend([("sub", chunk, s), ("second", chunk, s - 1)])
+        queue.append(("sub", chunk, PIECES - 1))
+        last_two = [("second", chunk, PIECES - 2), ("second", chunk, PIECES - 1)]
         if chunk + 1 < PASSES:
-            queue.extend([("first", chunk + 1, 0), ("second", chunk, PIECES - 1), ("first", chunk + 1, 1)])
+            queue.extend([("first", chunk + 1, 0)] + last_two + [("first", chunk + 1, 1)])
         else:
-            queue.extend([("second", chunk, PIECES - 1), ("first", chunk + 1, 0)])
+            queue.extend(last_two + [("first", chunk + 1, 0)])
+    queue.extend([("empty", 0, n) for n in VECTOR_EMPTIES])
     for chunk in range(PASSES, CHUNKS):
         queue.extend([("sub", chunk, 0), ("first", chunk, 1)])
         if chunk > PASSES:
             queue.append(("second", chunk - 1, 1))
-        queue.extend([("sub", chunk, 1), ("sub", chunk, 2), ("second", chunk, 0)])
+        queue.extend([("sub", chunk, 1), ("sub", chunk, 2)])
         if chunk + 1 < CHUNKS:
             queue.append(("first", chunk + 1, 0))
-        queue.append(("sub", chunk, 3))
+        queue.extend([("sub", chunk, 3), ("second", chunk, 0)])
     queue.append(("second", CHUNKS - 1, 1))
     queue.extend([("empty", 1, n) for n in range(0, WAVES[1], 2)])
     return queue
@@ -119,11 +127,16 @@ def vector_order():
 def scalar_order():
     queue = [("round", 0, 1), ("round", 0, 2)]
     queue.extend([("round", chunk, k) for chunk in range(1, PASSES + 1) for k in range(len(step_widths(chunk)))])
-    for k in range(2):
-        queue.extend([("empty", 0, 2 * k), ("empty", 0, 2 * k + 1), ("round", CHUNKS - 2, k)])
-    queue.extend([("empty", 0, n) for n in range(4, WAVES[0])])
-    for k in range(2):
-        queue.extend([("empty", 0, WAVES[0] + k), ("round", CHUNKS - 1, k)])
+    roundings = [("round", chunk, k) for chunk in range(PASSES + 1, CHUNKS) for k in range(2)]
+    joins = [("join", chunk, k) for chunk in range(PASSES, CHUNKS) for k in range(2) if is_wide(chunk, 2 * k)]
+    wave = [("empty", 0, n) for n in range(WAVES[0]) if n not in VECTOR_EMPTIES]
+    queue.extend(wave[:2] + roundings[:1] + wave[2:])
+    for i, task in enumerate(joins):
+        queue.append(task)
+        if task == ("join", PASSES, 1):
+            queue.append(("empty", 0, WAVES[0]))
+        queue.extend(roundings[i + 1 : i + 2])
+    queue.append(("empty", 0, WAVES[0] + 1))
     queue.extend([("empty", 1, n) for n in range(N_TILES) if n >= WAVES[1] or n % 2 == 1])
     return queue
 
@@ -149,25 +162,22 @@ def tile_mix_tierx_none_kernel(tc, x, w4_words, w4_scales, out):
         nc.vector.memset(planes[:].bitcast(U32), 0)
         w_scale = [planes[:, a * N : (a + 1) * N] for a in range(PASSES)]
 
-        def warm_up(count, code, scale, width):
-            unread = bank_tile(0)
-            for turn in range(count):
-                nc.tensor.matmul_mx(
-                    out=unread[:, :width],
-                    lhsT=code[:, :P].bitcast(E4M3),
-                    lhsT_scale=scale[:, :P],
-                    rhs=code[:, :width].bitcast(E4M3),
-                    rhs_scale=scale[:, :width],
-                    start=True,
-                    stop=True,
-                )
-
         zero_code = keep.tile([P, PAIR], U32, align_bytes=64)
         zero_scale = keep.tile([P, PAIR], U8, align_bytes=64)
         nc.vector.quantize_mx(
             out=zero_code[:].bitcast(E4M3), scales=zero_scale[:], in_=planes[:, : 2 * PACK * PAIR].bitcast(BF16)
         )
-        warm_up(WARM_ZEROS, zero_code, zero_scale, PAIR)
+        unread = bank_tile(0)
+        for turn in range(WARM_PASSES):
+            nc.tensor.matmul_mx(
+                out=unread[:, :PAIR],
+                lhsT=zero_code[:, :P].bitcast(E4M3),
+                lhsT_scale=zero_scale[:, :P],
+                rhs=zero_code[:].bitcast(E4M3),
+                rhs_scale=zero_scale[:],
+                start=True,
+                stop=True,
+            )
 
         early = WAVES[0] * P
         w_code = kept("w_code", PASSES, lambda a: [P, 2 * early], U8)
@@ -203,8 +213,6 @@ def tile_mix_tierx_none_kernel(tc, x, w4_words, w4_scales, out):
                 nc.vector.quantize_mx(
                     out=eye_code[:, block].bitcast(E4M3), scales=eye_scale[:, block], in_=eye_rows[j - trail][:]
                 )
-
-        warm_up(WARM_EYE, eye_code, eye_scale, T_TILE)
 
         scale_rows = w4_scales.bitcast(I32).rearrange("a (q r) n -> r q a n", r=4)
         for i, (chunk, col, width) in enumerate(loads):
@@ -245,30 +253,52 @@ def tile_mix_tierx_none_kernel(tc, x, w4_words, w4_scales, out):
                 in_=source[i][:].rearrange("p t j -> p (t j)"),
             )
 
+        def back_columns(chunk, s):
+            if is_wide(chunk, s):
+                return s // 2 * PAIR, PAIR, range(s % 2 * 2, s % 2 * 2 + 2)
+            return s * PIECE, PIECE, range(PACK)
+
         def read_back(chunk, s):
+            col, width, rows = back_columns(chunk, s)
             back = bank_tile(back_bank(chunk, s))
-            cols = slice(s * PIECE, (s + 1) * PIECE)
-            for j in range(PACK):
+            for place, j in enumerate(rows):
                 nc.tensor.matmul_mx(
-                    out=back[:, j * PIECE : (j + 1) * PIECE],
+                    out=back[:, place * width : (place + 1) * width],
                     lhsT=eye_code[:, j * P : (j + 1) * P].bitcast(E4M3),
                     lhsT_scale=eye_scale[:, j * P : (j + 1) * P],
-                    rhs=q_code[chunk][:, cols].bitcast(E4M3),
-                    rhs_scale=q_scale[chunk][:, cols],
+                    rhs=q_code[chunk][:, col : col + width].bitcast(E4M3),
+                    rhs_scale=q_scale[chunk][:, col : col + width],
                     start=True,
                     stop=True,
                 )
             return back
 
+        unjoined = {}
+
         def subtract(back, chunk, s):
-            col = s * PIECE
-            i = [i for i in parts_of(steps, chunk) if steps[i][1] <= col][-1]
-            local = slice(col - steps[i][1], col - steps[i][1] + PIECE)
+            col, width, rows = back_columns(chunk, s)
+            if is_wide(chunk, s):
+                k, u = divmod(s, 2)
+                if u == 0:
+                    unjoined[chunk, k] = keep.tile([P, 2, PAIR, 2], BF16, name="unjoined%d_%d" % (chunk, k))
+                target, run = unjoined[chunk, k][:, u, :, :], WIDE_RUN
+            else:
+                i = [i for i in parts_of(steps, chunk) if steps[i][1] <= col][-1]
+                target, run = rest[i][:, col - steps[i][1] : col - steps[i][1] + width, :], RUN
             nc.vector.tensor_tensor(
-                out=rest[i][:, local, :].rearrange("p (c i) j -> p c j i", i=RUN),
-                in0=raw_columns(chunk, col, PIECE).rearrange("p j (c i) -> p c j i", i=RUN),
-                in1=back[:].rearrange("p (j c i) -> p c j i", j=PACK, i=RUN),
+                out=target.rearrange("p (c i) j -> p c j i", i=run),
+                in0=raw_columns(chunk, col, width)[:, rows.start : rows.stop, :].rearrange(
+                    "p j (c i) -> p c j i", i=run
+                ),
+                in1=back[:].rearrange("p (j c i) -> p c j i", j=len(rows), i=run),
                 op=mybir.AluOpType.subtract,
+            )
+
+        def join(chunk, k):
+            source = unjoined[chunk, k][:].rearrange("p u t e -> p (u t e)").bitcast(U32)
+            target = rest[parts_of(steps, chunk)[k]][:].rearrange("p t j -> p (t j)").bitcast(U32)
+            nc.scalar.copy(
+                out=target.rearrange("p (t u) -> p t u", u=2), in_=source.rearrange("p (u t) -> p t u", u=2)
             )
 
         acc = {}
@@ -311,7 +341,9 @@ def tile_mix_tierx_none_kernel(tc, x, w4_words, w4_scales, out):
                 return [("first", chunk, s * PIECE // step_widths(chunk)[0])] + frees.get(back_bank(chunk, s), [])
             if kind == "sub":
                 return [("back",) + args]
-            if kind == "second":
+            if kind == "second" and is_wide(args[0], 2 * args[1]):
+                return [("join",) + args]
+            if kind in ("second", "join"):
                 chunk, col, width = steps[parts_of(steps, args[0])[args[1]]]
                 return [("sub", chunk, s) for s in range(col // PIECE, (col + width) // PIECE)]
             if kind == "pass":
@@ -339,6 +371,8 @@ def tile_mix_tierx_none_kernel(tc, x, w4_words, w4_scales, out):
                 frees[back_bank(*args)] = [("sub",) + args]
             elif kind == "sub":
                 subtract(backs[args], *args)
+            elif kind == "join":
+                join(*args)
             elif kind == "pass":
                 main_pass(*args)
                 frees[sum_bank(*args[:2])] = [("empty",) + args[:2]]

@@ -35,7 +35,8 @@ FIRST_PACE = 2
 SECOND_PACE = 3
 SECOND_LEAD = 3
 VECTOR_EMPTIES = (0, 2)
-WARM_PASSES = 6
+WARM_ZEROS = 4
+WARM_EYE = 2
 
 
 def load_widths(chunk):
@@ -162,22 +163,25 @@ def tile_mix_tierx_none_kernel(tc, x, w4_words, w4_scales, out):
         nc.vector.memset(planes[:].bitcast(U32), 0)
         w_scale = [planes[:, a * N : (a + 1) * N] for a in range(PASSES)]
 
+        def warm_up(count, code, scale, width):
+            unread = bank_tile(0)
+            for turn in range(count):
+                nc.tensor.matmul_mx(
+                    out=unread[:, :width],
+                    lhsT=code[:, :P].bitcast(E4M3),
+                    lhsT_scale=scale[:, :P],
+                    rhs=code[:, :width].bitcast(E4M3),
+                    rhs_scale=scale[:, :width],
+                    start=True,
+                    stop=True,
+                )
+
         zero_code = keep.tile([P, PAIR], U32, align_bytes=64)
         zero_scale = keep.tile([P, PAIR], U8, align_bytes=64)
         nc.vector.quantize_mx(
             out=zero_code[:].bitcast(E4M3), scales=zero_scale[:], in_=planes[:, : 2 * PACK * PAIR].bitcast(BF16)
         )
-        unread = bank_tile(0)
-        for turn in range(WARM_PASSES):
-            nc.tensor.matmul_mx(
-                out=unread[:, :PAIR],
-                lhsT=zero_code[:, :P].bitcast(E4M3),
-                lhsT_scale=zero_scale[:, :P],
-                rhs=zero_code[:].bitcast(E4M3),
-                rhs_scale=zero_scale[:],
-                start=True,
-                stop=True,
-            )
+        warm_up(WARM_ZEROS, zero_code, zero_scale, PAIR)
 
         early = WAVES[0] * P
         w_code = kept("w_code", PASSES, lambda a: [P, 2 * early], U8)
@@ -213,6 +217,8 @@ def tile_mix_tierx_none_kernel(tc, x, w4_words, w4_scales, out):
                 nc.vector.quantize_mx(
                     out=eye_code[:, block].bitcast(E4M3), scales=eye_scale[:, block], in_=eye_rows[j - trail][:]
                 )
+
+        warm_up(WARM_EYE, eye_code, eye_scale, T_TILE)
 
         scale_rows = w4_scales.bitcast(I32).rearrange("a (q r) n -> r q a n", r=4)
         for i, (chunk, col, width) in enumerate(loads):

@@ -35,16 +35,36 @@ FIRST_PACE = 2
 SECOND_PACE = 3
 SECOND_LEAD = 3
 VECTOR_EMPTIES = (0, 2)
+HEAD_ORDER = ((0, 0), (0, 1), (1, 0), (1, 1))
+HEAD_BACKS = (0, 0, 3, 4)
+NEXT_BACKS = (15, 19, 23, 25)
+THIRD_BACKS = (30, 32, 34, 36)
+V_HEAD = [("round", 0, 0), ("first", 0, 0), ("first", 0, 1), ("round", 0, 3), ("sub", 0, 0), ("first", 0, 2), ("first", 0, 3), ("sub", 0, 1), ("second", 0, 0), ("sub", 0, 2), ("second", 0, 1), ("sub", 0, 3), ("first", 1, 0), ("second", 0, 2), ("second", 0, 3), ("first", 1, 1)]
+V_FROM = 1
+W_FIRST = 0
+SCALES_FIRST = False
+FINE = {"round": 3, "first": 3, "second": 3}
+HALVED = 3
 WARM_ZEROS = 4
 WARM_EYE = 2
 
 
 def load_widths(chunk):
-    return [PAIR, PAIR] if chunk < PASSES else [T_TILE]
+    return [PAIR, PAIR] if chunk < HALVED else [T_TILE]
 
 
-def step_widths(chunk):
-    return [PIECE] * PIECES if chunk < PASSES else [PAIR, PAIR]
+def step_widths(kind, chunk):
+    return [PIECE] * PIECES if chunk < FINE[kind] else [PAIR, PAIR]
+
+
+def covering(kind, chunk, col, width):
+    step = step_widths(kind, chunk)[0]
+    return [(kind, chunk, k) for k in range(col // step, (col + width - 1) // step + 1)]
+
+
+def columns(kind, chunk, k):
+    step = step_widths(kind, chunk)[0]
+    return k * step, step
 
 
 def is_wide(chunk, s):
@@ -66,10 +86,14 @@ def parts_of(parts, chunk):
 
 
 def pass_order():
-    order = []
+    order = [(0, n, 0, tier, pair) for tier, pair in HEAD_ORDER for n in range(WAVES[0])]
     for half, wave in enumerate(WAVES):
-        order.extend([(half, n, a, tier) for a in range(PASSES) for tier in range(TIERS) for n in range(wave)])
-        order.extend([(half, n, a, tier) for n in range(wave, N_TILES) for a in range(PASSES) for tier in range(TIERS)])
+        order.extend(
+            [(half, n, a, tier, None) for a in range(PASSES) for tier in range(TIERS) for n in range(wave) if half or a]
+        )
+        order.extend(
+            [(half, n, a, tier, None) for n in range(wave, N_TILES) for a in range(PASSES) for tier in range(TIERS)]
+        )
     return [step for step in order if step[:2] != LAST_TILE or step[3] == 1]
 
 
@@ -83,12 +107,16 @@ def back_bank(chunk, s):
 
 def tensor_order():
     order = pass_order()
-    second = order.index((0, WAVES[0], 0, 0)) - SECOND_LEAD
+    second = order.index((0, WAVES[0], 0, 0, None)) - SECOND_LEAD
     ahead_of = {}
     for chunk in range(CHUNKS):
         for s in range(PIECES):
-            if chunk < PASSES:
-                step = max(0, order.index((0, 0, chunk, 0)) - FIRST_PACE * (PIECES - 1 - s))
+            if chunk == 0:
+                step = HEAD_BACKS[s]
+            elif chunk == 1:
+                step = NEXT_BACKS[s]
+            elif chunk < PASSES:
+                step = THIRD_BACKS[s]
             else:
                 step = second + SECOND_PACE * (PIECES * (chunk - PASSES) + s)
             ahead_of.setdefault(step, []).append(("back", chunk, s))
@@ -100,8 +128,8 @@ def tensor_order():
 
 
 def vector_order():
-    queue = [("round", 0, 0), ("first", 0, 0), ("first", 0, 1), ("round", 0, 3)]
-    for chunk in range(PASSES):
+    queue = list(V_HEAD)
+    for chunk in range(V_FROM, PASSES):
         queue.extend([("sub", chunk, 0), ("first", chunk, 2), ("first", chunk, 3)])
         for s in range(1, PIECES - 1):
             queue.extend([("sub", chunk, s), ("second", chunk, s - 1)])
@@ -126,8 +154,8 @@ def vector_order():
 
 
 def scalar_order():
-    queue = [("round", 0, 1), ("round", 0, 2)]
-    queue.extend([("round", chunk, k) for chunk in range(1, PASSES + 1) for k in range(len(step_widths(chunk)))])
+    queue = [("round", chunk, k) for chunk in range(PASSES + 1) for k in range(len(step_widths("round", chunk)))]
+    queue = [task for task in queue if task not in V_HEAD]
     roundings = [("round", chunk, k) for chunk in range(PASSES + 1, CHUNKS) for k in range(2)]
     joins = [("join", chunk, k) for chunk in range(PASSES, CHUNKS) for k in range(2) if is_wide(chunk, 2 * k)]
     wave = [("empty", 0, n) for n in range(WAVES[0]) if n not in VECTOR_EMPTIES]
@@ -157,7 +185,6 @@ def tile_mix_tierx_none_kernel(tc, x, w4_words, w4_scales, out):
             return [keep.tile(shape_of(i), dtype, align_bytes=64, name="%s%d" % (name, i)) for i in range(count)]
 
         loads = cut(load_widths)
-        steps = cut(step_widths)
 
         planes = keep.tile([P, PASSES * N], U8, align_bytes=64)
         nc.vector.memset(planes[:].bitcast(U32), 0)
@@ -187,8 +214,8 @@ def tile_mix_tierx_none_kernel(tc, x, w4_words, w4_scales, out):
         w_code = kept("w_code", PASSES, lambda a: [P, 2 * early], U8)
         w_late = keep.tile([P, PASSES, 2 * (N - early)], U8, align_bytes=64)
         raw = kept("raw", len(loads), lambda i: [P, PACK, loads[i][2]], F32)
-        rounded = kept("rounded", len(steps), lambda i: [P, steps[i][2], PACK], BF16)
-        rest = kept("rest", len(steps), lambda i: [P, steps[i][2], PACK], BF16)
+        rounded = kept("rounded", 2 * CHUNKS, lambda i: [P, PAIR, PACK], BF16)
+        rest = kept("rest", 2 * CHUNKS, lambda i: [P, PAIR, PACK], BF16)
         q_code = kept("q_code", CHUNKS, lambda c: [P, T_TILE], U32)
         q_scale = kept("q_scale", CHUNKS, lambda c: [P, T_TILE], U8)
         r_code = kept("r_code", CHUNKS, lambda c: [P, T_TILE], U32)
@@ -226,13 +253,22 @@ def tile_mix_tierx_none_kernel(tc, x, w4_words, w4_scales, out):
             t0 = half * T_TILE + col
             rows = x[a * P * PACK : (a + 1) * P * PACK, t0 : t0 + width]
             nc.sync.dma_start(out=raw[i][:], in_=rows.rearrange("(p j) t -> p j t", j=PACK))
-            if col + width == T_TILE and half == 0:
+            if half == 0 and (col + width == PAIR if chunk == 0 and SCALES_FIRST else col + width == T_TILE):
                 for r in range(4):
-                    nc.sync.dma_start(out=w_scale[a].bitcast(I32)[r:P:32, :], in_=scale_rows[r, :, a, :])
-                nc.sync.dma_start(out=w_code[a][:].bitcast(I32), in_=w4_words[a, :, : 2 * early].bitcast(I32))
+                    nc.sync.dma_start(
+                        out=w_scale[a].bitcast(I32)[r:P:32, : early // 4], in_=scale_rows[r, :, a, : early // 4]
+                    )
+            if chunk == 0 and W_FIRST and col + width == PAIR:
+                nc.sync.dma_start(out=w_code[a][:, : 2 * P * W_FIRST].bitcast(I32), in_=w4_words[a, :, : 2 * P * W_FIRST].bitcast(I32))
+            if col + width == T_TILE and half == 0 and (chunk or W_FIRST < WAVES[0]):
+                lo = 2 * P * W_FIRST if chunk == 0 else 0
+                nc.sync.dma_start(out=w_code[a][:, lo:].bitcast(I32), in_=w4_words[a, :, lo : 2 * early].bitcast(I32))
             if col + width == T_TILE and chunk == PASSES:
                 late = w4_words[:, :, 2 * early :].bitcast(I32).rearrange("a p n -> p a n")
                 nc.sync.dma_start(out=w_late[:].bitcast(I32), in_=late)
+                all_planes = planes[:].bitcast(I32).rearrange("p (a n) -> p a n", a=PASSES)
+                for r in range(4):
+                    nc.sync.dma_start(out=all_planes[r:P:32, :, early // 4 :], in_=scale_rows[r, :, :, early // 4 :])
 
         def weight_words(a, n):
             if n * P < early:
@@ -243,20 +279,23 @@ def tile_mix_tierx_none_kernel(tc, x, w4_words, w4_scales, out):
             i = [i for i in parts_of(loads, chunk) if loads[i][1] <= col][-1]
             return raw[i][:, :, col - loads[i][1] : col - loads[i][1] + width]
 
+        def window(tiles, chunk, col, width):
+            return tiles[2 * chunk + col // PAIR][:, col % PAIR : col % PAIR + width, :]
+
         def round_part(chunk, k, copy):
-            i = parts_of(steps, chunk)[k]
+            col, width = columns("round", chunk, k)
             copy(
-                out=rounded[i][:].rearrange("p (c i) j -> p c j i", i=RUN),
-                in_=raw_columns(*steps[i]).rearrange("p j (c i) -> p c j i", i=RUN),
+                out=window(rounded, chunk, col, width).rearrange("p (c i) j -> p c j i", i=RUN),
+                in_=raw_columns(chunk, col, width).rearrange("p j (c i) -> p c j i", i=RUN),
             )
 
-        def quantise(chunk, k, source, code, scale, dtype):
-            i = parts_of(steps, chunk)[k]
-            cols = slice(steps[i][1], steps[i][1] + steps[i][2])
+        def quantise(kind, chunk, k, source, code, scale, dtype):
+            col, width = columns(kind, chunk, k)
+            cols = slice(col, col + width)
             nc.vector.quantize_mx(
                 out=code[chunk][:, cols].bitcast(dtype),
                 scales=scale[chunk][:, cols],
-                in_=source[i][:].rearrange("p t j -> p (t j)"),
+                in_=window(source, chunk, col, width).rearrange("p t j -> p (t j)"),
             )
 
         def back_columns(chunk, s):
@@ -289,8 +328,7 @@ def tile_mix_tierx_none_kernel(tc, x, w4_words, w4_scales, out):
                     unjoined[chunk, k] = keep.tile([P, 2, PAIR, 2], BF16, name="unjoined%d_%d" % (chunk, k))
                 target, run = unjoined[chunk, k][:, u, :, :], WIDE_RUN
             else:
-                i = [i for i in parts_of(steps, chunk) if steps[i][1] <= col][-1]
-                target, run = rest[i][:, col - steps[i][1] : col - steps[i][1] + width, :], RUN
+                target, run = window(rest, chunk, col, width), RUN
             nc.vector.tensor_tensor(
                 out=target.rearrange("p (c i) j -> p c j i", i=run),
                 in0=raw_columns(chunk, col, width)[:, rows.start : rows.stop, :].rearrange(
@@ -302,7 +340,7 @@ def tile_mix_tierx_none_kernel(tc, x, w4_words, w4_scales, out):
 
         def join(chunk, k):
             source = unjoined[chunk, k][:].rearrange("p u t e -> p (u t e)").bitcast(U32)
-            target = rest[parts_of(steps, chunk)[k]][:].rearrange("p t j -> p (t j)").bitcast(U32)
+            target = rest[2 * chunk + k][:].rearrange("p t j -> p (t j)").bitcast(U32)
             nc.scalar.copy(
                 out=target.rearrange("p (t u) -> p t u", u=2), in_=source.rearrange("p (u t) -> p t u", u=2)
             )
@@ -310,17 +348,18 @@ def tile_mix_tierx_none_kernel(tc, x, w4_words, w4_scales, out):
         acc = {}
         second_tier = keep.tile([P, T_TILE], F32)
 
-        def main_pass(half, n, a, tier):
+        def main_pass(half, n, a, tier, pair):
             chunk = half * PASSES + a
-            opens = a == 0 and (tier == 0 or (half, n) == LAST_TILE)
+            opens = (half, n) not in acc
+            cols = slice(0, T_TILE) if pair is None else slice(pair * PAIR, (pair + 1) * PAIR)
             if opens:
                 acc[half, n] = bank_tile(sum_bank(half, n))
             nc.tensor.matmul_mx(
-                out=acc[half, n][:],
+                out=acc[half, n][:, cols],
                 lhsT=weight_words(a, n).bitcast(E2M1),
                 lhsT_scale=w_scale[a][:, n * P : (n + 1) * P],
-                rhs=q_code[chunk][:].bitcast(E4M3) if tier == 0 else r_code[chunk][:].bitcast(E5M2),
-                rhs_scale=q_scale[chunk][:] if tier == 0 else r_scale[chunk][:],
+                rhs=q_code[chunk][:, cols].bitcast(E4M3) if tier == 0 else r_code[chunk][:, cols].bitcast(E5M2),
+                rhs_scale=q_scale[chunk][:, cols] if tier == 0 else r_scale[chunk][:, cols],
                 start=opens,
                 stop=a == PASSES - 1 and tier == 1,
             )
@@ -341,24 +380,27 @@ def tile_mix_tierx_none_kernel(tc, x, w4_words, w4_scales, out):
         def needs(task):
             kind, args = task[0], task[1:]
             if kind == "first":
-                return [("round",) + args]
+                return covering("round", args[0], *columns(*task))
             if kind == "back":
                 chunk, s = args
-                return [("first", chunk, s * PIECE // step_widths(chunk)[0])] + frees.get(back_bank(chunk, s), [])
+                return covering("first", chunk, *back_columns(chunk, s)[:2]) + frees.get(back_bank(chunk, s), [])
             if kind == "sub":
                 return [("back",) + args]
-            if kind == "second" and is_wide(args[0], 2 * args[1]):
-                return [("join",) + args]
-            if kind in ("second", "join"):
-                chunk, col, width = steps[parts_of(steps, args[0])[args[1]]]
-                return [("sub", chunk, s) for s in range(col // PIECE, (col + width) // PIECE)]
+            if kind == "second":
+                col, width = columns(*task)
+                if is_wide(args[0], col // PIECE):
+                    return [("join", args[0], col // PAIR)]
+                return [("sub", args[0], s) for s in range(col // PIECE, (col + width) // PIECE)]
+            if kind == "join":
+                return [("sub", args[0], 2 * args[1]), ("sub", args[0], 2 * args[1] + 1)]
             if kind == "pass":
-                half, n, a, tier = args
+                half, n, a, tier, pair = args
                 chunk = half * PASSES + a
-                operand = [("second" if tier else "first", chunk, k) for k in range(len(step_widths(chunk)))]
+                col, width = (0, T_TILE) if pair is None else (pair * PAIR, PAIR)
+                operand = covering("second" if tier else "first", chunk, col, width)
                 return operand + ([] if (half, n) in acc else frees.get(sum_bank(half, n), []))
             if kind == "empty":
-                return [("pass",) + args + (PASSES - 1, 1)]
+                return [("pass",) + args + (PASSES - 1, 1, None)]
             return []
 
         backs = {}
@@ -369,9 +411,9 @@ def tile_mix_tierx_none_kernel(tc, x, w4_words, w4_scales, out):
             if kind == "round":
                 round_part(*args, copy)
             elif kind == "first":
-                quantise(*args, rounded, q_code, q_scale, E4M3)
+                quantise(*task, rounded, q_code, q_scale, E4M3)
             elif kind == "second":
-                quantise(*args, rest, r_code, r_scale, E5M2)
+                quantise(*task, rest, r_code, r_scale, E5M2)
             elif kind == "back":
                 backs[args] = read_back(*args)
                 frees[back_bank(*args)] = [("sub",) + args]

@@ -17,448 +17,319 @@ E2M1 = mybir.dt.float4_e2m1fn_x4
 P = 128
 PACK = 4
 PASSES = K // (P * PACK)
-T_TILE = 512
 N_TILES = N // P
-HALVES = T // T_TILE
-CHUNKS = HALVES * PASSES
-TIERS = 2
-LAST_TILE = (HALVES - 1, N_TILES - 1)
-PIECE = T_TILE // PACK
-PIECES = T_TILE // PIECE
-PAIR = 2 * PIECE
-BANKS = 8
+BANK = 512
+PART = BANK // 2
+PIECE = PART // 2
+QUARTERS = 2
+EARLY_PARTS = QUARTERS * PASSES
+PARTS = 2 * EARLY_PARTS
+LOW = N_TILES // 2
 SUM_BANKS = 6
-WAVES = (SUM_BANKS, SUM_BANKS - 1)
-RUN = 2
-WIDE_RUN = 4
-FIRST_PACE = 2
-SECOND_PACE = 3
-SECOND_LEAD = 3
-VECTOR_EMPTIES = (0, 2)
-HEAD_ORDER = ((0, 0), (0, 1), (1, 0), (1, 1))
-HEAD_BACKS = (0, 0, 3, 4)
-NEXT_BACKS = (15, 19, 23, 25)
-THIRD_BACKS = (30, 32, 34, 36)
-V_HEAD = [("round", 0, 0), ("first", 0, 0), ("first", 0, 1), ("round", 0, 3), ("sub", 0, 0), ("first", 0, 2), ("first", 0, 3), ("sub", 0, 1), ("second", 0, 0), ("sub", 0, 2), ("second", 0, 1), ("sub", 0, 3), ("first", 1, 0), ("second", 0, 2), ("second", 0, 3), ("first", 1, 1)]
-V_FROM = 1
-W_FIRST = 0
-SCALES_FIRST = False
-FINE = {"round": 3, "first": 3, "second": 3}
-HALVED = 3
-WARM_ZEROS = 4
-WARM_EYE = 2
+ALIGN = 256
+RUN = 4
+ONE_LOW, ONE_HIGH = 0x3F80, 0x3F800000
+WARM_UP = 5
+WAVE = 6
+PACE = 6
+SHARED = 3
+NARROW = (0, 1, 2, PARTS - 1)
 
 
-def load_widths(chunk):
-    return [PAIR, PAIR] if chunk < HALVED else [T_TILE]
-
-
-def step_widths(kind, chunk):
-    return [PIECE] * PIECES if chunk < FINE[kind] else [PAIR, PAIR]
-
-
-def covering(kind, chunk, col, width):
-    step = step_widths(kind, chunk)[0]
-    return [(kind, chunk, k) for k in range(col // step, (col + width - 1) // step + 1)]
-
-
-def columns(kind, chunk, k):
-    step = step_widths(kind, chunk)[0]
-    return k * step, step
-
-
-def is_wide(chunk, s):
-    return chunk >= PASSES and (chunk, s // 2) != (CHUNKS - 1, 1)
-
-
-def cut(widths_of):
-    parts = []
-    for chunk in range(CHUNKS):
-        col = 0
-        for width in widths_of(chunk):
-            parts.append((chunk, col, width))
-            col = col + width
-    return parts
-
-
-def parts_of(parts, chunk):
-    return [i for i, part in enumerate(parts) if part[0] == chunk]
+def part_place(part):
+    if part < EARLY_PARTS:
+        quarter, a = divmod(part, PASSES)
+        return a, quarter * PART
+    a, side = divmod(part - EARLY_PARTS, 2)
+    return a, BANK + side * PART
 
 
 def pass_order():
-    order = [(0, n, 0, tier, pair) for tier, pair in HEAD_ORDER for n in range(WAVES[0])]
-    for half, wave in enumerate(WAVES):
-        order.extend(
-            [(half, n, a, tier, None) for a in range(PASSES) for tier in range(TIERS) for n in range(wave) if half or a]
-        )
-        order.extend(
-            [(half, n, a, tier, None) for n in range(wave, N_TILES) for a in range(PASSES) for tier in range(TIERS)]
-        )
-    return [step for step in order if step[:2] != LAST_TILE or step[3] == 1]
+    low, high = range(LOW), range(LOW, N_TILES)
 
+    def sweep(part, tier, tiles):
+        span, a = divmod(part, PASSES)
+        return [(span, n, a, tier) for n in tiles]
 
-def sum_bank(half, n):
-    return (half * N_TILES + n) % SUM_BANKS
-
-
-def back_bank(chunk, s):
-    return BANKS - PIECES + s if chunk == 0 else SUM_BANKS + s % 2
+    order = sweep(0, 0, low) + sweep(0, 0, high)
+    for part in range(1, PASSES):
+        order.extend(sweep(part, 0, low) + sweep(part - 1, 1, range(N_TILES)) + sweep(part, 0, high))
+    part = PASSES
+    order.extend(sweep(part, 0, low) + sweep(part - 1, 1, range(N_TILES)) + sweep(part + 1, 0, low))
+    order.extend(sweep(part, 0, high) + sweep(part + 1, 0, high) + sweep(part, 1, range(N_TILES)))
+    order.extend(sweep(part + 2, 0, range(N_TILES)))
+    order.extend(sweep(part + 1, 1, range(N_TILES)) + [(2, 0, 0, 0)] + sweep(part + 2, 1, range(N_TILES)))
+    stages = ((0, 0), (1, 0), (0, 1), (2, 0))
+    for i, (a, tier) in enumerate(stages):
+        order.extend([(2, n, a, tier) for n in range(SUM_BANKS - 1) if (2, n, a, tier) not in order])
+        if i:
+            order.append((2, SUM_BANKS - 1) + stages[i - 1])
+    for n in range(N_TILES - 1):
+        order.extend([(2, n, a, tier) for tier in range(2) for a in range(PASSES) if (2, n, a, tier) not in order])
+    for span in (3, 4):
+        order.extend([(span, N_TILES - 1, a, tier) for a in range(PASSES) for tier in range(2)])
+    return order
 
 
 def tensor_order():
     order = pass_order()
-    second = order.index((0, WAVES[0], 0, 0, None)) - SECOND_LEAD
-    ahead_of = {}
-    for chunk in range(CHUNKS):
-        for s in range(PIECES):
-            if chunk == 0:
-                step = HEAD_BACKS[s]
-            elif chunk == 1:
-                step = NEXT_BACKS[s]
-            elif chunk < PASSES:
-                step = THIRD_BACKS[s]
+    queue, done, back, due = [], 0, 0, 0
+    for work in order:
+        while back < 2 * PARTS and due <= done:
+            queue.append(("back",) + divmod(back, 2))
+            back = back + 1
+            part, s = divmod(back, 2)
+            if part <= PASSES and s == 0:
+                due = order.index((part // PASSES, 0, part % PASSES, 0))
+            elif part <= PASSES:
+                due = done + (GAP if part else 0)
             else:
-                step = second + SECOND_PACE * (PIECES * (chunk - PASSES) + s)
-            ahead_of.setdefault(step, []).append(("back", chunk, s))
-    queue = []
-    for step, work in enumerate(order):
-        queue.extend(ahead_of.get(step, []))
+                due = done + (PACE if back <= 2 * PARTS - 5 else LATE_PACE)
         queue.append(("pass",) + work)
+        done = done + (2 if work[0] == 2 else 1)
     return queue
 
 
-def vector_order():
-    queue = list(V_HEAD)
-    for chunk in range(V_FROM, PASSES):
-        queue.extend([("sub", chunk, 0), ("first", chunk, 2), ("first", chunk, 3)])
-        for s in range(1, PIECES - 1):
-            queue.extend([("sub", chunk, s), ("second", chunk, s - 1)])
-        queue.append(("sub", chunk, PIECES - 1))
-        last_two = [("second", chunk, PIECES - 2), ("second", chunk, PIECES - 1)]
-        if chunk + 1 < PASSES:
-            queue.extend([("first", chunk + 1, 0)] + last_two + [("first", chunk + 1, 1)])
-        else:
-            queue.extend(last_two + [("first", chunk + 1, 0)])
-    queue.extend([("empty", 0, n) for n in VECTOR_EMPTIES])
-    for chunk in range(PASSES, CHUNKS):
-        queue.extend([("sub", chunk, 0), ("first", chunk, 1)])
-        if chunk > PASSES:
-            queue.append(("second", chunk - 1, 1))
-        queue.extend([("sub", chunk, 1), ("sub", chunk, 2)])
-        if chunk + 1 < CHUNKS:
-            queue.append(("first", chunk + 1, 0))
-        queue.extend([("sub", chunk, 3), ("second", chunk, 0)])
-    queue.append(("second", CHUNKS - 1, 1))
-    queue.extend([("empty", 1, n) for n in range(0, WAVES[1], 2)])
-    return queue
-
-
-def scalar_order():
-    queue = [("round", chunk, k) for chunk in range(PASSES + 1) for k in range(len(step_widths("round", chunk)))]
-    queue = [task for task in queue if task not in V_HEAD]
-    roundings = [("round", chunk, k) for chunk in range(PASSES + 1, CHUNKS) for k in range(2)]
-    joins = [("join", chunk, k) for chunk in range(PASSES, CHUNKS) for k in range(2) if is_wide(chunk, 2 * k)]
-    wave = [("empty", 0, n) for n in range(WAVES[0]) if n not in VECTOR_EMPTIES]
-    queue.extend(wave[:2] + roundings[:1] + wave[2:])
-    for i, task in enumerate(joins):
-        queue.append(task)
-        if task == ("join", PASSES, 1):
-            queue.append(("empty", 0, WAVES[0]))
-        queue.extend(roundings[i + 1 : i + 2])
-    queue.append(("empty", 0, WAVES[0] + 1))
-    queue.extend([("empty", 1, n) for n in range(N_TILES) if n >= WAVES[1] or n % 2 == 1])
-    return queue
+GAP = 2
+LATE_PACE = 4
+FIRST_BEHIND = 4
+ROUND_BEHIND = 2
 
 
 def tile_mix_tierx_none_kernel(tc, x, w4_words, w4_scales, out):
     nc = tc.nc
     with ExitStack() as ctx:
         keep = ctx.enter_context(tc.tile_pool(name="keep", bufs=1))
-        stage = ctx.enter_context(tc.tile_pool(name="stage", bufs=HALVES * N_TILES - 1))
         psum = ctx.enter_context(tc.psum_pool(name="psum", bufs=1))
         ctx.enter_context(tc.manual_schedule())
 
         def bank_tile(bank):
-            return psum.tile([P, T_TILE], F32, name="bank%d" % bank)
+            return psum.tile([P, BANK], F32, name="bank%d" % bank)
 
-        def kept(name, count, shape_of, dtype):
-            return [keep.tile(shape_of(i), dtype, align_bytes=64, name="%s%d" % (name, i)) for i in range(count)]
+        def kept(name, count, shape, dtype):
+            return [keep.tile(shape, dtype, align_bytes=ALIGN, name="%s%d" % (name, i)) for i in range(count)]
 
-        loads = cut(load_widths)
+        w_scale = kept("w_scale", PASSES, [P, N], U8)
+        for a in (PASSES - 1, 0, 1):
+            nc.vector.memset(w_scale[a][:].bitcast(U32), 0)
 
-        planes = keep.tile([P, PASSES * N], U8, align_bytes=64)
-        nc.vector.memset(planes[:].bitcast(U32), 0)
-        w_scale = [planes[:, a * N : (a + 1) * N] for a in range(PASSES)]
+        unread = bank_tile(0)
+        zeros = w_scale[PASSES - 1]
+        for turn in range(WARM_UP):
+            nc.tensor.matmul_mx(
+                out=unread[:],
+                lhsT=zeros[:, : PACK * P].bitcast(E4M3),
+                lhsT_scale=zeros[:, :P],
+                rhs=zeros[:].bitcast(E2M1),
+                rhs_scale=zeros[:, :BANK],
+                start=True,
+                stop=True,
+            )
 
-        def warm_up(count, code, scale, width):
-            unread = bank_tile(0)
-            for turn in range(count):
-                nc.tensor.matmul_mx(
-                    out=unread[:, :width],
-                    lhsT=code[:, :P].bitcast(E4M3),
-                    lhsT_scale=scale[:, :P],
-                    rhs=code[:, :width].bitcast(E4M3),
-                    rhs_scale=scale[:, :width],
-                    start=True,
-                    stop=True,
-                )
-
-        zero_code = keep.tile([P, PAIR], U32, align_bytes=64)
-        zero_scale = keep.tile([P, PAIR], U8, align_bytes=64)
-        nc.vector.quantize_mx(
-            out=zero_code[:].bitcast(E4M3), scales=zero_scale[:], in_=planes[:, : 2 * PACK * PAIR].bitcast(BF16)
-        )
-        warm_up(WARM_ZEROS, zero_code, zero_scale, PAIR)
-
-        early = WAVES[0] * P
-        w_code = kept("w_code", PASSES, lambda a: [P, 2 * early], U8)
-        w_late = keep.tile([P, PASSES, 2 * (N - early)], U8, align_bytes=64)
-        raw = kept("raw", len(loads), lambda i: [P, PACK, loads[i][2]], F32)
-        rounded = kept("rounded", 2 * CHUNKS, lambda i: [P, PAIR, PACK], BF16)
-        rest = kept("rest", 2 * CHUNKS, lambda i: [P, PAIR, PACK], BF16)
-        q_code = kept("q_code", CHUNKS, lambda c: [P, T_TILE], U32)
-        q_scale = kept("q_scale", CHUNKS, lambda c: [P, T_TILE], U8)
-        r_code = kept("r_code", CHUNKS, lambda c: [P, T_TILE], U32)
-        r_scale = kept("r_scale", CHUNKS, lambda c: [P, T_TILE], U8)
-
-        ramp = keep.tile([P, 2 * P + 2], F32)
+        ramp = keep.tile([P, 2 * P], F32, align_bytes=ALIGN)
         nc.gpsimd.iota(
-            ramp[:], pattern=[[-1, 2 * P + 2]], base=2, channel_multiplier=2, allow_small_or_imprecise_dtypes=True
+            ramp[:], pattern=[[1, 2 * P]], base=0, channel_multiplier=-2, allow_small_or_imprecise_dtypes=True
         )
-        marks = ramp[:].bitcast(BF16)
-        eye_rows = kept("eye_rows", PACK, lambda j: [P, PACK * P], BF16)
-        eye_code = keep.tile([P, PACK * P], U32, align_bytes=64)
-        eye_scale = keep.tile([P, PACK * P], U8, align_bytes=64)
-        trail = 2
-        for j in range(PACK + trail):
-            if j < PACK:
+        eye_rows = kept("eye_rows", 2, [P, 2, 2 * P], I32)
+        eye_code = keep.tile([P, PACK * P], U32, align_bytes=ALIGN)
+        eye_scale = keep.tile([P, PACK * P], U8, align_bytes=ALIGN)
+        for u in range(2):
+            for e, one in enumerate((ONE_LOW, ONE_HIGH)):
                 nc.vector.tensor_scalar(
-                    out=eye_rows[j][:],
-                    in0=marks[:, PACK - 1 - j : PACK - 1 - j + PACK * P],
-                    scalar1=1.0,
-                    scalar2=None,
+                    out=eye_rows[u][:, e, :],
+                    in0=ramp[:],
+                    scalar1=float(u),
+                    scalar2=float(one),
                     op0=mybir.AluOpType.is_equal,
+                    op1=mybir.AluOpType.mult,
                 )
-            if j >= trail:
-                block = slice((j - trail) * P, (j - trail + 1) * P)
-                nc.vector.quantize_mx(
-                    out=eye_code[:, block].bitcast(E4M3), scales=eye_scale[:, block], in_=eye_rows[j - trail][:]
-                )
-
-        warm_up(WARM_EYE, eye_code, eye_scale, T_TILE)
-
-        scale_rows = w4_scales.bitcast(I32).rearrange("a (q r) n -> r q a n", r=4)
-        for i, (chunk, col, width) in enumerate(loads):
-            half, a = divmod(chunk, PASSES)
-            t0 = half * T_TILE + col
-            rows = x[a * P * PACK : (a + 1) * P * PACK, t0 : t0 + width]
-            nc.sync.dma_start(out=raw[i][:], in_=rows.rearrange("(p j) t -> p j t", j=PACK))
-            if half == 0 and (col + width == PAIR if chunk == 0 and SCALES_FIRST else col + width == T_TILE):
-                for r in range(4):
-                    nc.sync.dma_start(
-                        out=w_scale[a].bitcast(I32)[r:P:32, : early // 4], in_=scale_rows[r, :, a, : early // 4]
-                    )
-            if chunk == 0 and W_FIRST and col + width == PAIR:
-                nc.sync.dma_start(out=w_code[a][:, : 2 * P * W_FIRST].bitcast(I32), in_=w4_words[a, :, : 2 * P * W_FIRST].bitcast(I32))
-            if col + width == T_TILE and half == 0 and (chunk or W_FIRST < WAVES[0]):
-                lo = 2 * P * W_FIRST if chunk == 0 else 0
-                nc.sync.dma_start(out=w_code[a][:, lo:].bitcast(I32), in_=w4_words[a, :, lo : 2 * early].bitcast(I32))
-            if col + width == T_TILE and chunk == PASSES:
-                late = w4_words[:, :, 2 * early :].bitcast(I32).rearrange("a p n -> p a n")
-                nc.sync.dma_start(out=w_late[:].bitcast(I32), in_=late)
-                all_planes = planes[:].bitcast(I32).rearrange("p (a n) -> p a n", a=PASSES)
-                for r in range(4):
-                    nc.sync.dma_start(out=all_planes[r:P:32, :, early // 4 :], in_=scale_rows[r, :, :, early // 4 :])
-
-        def weight_words(a, n):
-            if n * P < early:
-                return w_code[a][:, 2 * n * P : 2 * (n + 1) * P]
-            return w_late[:, a, 2 * (n * P - early) : 2 * ((n + 1) * P - early)]
-
-        def raw_columns(chunk, col, width):
-            i = [i for i in parts_of(loads, chunk) if loads[i][1] <= col][-1]
-            return raw[i][:, :, col - loads[i][1] : col - loads[i][1] + width]
-
-        def window(tiles, chunk, col, width):
-            return tiles[2 * chunk + col // PAIR][:, col % PAIR : col % PAIR + width, :]
-
-        def round_part(chunk, k, copy):
-            col, width = columns("round", chunk, k)
-            copy(
-                out=window(rounded, chunk, col, width).rearrange("p (c i) j -> p c j i", i=RUN),
-                in_=raw_columns(chunk, col, width).rearrange("p j (c i) -> p c j i", i=RUN),
-            )
-
-        def quantise(kind, chunk, k, source, code, scale, dtype):
-            col, width = columns(kind, chunk, k)
-            cols = slice(col, col + width)
+        for u in range(2):
+            block = slice(u * 2 * P, (u + 1) * 2 * P)
             nc.vector.quantize_mx(
-                out=code[chunk][:, cols].bitcast(dtype),
-                scales=scale[chunk][:, cols],
-                in_=window(source, chunk, col, width).rearrange("p t j -> p (t j)"),
+                out=eye_code[:, block].bitcast(E4M3),
+                scales=eye_scale[:, block],
+                in_=eye_rows[u][:].rearrange("p e w -> p (e w)").bitcast(BF16),
             )
 
-        def back_columns(chunk, s):
-            if is_wide(chunk, s):
-                return s // 2 * PAIR, PAIR, range(s % 2 * 2, s % 2 * 2 + 2)
-            return s * PIECE, PIECE, range(PACK)
+        w_code = kept("w_code", 2 * PASSES, [P, 2 * LOW * P], U8)
+        raw_early = kept("raw_early", EARLY_PARTS, [P, PACK, PART], F32)
+        raw_late = kept("raw_late", PASSES, [P, PACK, BANK], F32)
+        rounded = kept("rounded", PARTS, [P, PART, PACK], BF16)
+        rest = kept("rest", PARTS, [P, PART, PACK], BF16)
+        unjoined = {part: keep.tile([P, 2, PART, 2], BF16, align_bytes=ALIGN, name="unjoined%d" % part) for part in range(PARTS) if part not in NARROW}
+        q_code = kept("q_code", PASSES, [P, T], U32)
+        q_scale = kept("q_scale", PASSES, [P, T], U8)
+        r_code = kept("r_code", PASSES, [P, T], U32)
+        r_scale = kept("r_scale", PASSES, [P, T], U8)
 
-        def read_back(chunk, s):
-            col, width, rows = back_columns(chunk, s)
-            back = bank_tile(back_bank(chunk, s))
+        scale_rows = w4_scales.bitcast(I32).rearrange("a (q r) n -> a r q n", r=4)
+
+        def load_x(target, a, t0, width):
+            rows = x[a * P * PACK : (a + 1) * P * PACK, t0 : t0 + width]
+            nc.sync.dma_start(out=target[:], in_=rows.rearrange("(p j) t -> p j t", j=PACK))
+
+        def load_words(a, side):
+            words = w4_words[a, :, side * 2 * LOW * P : (side + 1) * 2 * LOW * P]
+            nc.sync.dma_start(out=w_code[2 * a + side][:].bitcast(I32), in_=words.bitcast(I32))
+
+        for part in range(EARLY_PARTS):
+            load_x(raw_early[part], *part_place(part), PART)
+            if 0 < part <= PASSES:
+                load_words(part - 1, 1)
+            if part < PASSES:
+                for r in range(4):
+                    nc.sync.dma_start(out=w_scale[part][:].bitcast(I32)[r:P:32, :], in_=scale_rows[part, r])
+                load_words(part, 0)
+        for a in range(PASSES):
+            load_x(raw_late[a], a, BANK, BANK)
+
+        def raw(part):
+            if part < EARLY_PARTS:
+                return raw_early[part][:]
+            a, t0 = part_place(part)
+            return raw_late[a][:, :, t0 - BANK : t0 - BANK + PART]
+
+        def round_x(part, cols, copy):
+            copy(
+                out=rounded[part][:, cols, :].rearrange("p (c i) j -> p c j i", i=RUN),
+                in_=raw(part)[:, :, cols].rearrange("p j (c i) -> p c j i", i=RUN),
+            )
+
+        def quantise(part, cols, source, code, scale, dtype):
+            a, t0 = part_place(part)
+            span = slice(t0 + cols.start, t0 + cols.stop)
+            nc.vector.quantize_mx(
+                out=code[a][:, span].bitcast(dtype),
+                scales=scale[a][:, span],
+                in_=source[part][:, cols, :].rearrange("p t j -> p (t j)"),
+            )
+
+        whole = slice(0, PART)
+        pieces = (slice(0, PIECE), slice(PIECE, PART))
+
+        def first(part, cols=whole):
+            quantise(part, cols, rounded, q_code, q_scale, E4M3)
+
+        def second(part, cols=whole):
+            quantise(part, cols, rest, r_code, r_scale, E5M2)
+
+        def back_shape(part, s):
+            if part in NARROW:
+                return pieces[s], range(PACK)
+            return whole, range(2 * s, 2 * s + 2)
+
+        def read_back(part, s):
+            cols, rows = back_shape(part, s)
+            a, t0 = part_place(part)
+            width = cols.stop - cols.start
+            span = slice(t0 + cols.start, t0 + cols.stop)
+            back = bank_tile(LOW + (2 * part + s) % 4 if part < PASSES - 1 else SUM_BANKS + s)
             for place, j in enumerate(rows):
                 nc.tensor.matmul_mx(
                     out=back[:, place * width : (place + 1) * width],
                     lhsT=eye_code[:, j * P : (j + 1) * P].bitcast(E4M3),
                     lhsT_scale=eye_scale[:, j * P : (j + 1) * P],
-                    rhs=q_code[chunk][:, col : col + width].bitcast(E4M3),
-                    rhs_scale=q_scale[chunk][:, col : col + width],
+                    rhs=q_code[a][:, span].bitcast(E4M3),
+                    rhs_scale=q_scale[a][:, span],
                     start=True,
                     stop=True,
                 )
             return back
 
-        unjoined = {}
-
-        def subtract(back, chunk, s):
-            col, width, rows = back_columns(chunk, s)
-            if is_wide(chunk, s):
-                k, u = divmod(s, 2)
-                if u == 0:
-                    unjoined[chunk, k] = keep.tile([P, 2, PAIR, 2], BF16, name="unjoined%d_%d" % (chunk, k))
-                target, run = unjoined[chunk, k][:, u, :, :], WIDE_RUN
-            else:
-                target, run = window(rest, chunk, col, width), RUN
+        def subtract(back, part, s):
+            cols, rows = back_shape(part, s)
+            target = rest[part][:, cols, :] if part in NARROW else unjoined[part][:, s, :, :]
             nc.vector.tensor_tensor(
-                out=target.rearrange("p (c i) j -> p c j i", i=run),
-                in0=raw_columns(chunk, col, width)[:, rows.start : rows.stop, :].rearrange(
-                    "p j (c i) -> p c j i", i=run
-                ),
-                in1=back[:].rearrange("p (j c i) -> p c j i", j=len(rows), i=run),
+                out=target.rearrange("p (c i) j -> p c j i", i=RUN),
+                in0=raw(part)[:, rows.start : rows.stop, cols].rearrange("p j (c i) -> p c j i", i=RUN),
+                in1=back[:].rearrange("p (j c i) -> p c j i", j=len(rows), i=RUN),
                 op=mybir.AluOpType.subtract,
             )
 
-        def join(chunk, k):
-            source = unjoined[chunk, k][:].rearrange("p u t e -> p (u t e)").bitcast(U32)
-            target = rest[2 * chunk + k][:].rearrange("p t j -> p (t j)").bitcast(U32)
-            nc.scalar.copy(
-                out=target.rearrange("p (t u) -> p t u", u=2), in_=source.rearrange("p (u t) -> p t u", u=2)
+        def join(part, copy, dtype):
+            source = unjoined[part][:].rearrange("p u t e -> p (u t e)").bitcast(dtype)
+            target = rest[part][:].rearrange("p t j -> p (t j)").bitcast(dtype)
+            copy(
+                out=target.rearrange("p (c i u) -> p c u i", u=2, i=RUN),
+                in_=source.rearrange("p (u c i) -> p c u i", u=2, i=RUN),
             )
+
+        def behind_subtraction(part, s):
+            ahead = part + 1
+            if s == 0 and ahead < SHARED:
+                round_x(ahead, pieces[0], nc.vector.tensor_copy)
+                round_x(ahead, pieces[1], nc.scalar.copy)
+            for later in range(SHARED, PARTS):
+                if 2 * part + s == (later + PASSES if EARLY_PARTS <= later < PARTS - 1 else 2 * later - (3 if later < EARLY_PARTS else 5)):
+                    round_x(later, whole, nc.scalar.copy)
+            if ahead == 1 and s == 0:
+                first(ahead, pieces[0])
+                first(ahead, pieces[1])
+            if 1 < ahead <= SCALAR_JOINS + 1 and s == (1 if ahead <= SHARED else 0):
+                first(ahead)
+            if s == 0 and part - 1 not in NARROW and 0 < part <= SCALAR_JOINS:
+                join(part - 1, nc.vector.tensor_copy, I32)
+            if s == 1 and part not in NARROW and part >= SCALAR_JOINS:
+                join(part, nc.scalar.copy, U32)
+            if s == 1 and part and part - 1 not in NARROW:
+                second(part - 1)
+            if s == 1 and SCALAR_JOINS + 1 < part + 2 < PARTS:
+                first(part + 2)
+            if s == 1 and part in NARROW:
+                second(part)
 
         acc = {}
-        second_tier = keep.tile([P, T_TILE], F32)
+        left = {}
+        results = kept("result", 2 * N_TILES + 1, [P, BANK], F32)
 
-        def main_pass(half, n, a, tier, pair):
-            chunk = half * PASSES + a
-            opens = (half, n) not in acc
-            cols = slice(0, T_TILE) if pair is None else slice(pair * PAIR, (pair + 1) * PAIR)
+        def group_of(span, n):
+            return (span, n // 2) if span < QUARTERS else (span, n)
+
+        for span, n, a, tier in pass_order():
+            left[group_of(span, n)] = left.get(group_of(span, n), 0) + 1
+
+        def main_pass(span, n, a, tier):
+            group = group_of(span, n)
+            opens = group not in acc
             if opens:
-                acc[half, n] = bank_tile(sum_bank(half, n))
+                acc[group] = bank_tile(len(acc) % SUM_BANKS)
+            t0, width = [(0, PART), (PART, PART), (BANK, BANK), (BANK, PART), (BANK + PART, PART)][span]
+            place = n % 2 * PART if span < QUARTERS else 0
+            code, scale, dtype = (r_code, r_scale, E5M2) if tier else (q_code, q_scale, E4M3)
+            left[group] = left[group] - 1
             nc.tensor.matmul_mx(
-                out=acc[half, n][:, cols],
-                lhsT=weight_words(a, n).bitcast(E2M1),
+                out=acc[group][:, place : place + width],
+                lhsT=w_code[2 * a + n // LOW][:, n % LOW * 2 * P : (n % LOW + 1) * 2 * P].bitcast(E2M1),
                 lhsT_scale=w_scale[a][:, n * P : (n + 1) * P],
-                rhs=q_code[chunk][:, cols].bitcast(E4M3) if tier == 0 else r_code[chunk][:, cols].bitcast(E5M2),
-                rhs_scale=q_scale[chunk][:, cols] if tier == 0 else r_scale[chunk][:, cols],
+                rhs=code[a][:, t0 : t0 + width].bitcast(dtype),
+                rhs_scale=scale[a][:, t0 : t0 + width],
                 start=opens,
-                stop=a == PASSES - 1 and tier == 1,
+                stop=left[group] == 0,
             )
+            if left[group] == 0:
+                index = list(acc).index(group)
+                copy = nc.vector.tensor_copy if index % 2 and span >= QUARTERS else nc.scalar.copy
+                result = results[index]
+                if span < QUARTERS:
+                    copy(out=result[:], in_=acc[group][:])
+                    rows = out[(n - 1) * P : (n + 1) * P, t0 : t0 + width]
+                    nc.sync.dma_start(
+                        out=rows.rearrange("(h p) t -> p h t", h=2), in_=result[:].rearrange("p (h t) -> p h t", h=2)
+                    )
+                else:
+                    copy(out=result[:, :width], in_=acc[group][:, :width])
+                    nc.sync.dma_start(out=out[n * P : (n + 1) * P, t0 : t0 + width], in_=result[:, :width])
 
-        def empty(half, n, copy):
-            if (half, n) == LAST_TILE:
-                for s in range(PIECES):
-                    cols = slice(s * PIECE, (s + 1) * PIECE)
-                    copy(out=second_tier[:, cols], in_=acc[half, n][:, cols])
+        round_x(0, pieces[0], nc.vector.tensor_copy)
+        round_x(0, pieces[1], nc.scalar.copy)
+        first(0, pieces[0])
+        first(0, pieces[1])
+        for task in tensor_order():
+            if task[0] == "back":
+                subtract(read_back(*task[1:]), *task[1:])
+                behind_subtraction(*task[1:])
             else:
-                result = stage.tile([P, T_TILE], F32, name="result")
-                copy(out=result[:], in_=acc[half, n][:])
-                t0 = half * T_TILE
-                nc.sync.dma_start(out=out[n * P : (n + 1) * P, t0 : t0 + T_TILE], in_=result[:])
+                main_pass(*task[1:])
 
-        frees = {}
 
-        def needs(task):
-            kind, args = task[0], task[1:]
-            if kind == "first":
-                return covering("round", args[0], *columns(*task))
-            if kind == "back":
-                chunk, s = args
-                return covering("first", chunk, *back_columns(chunk, s)[:2]) + frees.get(back_bank(chunk, s), [])
-            if kind == "sub":
-                return [("back",) + args]
-            if kind == "second":
-                col, width = columns(*task)
-                if is_wide(args[0], col // PIECE):
-                    return [("join", args[0], col // PAIR)]
-                return [("sub", args[0], s) for s in range(col // PIECE, (col + width) // PIECE)]
-            if kind == "join":
-                return [("sub", args[0], 2 * args[1]), ("sub", args[0], 2 * args[1] + 1)]
-            if kind == "pass":
-                half, n, a, tier, pair = args
-                chunk = half * PASSES + a
-                col, width = (0, T_TILE) if pair is None else (pair * PAIR, PAIR)
-                operand = covering("second" if tier else "first", chunk, col, width)
-                return operand + ([] if (half, n) in acc else frees.get(sum_bank(half, n), []))
-            if kind == "empty":
-                return [("pass",) + args + (PASSES - 1, 1, None)]
-            return []
-
-        backs = {}
-
-        def issue(engine, task):
-            kind, args = task[0], task[1:]
-            copy = nc.vector.tensor_copy if engine == "vector" else nc.scalar.copy
-            if kind == "round":
-                round_part(*args, copy)
-            elif kind == "first":
-                quantise(*task, rounded, q_code, q_scale, E4M3)
-            elif kind == "second":
-                quantise(*task, rest, r_code, r_scale, E5M2)
-            elif kind == "back":
-                backs[args] = read_back(*args)
-                frees[back_bank(*args)] = [("sub",) + args]
-            elif kind == "sub":
-                subtract(backs[args], *args)
-            elif kind == "join":
-                join(*args)
-            elif kind == "pass":
-                main_pass(*args)
-                frees[sum_bank(*args[:2])] = [("empty",) + args[:2]]
-            else:
-                empty(*args, copy)
-
-        queues = {"vector": vector_order(), "scalar": scalar_order(), "tensor": tensor_order()}
-        issued = set()
-        while any(queues.values()):
-            before = len(issued)
-            for engine, queue in queues.items():
-                if queue and all(step in issued for step in needs(queue[0])):
-                    task = queue[0]
-                    issue(engine, task)
-                    issued.add(task)
-                    queue.remove(task)
-            assert len(issued) > before
-
-        half, n = LAST_TILE
-        total = keep.tile([P, T_TILE], F32)
-        for s in range(PIECES):
-            cols = slice(s * PIECE, (s + 1) * PIECE)
-            small = bank_tile(sum_bank(half, n) + 1 + s)
-            for a in range(PASSES):
-                chunk = half * PASSES + a
-                nc.tensor.matmul_mx(
-                    out=small[:, :PIECE],
-                    lhsT=weight_words(a, n).bitcast(E2M1),
-                    lhsT_scale=w_scale[a][:, n * P : (n + 1) * P],
-                    rhs=q_code[chunk][:, cols].bitcast(E4M3),
-                    rhs_scale=q_scale[chunk][:, cols],
-                    start=(a == 0),
-                    stop=(a == PASSES - 1),
-                )
-            nc.vector.tensor_tensor(
-                out=total[:, cols], in0=small[:, :PIECE], in1=second_tier[:, cols], op=mybir.AluOpType.add
-            )
-            if s % 2 == 1:
-                first = (s - 1) * PIECE
-                t0 = half * T_TILE + first
-                nc.sync.dma_start(out=out[n * P : (n + 1) * P, t0 : t0 + PAIR], in_=total[:, first : first + PAIR])
+SCALAR_JOINS = 8

@@ -250,8 +250,8 @@ def tile_mix_tierx_none_kernel(tc, x, w4_words, w4_scales, out):
             source = unjoined[part][:].rearrange("p u t e -> p (u t e)").bitcast(dtype)
             target = rest[part][:].rearrange("p t j -> p (t j)").bitcast(dtype)
             copy(
-                out=target.rearrange("p (c i u) -> p c u i", u=2, i=RUN),
-                in_=source.rearrange("p (u c i) -> p c u i", u=2, i=RUN),
+                out=target.rearrange("p (t u) -> p t u", u=2),
+                in_=source.rearrange("p (u t) -> p t u", u=2),
             )
 
         def behind_subtraction(part, s):

@@ -21,79 +21,73 @@ N_TILES = N // P
 BANK = 512
 PART = BANK // 2
 PIECE = PART // 2
-QUARTERS = 2
-EARLY_PARTS = QUARTERS * PASSES
-PARTS = 2 * EARLY_PARTS
-LOW = N_TILES // 2
+HALVES = T // BANK
+CHUNKS = HALVES * PASSES
+PARTS = 2 * CHUNKS
+EARLY_PARTS = 2 * PASSES
 SUM_BANKS = 6
 ALIGN = 256
 RUN = 4
 ONE_LOW, ONE_HIGH = 0x3F80, 0x3F800000
 WARM_UP = 5
-WAVE = 6
+WAVE = SUM_BANKS
+FIRST_TILES = WAVE // 2
 PACE = 6
+EARLY_PACE = 10
+GAP = 3
 SHARED = 3
-NARROW = (0, 1, 2, PARTS - 1)
+NARROW = (0, 1, 2, 3, 5)
+HALVED = 4
+VECTOR_JOINS = ()
+SECOND_HALF_START = 72
+THIRD_START = 26
+EARLY_GAP = 4
 
 
 def part_place(part):
-    if part < EARLY_PARTS:
-        quarter, a = divmod(part, PASSES)
-        return a, quarter * PART
-    a, side = divmod(part - EARLY_PARTS, 2)
-    return a, BANK + side * PART
+    chunk, side = divmod(part, 2)
+    half, a = divmod(chunk, PASSES)
+    return a, half * BANK + side * PART
 
 
 def pass_order():
-    low, high = range(LOW), range(LOW, N_TILES)
+    def sweep(half, a, tier, side=None):
+        return [(half, n, a, tier, side) for n in range(WAVE)]
 
-    def sweep(part, tier, tiles):
-        span, a = divmod(part, PASSES)
-        return [(span, n, a, tier) for n in tiles]
-
-    order = sweep(0, 0, low) + sweep(0, 0, high)
-    for part in range(1, PASSES):
-        order.extend(sweep(part, 0, low) + sweep(part - 1, 1, range(N_TILES)) + sweep(part, 0, high))
-    part = PASSES
-    order.extend(sweep(part, 0, low) + sweep(part - 1, 1, range(N_TILES)) + sweep(part + 1, 0, low))
-    order.extend(sweep(part, 0, high) + sweep(part + 1, 0, high) + sweep(part, 1, range(N_TILES)))
-    order.extend(sweep(part + 2, 0, range(N_TILES)))
-    order.extend(sweep(part + 1, 1, range(N_TILES)) + [(2, 0, 0, 0)] + sweep(part + 2, 1, range(N_TILES)))
-    stages = ((0, 0), (1, 0), (0, 1), (2, 0))
+    order = sweep(0, 0, 0, 0) + sweep(0, 0, 0, 1) + sweep(0, 0, 1, 0) + sweep(0, 0, 1, 1)
+    order.extend(sweep(0, 1, 0) + sweep(0, 1, 1, 0) + sweep(0, 1, 1, 1) + sweep(0, 2, 0) + sweep(0, 2, 1))
+    for n in range(WAVE, N_TILES):
+        order.extend([(0, n, a, tier, None) for a in range(PASSES) for tier in range(2)])
+    stages = ((0, 0), (1, 0), (0, 1), (2, 0), (1, 1))
     for i, (a, tier) in enumerate(stages):
-        order.extend([(2, n, a, tier) for n in range(SUM_BANKS - 1) if (2, n, a, tier) not in order])
+        order.extend([(1, n, a, tier, None) for n in range(WAVE - 1 if i + 1 < len(stages) else SWEPT)])
         if i:
-            order.append((2, SUM_BANKS - 1) + stages[i - 1])
+            order.append((1, WAVE - 1) + stages[i - 1] + (None,))
     for n in range(N_TILES - 1):
-        order.extend([(2, n, a, tier) for tier in range(2) for a in range(PASSES) if (2, n, a, tier) not in order])
-    for span in (3, 4):
-        order.extend([(span, N_TILES - 1, a, tier) for a in range(PASSES) for tier in range(2)])
+        order.extend(
+            [(1, n, a, tier, None) for tier in range(2) for a in range(PASSES) if (1, n, a, tier, None) not in order]
+        )
+    for side in range(2):
+        order.extend([(1, N_TILES - 1, a, tier, side) for a in range(PASSES) for tier in range(2)])
     return order
 
 
 def tensor_order():
-    order = pass_order()
     queue, done, back, due = [], 0, 0, 0
-    for work in order:
+    for work in pass_order():
         while back < 2 * PARTS and due <= done:
             queue.append(("back",) + divmod(back, 2))
             back = back + 1
             part, s = divmod(back, 2)
-            if part <= PASSES and s == 0:
-                due = order.index((part // PASSES, 0, part % PASSES, 0))
-            elif part <= PASSES:
-                due = done + (GAP if part else 0)
+            if part < 3:
+                due = (0, WAVE, 3 * WAVE)[part] + s * (0, GAP, EARLY_GAP)[part]
+            elif part <= EARLY_PARTS:
+                due = THIRD_START + EARLY_PACE * (part - 3) + s * EARLY_GAP
             else:
-                due = done + (PACE if back <= 2 * PARTS - 5 else LATE_PACE)
+                due = SECOND_HALF_START + PACE * (back - 2 * EARLY_PARTS - 2)
         queue.append(("pass",) + work)
-        done = done + (2 if work[0] == 2 else 1)
+        done = done + (2 if work[-1] is None else 1)
     return queue
-
-
-GAP = 2
-LATE_PACE = 4
-FIRST_BEHIND = 4
-ROUND_BEHIND = 2
 
 
 def tile_mix_tierx_none_kernel(tc, x, w4_words, w4_scales, out):
@@ -109,18 +103,23 @@ def tile_mix_tierx_none_kernel(tc, x, w4_words, w4_scales, out):
         def kept(name, count, shape, dtype):
             return [keep.tile(shape, dtype, align_bytes=ALIGN, name="%s%d" % (name, i)) for i in range(count)]
 
-        w_scale = kept("w_scale", PASSES, [P, N], U8)
-        for a in (PASSES - 1, 0, 1):
-            nc.vector.memset(w_scale[a][:].bitcast(U32), 0)
+        early = WAVE * P
+        late = (N_TILES - WAVE) * P
+        planes = kept("planes", PASSES - 1, [P, early], U8)
+        last_planes = keep.tile([P, early + PASSES * late], U8, align_bytes=ALIGN)
+        for plane in [last_planes] + planes:
+            nc.vector.memset(plane[:].bitcast(U32), 0)
+        early_scale = [plane[:] for plane in planes] + [last_planes[:, :early]]
+        late_scale = last_planes[:, early:].rearrange("p (a n) -> p a n", a=PASSES)
 
         unread = bank_tile(0)
-        zeros = w_scale[PASSES - 1]
+        zeros = last_planes
         for turn in range(WARM_UP):
             nc.tensor.matmul_mx(
                 out=unread[:],
                 lhsT=zeros[:, : PACK * P].bitcast(E4M3),
                 lhsT_scale=zeros[:, :P],
-                rhs=zeros[:].bitcast(E2M1),
+                rhs=zeros[:, : 2 * BANK].bitcast(E2M1),
                 rhs_scale=zeros[:, :BANK],
                 start=True,
                 stop=True,
@@ -151,9 +150,11 @@ def tile_mix_tierx_none_kernel(tc, x, w4_words, w4_scales, out):
                 in_=eye_rows[u][:].rearrange("p e w -> p (e w)").bitcast(BF16),
             )
 
-        w_code = kept("w_code", 2 * PASSES, [P, 2 * LOW * P], U8)
-        raw_early = kept("raw_early", EARLY_PARTS, [P, PACK, PART], F32)
-        raw_late = kept("raw_late", PASSES, [P, PACK, BANK], F32)
+        w_first = keep.tile([P, 2 * FIRST_TILES * P], U8, align_bytes=ALIGN)
+        w_code = kept("w_code", PASSES, [P, 2 * WAVE * P], U8)
+        w_late = keep.tile([P, PASSES, 2 * (N_TILES - WAVE) * P], U8, align_bytes=ALIGN)
+        raw_early = kept("raw_early", 2 * HALVED, [P, PACK, PART], F32)
+        raw_late = kept("raw_late", CHUNKS - HALVED, [P, PACK, BANK], F32)
         rounded = kept("rounded", PARTS, [P, PART, PACK], BF16)
         rest = kept("rest", PARTS, [P, PART, PACK], BF16)
         unjoined = {part: keep.tile([P, 2, PART, 2], BF16, align_bytes=ALIGN, name="unjoined%d" % part) for part in range(PARTS) if part not in NARROW}
@@ -162,32 +163,54 @@ def tile_mix_tierx_none_kernel(tc, x, w4_words, w4_scales, out):
         r_code = kept("r_code", PASSES, [P, T], U32)
         r_scale = kept("r_scale", PASSES, [P, T], U8)
 
-        scale_rows = w4_scales.bitcast(I32).rearrange("a (q r) n -> a r q n", r=4)
+        scale_rows = w4_scales.bitcast(I32).rearrange("a (q r) n -> r q a n", r=4)
 
         def load_x(target, a, t0, width):
             rows = x[a * P * PACK : (a + 1) * P * PACK, t0 : t0 + width]
             nc.sync.dma_start(out=target[:], in_=rows.rearrange("(p j) t -> p j t", j=PACK))
 
-        def load_words(a, side):
-            words = w4_words[a, :, side * 2 * LOW * P : (side + 1) * 2 * LOW * P]
-            nc.sync.dma_start(out=w_code[2 * a + side][:].bitcast(I32), in_=words.bitcast(I32))
+        def load_weights(a, target, first, last):
+            words = w4_words[a, :, 2 * first * P : 2 * last * P]
+            nc.sync.dma_start(out=target.bitcast(I32), in_=words.bitcast(I32))
 
-        for part in range(EARLY_PARTS):
-            load_x(raw_early[part], *part_place(part), PART)
-            if 0 < part <= PASSES:
-                load_words(part - 1, 1)
-            if part < PASSES:
+        def load_scales(a):
+            for r in range(4):
+                nc.sync.dma_start(out=early_scale[a].bitcast(I32)[r:P:32, :], in_=scale_rows[r, :, a, : early // 4])
+
+        for chunk in range(CHUNKS):
+            a, t0 = part_place(2 * chunk)
+            if chunk < HALVED:
+                load_x(raw_early[2 * chunk], a, t0, PART)
+                load_x(raw_early[2 * chunk + 1], a, t0 + PART, PART)
+            else:
+                load_x(raw_late[chunk - HALVED], a, t0, BANK)
+            if chunk == 0:
+                load_scales(a)
+                load_weights(a, w_first[:], 0, FIRST_TILES)
+                load_weights(a, w_code[a][:, 2 * FIRST_TILES * P :], FIRST_TILES, WAVE)
+            elif chunk < PASSES:
+                load_scales(a)
+                load_weights(a, w_code[a][:], 0, WAVE)
+            if chunk == PASSES + 1:
+                words = w4_words[:, :, 2 * early :].bitcast(I32).rearrange("a p n -> p a n")
+                nc.sync.dma_start(out=w_late[:].bitcast(I32), in_=words)
                 for r in range(4):
-                    nc.sync.dma_start(out=w_scale[part][:].bitcast(I32)[r:P:32, :], in_=scale_rows[part, r])
-                load_words(part, 0)
-        for a in range(PASSES):
-            load_x(raw_late[a], a, BANK, BANK)
+                    nc.sync.dma_start(out=late_scale.bitcast(I32)[r:P:32], in_=scale_rows[r, :, :, early // 4 :])
+
+        def weight_words(a, n):
+            if n >= WAVE:
+                return w_late[:, a, 2 * (n - WAVE) * P : 2 * (n - WAVE + 1) * P]
+            return (w_first if a == 0 and n < FIRST_TILES else w_code[a])[:, 2 * n * P : 2 * (n + 1) * P]
+
+        def weight_scales(a, n):
+            if n >= WAVE:
+                return late_scale[:, a, (n - WAVE) * P : (n - WAVE + 1) * P]
+            return early_scale[a][:, n * P : (n + 1) * P]
 
         def raw(part):
-            if part < EARLY_PARTS:
+            if part < 2 * HALVED:
                 return raw_early[part][:]
-            a, t0 = part_place(part)
-            return raw_late[a][:, :, t0 - BANK : t0 - BANK + PART]
+            return raw_late[part // 2 - HALVED][:, :, part % 2 * PART : (part % 2 + 1) * PART]
 
         def round_x(part, cols, copy):
             copy(
@@ -223,7 +246,7 @@ def tile_mix_tierx_none_kernel(tc, x, w4_words, w4_scales, out):
             a, t0 = part_place(part)
             width = cols.stop - cols.start
             span = slice(t0 + cols.start, t0 + cols.stop)
-            back = bank_tile(LOW + (2 * part + s) % 4 if part < PASSES - 1 else SUM_BANKS + s)
+            back = bank_tile(SUM_BANKS + s)
             for place, j in enumerate(rows):
                 nc.tensor.matmul_mx(
                     out=back[:, place * width : (place + 1) * width],
@@ -254,76 +277,78 @@ def tile_mix_tierx_none_kernel(tc, x, w4_words, w4_scales, out):
                 in_=source.rearrange("p (u t) -> p t u", u=2),
             )
 
+        def share_rounding(part):
+            round_x(part, pieces[0], nc.vector.tensor_copy)
+            round_x(part, pieces[1], nc.scalar.copy)
+
         def behind_subtraction(part, s):
-            ahead = part + 1
-            if s == 0 and ahead < SHARED:
-                round_x(ahead, pieces[0], nc.vector.tensor_copy)
-                round_x(ahead, pieces[1], nc.scalar.copy)
-            for later in range(SHARED, PARTS):
-                if 2 * part + s == (later + PASSES if EARLY_PARTS <= later < PARTS - 1 else 2 * later - (3 if later < EARLY_PARTS else 5)):
-                    round_x(later, whole, nc.scalar.copy)
-            if ahead == 1 and s == 0:
-                first(ahead, pieces[0])
-                first(ahead, pieces[1])
-            if 1 < ahead <= SCALAR_JOINS + 1 and s == (1 if ahead <= SHARED else 0):
-                first(ahead)
-            if s == 0 and part - 1 not in NARROW and 0 < part <= SCALAR_JOINS:
-                join(part - 1, nc.vector.tensor_copy, I32)
-            if s == 1 and part not in NARROW and part >= SCALAR_JOINS:
+            back = 2 * part + s
+            for later in range(2, PARTS):
+                if back == 2 * later - 3:
+                    if later <= SHARED:
+                        for cols in pieces[later - 2 :]:
+                            round_x(later, cols, nc.scalar.copy)
+                    else:
+                        round_x(later, whole, nc.scalar.copy)
+            if s == 0 and part and part - 1 not in NARROW:
+                join(part - 1, nc.scalar.copy, U32)
+            if back == 2 * PARTS - 1:
                 join(part, nc.scalar.copy, U32)
-            if s == 1 and part and part - 1 not in NARROW:
+            if back == 0:
+                first(1)
+            if back == 3:
+                first(2, pieces[0])
+            if SHARED < part + 1 < PARTS and s == 0:
+                first(part + 1)
+            if part and part - 1 not in AT_ONCE and s == (part - 1 not in NARROW):
                 second(part - 1)
-            if s == 1 and SCALAR_JOINS + 1 < part + 2 < PARTS:
-                first(part + 2)
-            if s == 1 and part in NARROW:
+            if s == 1 and part in AT_ONCE:
                 second(part)
+            if back == 3:
+                round_x(SHARED, pieces[0], nc.vector.tensor_copy)
+                first(2, pieces[1])
+                first(SHARED)
 
         acc = {}
         left = {}
         results = kept("result", 2 * N_TILES + 1, [P, BANK], F32)
 
-        def group_of(span, n):
-            return (span, n // 2) if span < QUARTERS else (span, n)
+        def group_of(half, n, side):
+            return (half, n, side if (half, n) == (HALVES - 1, N_TILES - 1) else None)
 
-        for span, n, a, tier in pass_order():
-            left[group_of(span, n)] = left.get(group_of(span, n), 0) + 1
+        for half, n, a, tier, side in pass_order():
+            left[group_of(half, n, side)] = left.get(group_of(half, n, side), 0) + 1
 
-        def main_pass(span, n, a, tier):
-            group = group_of(span, n)
+        def main_pass(half, n, a, tier, side):
+            group = group_of(half, n, side)
             opens = group not in acc
             if opens:
                 acc[group] = bank_tile(len(acc) % SUM_BANKS)
-            t0, width = [(0, PART), (PART, PART), (BANK, BANK), (BANK, PART), (BANK + PART, PART)][span]
-            place = n % 2 * PART if span < QUARTERS else 0
+            cols = slice(0, BANK) if side is None else slice(side * PART, (side + 1) * PART)
+            span = slice(half * BANK + cols.start, half * BANK + cols.stop)
             code, scale, dtype = (r_code, r_scale, E5M2) if tier else (q_code, q_scale, E4M3)
             left[group] = left[group] - 1
             nc.tensor.matmul_mx(
-                out=acc[group][:, place : place + width],
-                lhsT=w_code[2 * a + n // LOW][:, n % LOW * 2 * P : (n % LOW + 1) * 2 * P].bitcast(E2M1),
-                lhsT_scale=w_scale[a][:, n * P : (n + 1) * P],
-                rhs=code[a][:, t0 : t0 + width].bitcast(dtype),
-                rhs_scale=scale[a][:, t0 : t0 + width],
+                out=acc[group][:, cols],
+                lhsT=weight_words(a, n).bitcast(E2M1),
+                lhsT_scale=weight_scales(a, n),
+                rhs=code[a][:, span].bitcast(dtype),
+                rhs_scale=scale[a][:, span],
                 start=opens,
                 stop=left[group] == 0,
             )
             if left[group] == 0:
                 index = list(acc).index(group)
-                copy = nc.vector.tensor_copy if index % 2 and span >= QUARTERS else nc.scalar.copy
-                result = results[index]
-                if span < QUARTERS:
-                    copy(out=result[:], in_=acc[group][:])
-                    rows = out[(n - 1) * P : (n + 1) * P, t0 : t0 + width]
-                    nc.sync.dma_start(
-                        out=rows.rearrange("(h p) t -> p h t", h=2), in_=result[:].rearrange("p (h t) -> p h t", h=2)
-                    )
-                else:
-                    copy(out=result[:, :width], in_=acc[group][:, :width])
-                    nc.sync.dma_start(out=out[n * P : (n + 1) * P, t0 : t0 + width], in_=result[:, :width])
+                copy = nc.scalar.copy if index % 2 else nc.vector.tensor_copy
+                if group[2] is None:
+                    cols, span = slice(0, BANK), slice(half * BANK, (half + 1) * BANK)
+                copy(out=results[index][:, cols], in_=acc[group][:, cols])
+                nc.sync.dma_start(out=out[n * P : (n + 1) * P, span], in_=results[index][:, cols])
 
-        round_x(0, pieces[0], nc.vector.tensor_copy)
-        round_x(0, pieces[1], nc.scalar.copy)
+        share_rounding(0)
         first(0, pieces[0])
         first(0, pieces[1])
+        share_rounding(1)
         for task in tensor_order():
             if task[0] == "back":
                 subtract(read_back(*task[1:]), *task[1:])
@@ -332,4 +357,6 @@ def tile_mix_tierx_none_kernel(tc, x, w4_words, w4_scales, out):
                 main_pass(*task[1:])
 
 
-SCALAR_JOINS = 8
+ROUND_LEAD = 5
+AT_ONCE = (0, 1, 3, 5, PARTS - 1)
+SWEPT = 3

@@ -36,11 +36,11 @@ PACE = 6
 EARLY_PACE = 10
 GAP = 3
 SHARED = 3
-NARROW = (0, 1, 2, 3, 5)
+NARROW = (0, 1, 2, 5)
 HALVED = 4
 VECTOR_JOINS = ()
-SECOND_HALF_START = 72
-THIRD_START = 26
+SECOND_HALF_START = 78
+THIRD_START = 40
 EARLY_GAP = 4
 
 
@@ -54,8 +54,10 @@ def pass_order():
     def sweep(half, a, tier, side=None):
         return [(half, n, a, tier, side) for n in range(WAVE)]
 
-    order = sweep(0, 0, 0, 0) + sweep(0, 0, 0, 1) + sweep(0, 0, 1, 0) + sweep(0, 0, 1, 1)
-    order.extend(sweep(0, 1, 0) + sweep(0, 1, 1, 0) + sweep(0, 1, 1, 1) + sweep(0, 2, 0) + sweep(0, 2, 1))
+    order = sweep(0, 0, 0, 0)
+    for part in range(1, 4):
+        order.extend(sweep(0, part // 2, 0, part % 2) + sweep(0, (part - 1) // 2, 1, (part - 1) % 2))
+    order.extend(sweep(0, 2, 0) + sweep(0, 1, 1, 1) + sweep(0, 2, 1))
     for n in range(WAVE, N_TILES):
         order.extend([(0, n, a, tier, None) for a in range(PASSES) for tier in range(2)])
     stages = ((0, 0), (1, 0), (0, 1), (2, 0), (1, 1))
@@ -79,10 +81,10 @@ def tensor_order():
             queue.append(("back",) + divmod(back, 2))
             back = back + 1
             part, s = divmod(back, 2)
-            if part < 3:
-                due = (0, WAVE, 3 * WAVE)[part] + s * (0, GAP, EARLY_GAP)[part]
+            if part < 4:
+                due = max(2 * part - 1, 0) * WAVE + s * (EARLY_GAP if part else 0)
             elif part <= EARLY_PARTS:
-                due = THIRD_START + EARLY_PACE * (part - 3) + s * EARLY_GAP
+                due = (40, 42, 46, 50, 60, 60)[back - 8]
             else:
                 due = SECOND_HALF_START + PACE * (back - 2 * EARLY_PARTS - 2)
         queue.append(("pass",) + work)
@@ -142,13 +144,16 @@ def tile_mix_tierx_none_kernel(tc, x, w4_words, w4_scales, out):
                     op0=mybir.AluOpType.is_equal,
                     op1=mybir.AluOpType.mult,
                 )
-        for u in range(2):
+
+        def quantise_eye(u):
             block = slice(u * 2 * P, (u + 1) * 2 * P)
             nc.vector.quantize_mx(
                 out=eye_code[:, block].bitcast(E4M3),
                 scales=eye_scale[:, block],
                 in_=eye_rows[u][:].rearrange("p e w -> p (e w)").bitcast(BF16),
             )
+
+        quantise_eye(0)
 
         w_first = keep.tile([P, 2 * FIRST_TILES * P], U8, align_bytes=ALIGN)
         w_code = kept("w_code", PASSES, [P, 2 * WAVE * P], U8)
@@ -181,6 +186,9 @@ def tile_mix_tierx_none_kernel(tc, x, w4_words, w4_scales, out):
             a, t0 = part_place(2 * chunk)
             if chunk < HALVED:
                 load_x(raw_early[2 * chunk], a, t0, PART)
+                if chunk == 1:
+                    load_scales(a)
+                    load_weights(a, w_code[a][:], 0, WAVE)
                 load_x(raw_early[2 * chunk + 1], a, t0 + PART, PART)
             else:
                 load_x(raw_late[chunk - HALVED], a, t0, BANK)
@@ -188,7 +196,7 @@ def tile_mix_tierx_none_kernel(tc, x, w4_words, w4_scales, out):
                 load_scales(a)
                 load_weights(a, w_first[:], 0, FIRST_TILES)
                 load_weights(a, w_code[a][:, 2 * FIRST_TILES * P :], FIRST_TILES, WAVE)
-            elif chunk < PASSES:
+            elif chunk == 2:
                 load_scales(a)
                 load_weights(a, w_code[a][:], 0, WAVE)
             if chunk == PASSES + 1:
@@ -284,30 +292,23 @@ def tile_mix_tierx_none_kernel(tc, x, w4_words, w4_scales, out):
         def behind_subtraction(part, s):
             back = 2 * part + s
             for later in range(2, PARTS):
-                if back == 2 * later - 3:
-                    if later <= SHARED:
-                        for cols in pieces[later - 2 :]:
-                            round_x(later, cols, nc.scalar.copy)
-                    else:
-                        round_x(later, whole, nc.scalar.copy)
+                if back == (2 * later - 3 if later != 8 else 14):
+                    for cols in pieces if later == 2 else [whole]:
+                        round_x(later, cols, nc.scalar.copy)
             if s == 0 and part and part - 1 not in NARROW:
                 join(part - 1, nc.scalar.copy, U32)
             if back == 2 * PARTS - 1:
                 join(part, nc.scalar.copy, U32)
-            if back == 0:
-                first(1)
-            if back == 3:
-                first(2, pieces[0])
-            if SHARED < part + 1 < PARTS and s == 0:
+            if part == 1:
+                first(2, pieces[s])
+            elif s == 0 and part + 1 < PARTS and part + 1 != EARLY_PARTS - 1:
                 first(part + 1)
-            if part and part - 1 not in AT_ONCE and s == (part - 1 not in NARROW):
+            if s == 1 and part + 2 == EARLY_PARTS - 1:
+                first(part + 2)
+            if s == 1 and part and part - 1 not in AT_ONCE:
                 second(part - 1)
             if s == 1 and part in AT_ONCE:
                 second(part)
-            if back == 3:
-                round_x(SHARED, pieces[0], nc.vector.tensor_copy)
-                first(2, pieces[1])
-                first(SHARED)
 
         acc = {}
         left = {}
@@ -339,13 +340,14 @@ def tile_mix_tierx_none_kernel(tc, x, w4_words, w4_scales, out):
             )
             if left[group] == 0:
                 index = list(acc).index(group)
-                copy = nc.scalar.copy if index % 2 else nc.vector.tensor_copy
+                copy = nc.vector.tensor_copy if index % 2 else nc.scalar.copy
                 if group[2] is None:
                     cols, span = slice(0, BANK), slice(half * BANK, (half + 1) * BANK)
                 copy(out=results[index][:, cols], in_=acc[group][:, cols])
                 nc.sync.dma_start(out=out[n * P : (n + 1) * P, span], in_=results[index][:, cols])
 
         share_rounding(0)
+        quantise_eye(1)
         first(0, pieces[0])
         first(0, pieces[1])
         share_rounding(1)
@@ -358,5 +360,5 @@ def tile_mix_tierx_none_kernel(tc, x, w4_words, w4_scales, out):
 
 
 ROUND_LEAD = 5
-AT_ONCE = (0, 1, 3, 5, PARTS - 1)
-SWEPT = 3
+AT_ONCE = (0, 1, 2, 5, PARTS - 1)
+SWEPT = 5

@@ -37,7 +37,7 @@ EARLY_PACE = 10
 GAP = 3
 SHARED = 3
 NARROW = (0, 1, 2, 5)
-HALVED = 4
+LATE_BEHIND = 8
 VECTOR_JOINS = ()
 SECOND_HALF_START = 78
 THIRD_START = 40
@@ -82,7 +82,7 @@ def tensor_order():
             back = back + 1
             part, s = divmod(back, 2)
             if part < 4:
-                due = max(2 * part - 1, 0) * WAVE + s * (EARLY_GAP if part else 0)
+                due = 9 + 3 * s if part == 1 else max(2 * part - 1, 0) * WAVE + s * (EARLY_GAP if part else 0)
             elif part <= EARLY_PARTS:
                 due = (40, 42, 46, 50, 60, 60)[back - 8]
             else:
@@ -155,11 +155,10 @@ def tile_mix_tierx_none_kernel(tc, x, w4_words, w4_scales, out):
 
         quantise_eye(0)
 
-        w_first = keep.tile([P, 2 * FIRST_TILES * P], U8, align_bytes=ALIGN)
-        w_code = kept("w_code", PASSES, [P, 2 * WAVE * P], U8)
-        w_late = keep.tile([P, PASSES, 2 * (N_TILES - WAVE) * P], U8, align_bytes=ALIGN)
-        raw_early = kept("raw_early", 2 * HALVED, [P, PACK, PART], F32)
-        raw_late = kept("raw_late", CHUNKS - HALVED, [P, PACK, BANK], F32)
+        w_code = kept("w_code", 2 * (PASSES - 1), [P, early], U8)
+        w_last = keep.tile([P, 2 * early], U8, align_bytes=ALIGN)
+        w_late = keep.tile([P, PASSES, 2 * late], U8, align_bytes=ALIGN)
+        raw = kept("raw", PARTS, [P, PACK, PART], F32)
         rounded = kept("rounded", PARTS, [P, PART, PACK], BF16)
         rest = kept("rest", PARTS, [P, PART, PACK], BF16)
         unjoined = {part: keep.tile([P, 2, PART, 2], BF16, align_bytes=ALIGN, name="unjoined%d" % part) for part in range(PARTS) if part not in NARROW}
@@ -182,24 +181,17 @@ def tile_mix_tierx_none_kernel(tc, x, w4_words, w4_scales, out):
             for r in range(4):
                 nc.sync.dma_start(out=early_scale[a].bitcast(I32)[r:P:32, :], in_=scale_rows[r, :, a, : early // 4])
 
-        for chunk in range(CHUNKS):
-            a, t0 = part_place(2 * chunk)
-            if chunk < HALVED:
-                load_x(raw_early[2 * chunk], a, t0, PART)
-                if chunk == 1:
-                    load_scales(a)
-                    load_weights(a, w_code[a][:], 0, WAVE)
-                load_x(raw_early[2 * chunk + 1], a, t0 + PART, PART)
-            else:
-                load_x(raw_late[chunk - HALVED], a, t0, BANK)
-            if chunk == 0:
-                load_scales(a)
-                load_weights(a, w_first[:], 0, FIRST_TILES)
-                load_weights(a, w_code[a][:, 2 * FIRST_TILES * P :], FIRST_TILES, WAVE)
-            elif chunk == 2:
-                load_scales(a)
-                load_weights(a, w_code[a][:], 0, WAVE)
-            if chunk == PASSES + 1:
+        for part in range(PARTS):
+            load_x(raw[part], *part_place(part), PART)
+            if part in (1, 2):
+                load_scales(part - 1)
+                load_weights(part - 1, w_code[2 * part - 2][:], 0, FIRST_TILES)
+            if part in (1, 3):
+                load_weights(part // 2, w_code[part][:], FIRST_TILES, WAVE)
+            if part == EARLY_PARTS - 1:
+                load_scales(PASSES - 1)
+                load_weights(PASSES - 1, w_last[:], 0, WAVE)
+            if part == LATE_BEHIND:
                 words = w4_words[:, :, 2 * early :].bitcast(I32).rearrange("a p n -> p a n")
                 nc.sync.dma_start(out=w_late[:].bitcast(I32), in_=words)
                 for r in range(4):
@@ -208,22 +200,20 @@ def tile_mix_tierx_none_kernel(tc, x, w4_words, w4_scales, out):
         def weight_words(a, n):
             if n >= WAVE:
                 return w_late[:, a, 2 * (n - WAVE) * P : 2 * (n - WAVE + 1) * P]
-            return (w_first if a == 0 and n < FIRST_TILES else w_code[a])[:, 2 * n * P : 2 * (n + 1) * P]
+            if a == PASSES - 1:
+                return w_last[:, 2 * n * P : 2 * (n + 1) * P]
+            side, place = divmod(n, FIRST_TILES)
+            return w_code[2 * a + side][:, 2 * place * P : 2 * (place + 1) * P]
 
         def weight_scales(a, n):
             if n >= WAVE:
                 return late_scale[:, a, (n - WAVE) * P : (n - WAVE + 1) * P]
             return early_scale[a][:, n * P : (n + 1) * P]
 
-        def raw(part):
-            if part < 2 * HALVED:
-                return raw_early[part][:]
-            return raw_late[part // 2 - HALVED][:, :, part % 2 * PART : (part % 2 + 1) * PART]
-
         def round_x(part, cols, copy):
             copy(
                 out=rounded[part][:, cols, :].rearrange("p (c i) j -> p c j i", i=RUN),
-                in_=raw(part)[:, :, cols].rearrange("p j (c i) -> p c j i", i=RUN),
+                in_=raw[part][:, :, cols].rearrange("p j (c i) -> p c j i", i=RUN),
             )
 
         def quantise(part, cols, source, code, scale, dtype):
@@ -272,7 +262,7 @@ def tile_mix_tierx_none_kernel(tc, x, w4_words, w4_scales, out):
             target = rest[part][:, cols, :] if part in NARROW else unjoined[part][:, s, :, :]
             nc.vector.tensor_tensor(
                 out=target.rearrange("p (c i) j -> p c j i", i=RUN),
-                in0=raw(part)[:, rows.start : rows.stop, cols].rearrange("p j (c i) -> p c j i", i=RUN),
+                in0=raw[part][:, rows.start : rows.stop, cols].rearrange("p j (c i) -> p c j i", i=RUN),
                 in1=back[:].rearrange("p (j c i) -> p c j i", j=len(rows), i=RUN),
                 op=mybir.AluOpType.subtract,
             )
@@ -292,27 +282,31 @@ def tile_mix_tierx_none_kernel(tc, x, w4_words, w4_scales, out):
         def behind_subtraction(part, s):
             back = 2 * part + s
             for later in range(2, PARTS):
-                if back == (2 * later - 3 if later != 8 else 14):
+                if back == 2 * later - 3:
                     for cols in pieces if later == 2 else [whole]:
                         round_x(later, cols, nc.scalar.copy)
             if s == 0 and part and part - 1 not in NARROW:
                 join(part - 1, nc.scalar.copy, U32)
             if back == 2 * PARTS - 1:
                 join(part, nc.scalar.copy, U32)
-            if part == 1:
-                first(2, pieces[s])
-            elif s == 0 and part + 1 < PARTS and part + 1 != EARLY_PARTS - 1:
+            if back == 2:
+                first(2, pieces[0])
+                first(2, pieces[1])
+            elif s == 0 and 1 < part + 1 < PARTS and part + 1 != EARLY_PARTS - 1:
                 first(part + 1)
             if s == 1 and part + 2 == EARLY_PARTS - 1:
                 first(part + 2)
             if s == 1 and part and part - 1 not in AT_ONCE:
                 second(part - 1)
             if s == 1 and part in AT_ONCE:
-                second(part)
+                for cols in pieces if part < 3 else [whole]:
+                    second(part, cols)
 
         acc = {}
         left = {}
-        results = kept("result", 2 * N_TILES + 1, [P, BANK], F32)
+        pairs = kept("pair", WAVE // 2, [P, 2, BANK], F32)
+        results = [pairs[i // 2][:, i % 2, :] for i in range(WAVE)]
+        results.extend([tile[:] for tile in kept("result", 2 * N_TILES + 1 - WAVE, [P, BANK], F32)])
 
         def group_of(half, n, side):
             return (half, n, side if (half, n) == (HALVES - 1, N_TILES - 1) else None)
@@ -344,13 +338,19 @@ def tile_mix_tierx_none_kernel(tc, x, w4_words, w4_scales, out):
                 if group[2] is None:
                     cols, span = slice(0, BANK), slice(half * BANK, (half + 1) * BANK)
                 copy(out=results[index][:, cols], in_=acc[group][:, cols])
-                nc.sync.dma_start(out=out[n * P : (n + 1) * P, span], in_=results[index][:, cols])
+                if index >= WAVE:
+                    nc.sync.dma_start(out=out[n * P : (n + 1) * P, span], in_=results[index][:, cols])
+                elif index % 2:
+                    rows = out[(n - 1) * P : (n + 1) * P, span].rearrange("(h p) t -> p h t", h=2)
+                    nc.sync.dma_start(out=rows, in_=pairs[index // 2][:])
 
         share_rounding(0)
         quantise_eye(1)
         first(0, pieces[0])
         first(0, pieces[1])
         share_rounding(1)
+        first(1, pieces[0])
+        first(1, pieces[1])
         for task in tensor_order():
             if task[0] == "back":
                 subtract(read_back(*task[1:]), *task[1:])
@@ -361,4 +361,4 @@ def tile_mix_tierx_none_kernel(tc, x, w4_words, w4_scales, out):
 
 ROUND_LEAD = 5
 AT_ONCE = (0, 1, 2, 5, PARTS - 1)
-SWEPT = 5
+SWEPT = 4

@@ -17,78 +17,89 @@ E2M1 = mybir.dt.float4_e2m1fn_x4
 P = 128
 PACK = 4
 PASSES = K // (P * PACK)
+TIERS = 2
 N_TILES = N // P
 BANK = 512
 PART = BANK // 2
 PIECE = PART // 2
 HALVES = T // BANK
-CHUNKS = HALVES * PASSES
-PARTS = 2 * CHUNKS
-EARLY_PARTS = 2 * PASSES
-SUM_BANKS = 6
+HALF_PARTS = 2 * PASSES
+PARTS = HALVES * HALF_PARTS
+WAVE = 6
 ALIGN = 256
 RUN = 4
-ONE_LOW, ONE_HIGH = 0x3F80, 0x3F800000
-WARM_UP = 5
-WAVE = SUM_BANKS
-FIRST_TILES = WAVE // 2
-PACE = 6
-EARLY_PACE = 10
-GAP = 3
-SHARED = 3
-NARROW = (0, 1, 2, 5)
-LATE_BEHIND = 8
-VECTOR_JOINS = ()
-SECOND_HALF_START = 78
-THIRD_START = 40
+ONE = (0x3F80, 0x3F800000)
+WARM_UP = 6
+
+BY_SIDES = 4
+NARROW = (0, 1, 2, HALF_PARTS - 1)
 EARLY_GAP = 4
+LATE_GAP = 6
+SWEPT = 4
+LATE_BEHIND = 8
 
 
-def part_place(part):
+def place_of(part):
     chunk, side = divmod(part, 2)
     half, a = divmod(chunk, PASSES)
     return a, half * BANK + side * PART
 
 
-def pass_order():
-    def sweep(half, a, tier, side=None):
-        return [(half, n, a, tier, side) for n in range(WAVE)]
+def sweep(half, a, tier, side=None, tiles=range(WAVE)):
+    return [(half, n, a, tier, side) for n in tiles]
 
-    order = sweep(0, 0, 0, 0)
-    for part in range(1, 4):
-        order.extend(sweep(0, part // 2, 0, part % 2) + sweep(0, (part - 1) // 2, 1, (part - 1) % 2))
-    order.extend(sweep(0, 2, 0) + sweep(0, 1, 1, 1) + sweep(0, 2, 1))
+
+def part_sweep(part, tier):
+    return sweep(0, part // 2, tier, part % 2)
+
+
+def pass_order():
+    order = part_sweep(0, 0)
+    for part in range(1, BY_SIDES):
+        order.extend(part_sweep(part, 0) + part_sweep(part - 1, 1))
+    order.extend(sweep(0, PASSES - 1, 0) + part_sweep(BY_SIDES - 1, 1) + sweep(0, PASSES - 1, 1))
     for n in range(WAVE, N_TILES):
-        order.extend([(0, n, a, tier, None) for a in range(PASSES) for tier in range(2)])
-    stages = ((0, 0), (1, 0), (0, 1), (2, 0), (1, 1))
+        order.extend([(0, n, a, tier, None) for a in range(PASSES) for tier in range(TIERS)])
+    stages = [(0, 0), (1, 0), (0, 1), (2, 0), (1, 1)]
     for i, (a, tier) in enumerate(stages):
-        order.extend([(1, n, a, tier, None) for n in range(WAVE - 1 if i + 1 < len(stages) else SWEPT)])
+        order.extend(sweep(1, a, tier, tiles=range(WAVE - 1 if i + 1 < len(stages) else SWEPT)))
         if i:
-            order.append((1, WAVE - 1) + stages[i - 1] + (None,))
+            order.extend(sweep(1, *stages[i - 1], tiles=[WAVE - 1]))
     for n in range(N_TILES - 1):
-        order.extend(
-            [(1, n, a, tier, None) for tier in range(2) for a in range(PASSES) if (1, n, a, tier, None) not in order]
-        )
+        todo = [(1, n, a, tier, None) for tier in range(TIERS) for a in range(PASSES)]
+        order.extend([work for work in todo if work not in order])
     for side in range(2):
-        order.extend([(1, N_TILES - 1, a, tier, side) for a in range(PASSES) for tier in range(2)])
+        order.extend([(1, N_TILES - 1, a, tier, side) for a in range(PASSES) for tier in range(TIERS)])
     return order
 
 
 def tensor_order():
-    queue, done, back, due = [], 0, 0, 0
-    for work in pass_order():
-        while back < 2 * PARTS and due <= done:
-            queue.append(("back",) + divmod(back, 2))
-            back = back + 1
-            part, s = divmod(back, 2)
-            if part < 4:
-                due = 9 + 3 * s if part == 1 else max(2 * part - 1, 0) * WAVE + s * (EARLY_GAP if part else 0)
-            elif part <= EARLY_PARTS:
-                due = (40, 42, 46, 50, 60, 60)[back - 8]
-            else:
-                due = SECOND_HALF_START + PACE * (back - 2 * EARLY_PARTS - 2)
-        queue.append(("pass",) + work)
+    order = pass_order()
+    start, done = {}, 0
+    for work in order:
+        start[work] = done
         done = done + (2 if work[-1] is None else 1)
+
+    def place(part, s):
+        if part == 0:
+            return 0
+        if part == 1:
+            return start[part_sweep(1, 0)[0]] + (s + 1) * WAVE // 2
+        if part < HALF_PARTS:
+            if part < BY_SIDES:
+                return start[part_sweep(part, 0)[0]] + EARLY_GAP * s
+            behind = 2 * (part - BY_SIDES) + s - 1
+            return start[sweep(0, PASSES - 1, 0)[0]] + (EARLY_GAP * behind if behind >= 0 else -EARLY_GAP // 2)
+        if part == HALF_PARTS:
+            return start[sweep(0, PASSES - 1, 1)[0]]
+        return start[0, WAVE, 0, 0, None] + LATE_GAP * (2 * (part - HALF_PARTS) + s - 1)
+
+    backs = [(part, s) for part in range(PARTS) for s in range(2)]
+    queue = []
+    for work in order:
+        queue.extend([("back",) + back for back in backs if place(*back) <= start[work]])
+        backs = [back for back in backs if place(*back) > start[work]]
+        queue.append(("pass",) + work)
     return queue
 
 
@@ -105,8 +116,7 @@ def tile_mix_tierx_none_kernel(tc, x, w4_words, w4_scales, out):
         def kept(name, count, shape, dtype):
             return [keep.tile(shape, dtype, align_bytes=ALIGN, name="%s%d" % (name, i)) for i in range(count)]
 
-        early = WAVE * P
-        late = (N_TILES - WAVE) * P
+        early, late = WAVE * P, (N_TILES - WAVE) * P
         planes = kept("planes", PASSES - 1, [P, early], U8)
         last_planes = keep.tile([P, early + PASSES * late], U8, align_bytes=ALIGN)
         for plane in [last_planes] + planes:
@@ -115,14 +125,13 @@ def tile_mix_tierx_none_kernel(tc, x, w4_words, w4_scales, out):
         late_scale = last_planes[:, early:].rearrange("p (a n) -> p a n", a=PASSES)
 
         unread = bank_tile(0)
-        zeros = last_planes
         for turn in range(WARM_UP):
             nc.tensor.matmul_mx(
                 out=unread[:],
-                lhsT=zeros[:, : PACK * P].bitcast(E4M3),
-                lhsT_scale=zeros[:, :P],
-                rhs=zeros[:, : 2 * BANK].bitcast(E2M1),
-                rhs_scale=zeros[:, :BANK],
+                lhsT=last_planes[:, : PACK * P].bitcast(E4M3),
+                lhsT_scale=last_planes[:, :P],
+                rhs=last_planes[:, : 2 * BANK].bitcast(E2M1),
+                rhs_scale=last_planes[:, :BANK],
                 start=True,
                 stop=True,
             )
@@ -135,33 +144,34 @@ def tile_mix_tierx_none_kernel(tc, x, w4_words, w4_scales, out):
         eye_code = keep.tile([P, PACK * P], U32, align_bytes=ALIGN)
         eye_scale = keep.tile([P, PACK * P], U8, align_bytes=ALIGN)
         for u in range(2):
-            for e, one in enumerate((ONE_LOW, ONE_HIGH)):
+            for e in range(2):
                 nc.vector.tensor_scalar(
                     out=eye_rows[u][:, e, :],
                     in0=ramp[:],
                     scalar1=float(u),
-                    scalar2=float(one),
+                    scalar2=float(ONE[e]),
                     op0=mybir.AluOpType.is_equal,
                     op1=mybir.AluOpType.mult,
                 )
 
         def quantise_eye(u):
-            block = slice(u * 2 * P, (u + 1) * 2 * P)
+            blocks = slice(u * 2 * P, (u + 1) * 2 * P)
             nc.vector.quantize_mx(
-                out=eye_code[:, block].bitcast(E4M3),
-                scales=eye_scale[:, block],
+                out=eye_code[:, blocks].bitcast(E4M3),
+                scales=eye_scale[:, blocks],
                 in_=eye_rows[u][:].rearrange("p e w -> p (e w)").bitcast(BF16),
             )
 
         quantise_eye(0)
 
-        w_code = kept("w_code", 2 * (PASSES - 1), [P, early], U8)
+        w_early = kept("w_early", 2 * (PASSES - 1), [P, early], U8)
         w_last = keep.tile([P, 2 * early], U8, align_bytes=ALIGN)
         w_late = keep.tile([P, PASSES, 2 * late], U8, align_bytes=ALIGN)
         raw = kept("raw", PARTS, [P, PACK, PART], F32)
         rounded = kept("rounded", PARTS, [P, PART, PACK], BF16)
         rest = kept("rest", PARTS, [P, PART, PACK], BF16)
-        unjoined = {part: keep.tile([P, 2, PART, 2], BF16, align_bytes=ALIGN, name="unjoined%d" % part) for part in range(PARTS) if part not in NARROW}
+        wide = [part for part in range(PARTS) if part not in NARROW]
+        unjoined = dict(zip(wide, kept("unjoined", len(wide), [P, 2, PART, 2], BF16)))
         q_code = kept("q_code", PASSES, [P, T], U32)
         q_scale = kept("q_scale", PASSES, [P, T], U8)
         r_code = kept("r_code", PASSES, [P, T], U32)
@@ -169,46 +179,48 @@ def tile_mix_tierx_none_kernel(tc, x, w4_words, w4_scales, out):
 
         scale_rows = w4_scales.bitcast(I32).rearrange("a (q r) n -> r q a n", r=4)
 
-        def load_x(target, a, t0, width):
-            rows = x[a * P * PACK : (a + 1) * P * PACK, t0 : t0 + width]
-            nc.sync.dma_start(out=target[:], in_=rows.rearrange("(p j) t -> p j t", j=PACK))
-
-        def load_weights(a, target, first, last):
-            words = w4_words[a, :, 2 * first * P : 2 * last * P]
-            nc.sync.dma_start(out=target.bitcast(I32), in_=words.bitcast(I32))
-
         def load_scales(a):
             for r in range(4):
                 nc.sync.dma_start(out=early_scale[a].bitcast(I32)[r:P:32, :], in_=scale_rows[r, :, a, : early // 4])
 
+        def load_words(target, a, first_byte, last_byte):
+            nc.sync.dma_start(out=target[:].bitcast(I32), in_=w4_words[a, :, first_byte:last_byte].bitcast(I32))
+
         for part in range(PARTS):
-            load_x(raw[part], *part_place(part), PART)
-            if part in (1, 2):
-                load_scales(part - 1)
-                load_weights(part - 1, w_code[2 * part - 2][:], 0, FIRST_TILES)
-            if part in (1, 3):
-                load_weights(part // 2, w_code[part][:], FIRST_TILES, WAVE)
-            if part == EARLY_PARTS - 1:
-                load_scales(PASSES - 1)
-                load_weights(PASSES - 1, w_last[:], 0, WAVE)
+            a, t0 = place_of(part)
+            rows = x[a * P * PACK : (a + 1) * P * PACK, t0 : t0 + PART]
+            nc.sync.dma_start(out=raw[part][:], in_=rows.rearrange("(p j) t -> p j t", j=PACK))
+            if part == 1:
+                load_scales(0)
+                load_words(w_early[0], 0, 0, early)
+                load_words(w_early[1], 0, early, 2 * early)
+            if part == 2:
+                load_scales(1)
+                load_words(w_early[2], 1, 0, early)
+            if part == 3:
+                load_words(w_early[3], 1, early, 2 * early)
+            if part == HALF_PARTS - 1:
+                load_scales(2)
+                load_words(w_last, 2, 0, 2 * early)
             if part == LATE_BEHIND:
                 words = w4_words[:, :, 2 * early :].bitcast(I32).rearrange("a p n -> p a n")
                 nc.sync.dma_start(out=w_late[:].bitcast(I32), in_=words)
                 for r in range(4):
                     nc.sync.dma_start(out=late_scale.bitcast(I32)[r:P:32], in_=scale_rows[r, :, :, early // 4 :])
 
-        def weight_words(a, n):
+        def weights(a, n):
             if n >= WAVE:
-                return w_late[:, a, 2 * (n - WAVE) * P : 2 * (n - WAVE + 1) * P]
-            if a == PASSES - 1:
-                return w_last[:, 2 * n * P : 2 * (n + 1) * P]
-            side, place = divmod(n, FIRST_TILES)
-            return w_code[2 * a + side][:, 2 * place * P : 2 * (place + 1) * P]
+                m = n - WAVE
+                return w_late[:, a, 2 * m * P : 2 * (m + 1) * P], late_scale[:, a, m * P : (m + 1) * P]
+            tile, m = (w_last, n) if a == PASSES - 1 else (w_early[2 * a + 2 * n // WAVE], n % (WAVE // 2))
+            return tile[:, 2 * m * P : 2 * (m + 1) * P], early_scale[a][:, n * P : (n + 1) * P]
 
-        def weight_scales(a, n):
-            if n >= WAVE:
-                return late_scale[:, a, (n - WAVE) * P : (n - WAVE + 1) * P]
-            return early_scale[a][:, n * P : (n + 1) * P]
+        whole = slice(0, PART)
+        pieces = (slice(0, PIECE), slice(PIECE, PART))
+
+        def columns(part, cols):
+            t0 = place_of(part)[1]
+            return slice(t0 + cols.start, t0 + cols.stop)
 
         def round_x(part, cols, copy):
             copy(
@@ -217,48 +229,33 @@ def tile_mix_tierx_none_kernel(tc, x, w4_words, w4_scales, out):
             )
 
         def quantise(part, cols, source, code, scale, dtype):
-            a, t0 = part_place(part)
-            span = slice(t0 + cols.start, t0 + cols.stop)
+            a = place_of(part)[0]
             nc.vector.quantize_mx(
-                out=code[a][:, span].bitcast(dtype),
-                scales=scale[a][:, span],
+                out=code[a][:, columns(part, cols)].bitcast(dtype),
+                scales=scale[a][:, columns(part, cols)],
                 in_=source[part][:, cols, :].rearrange("p t j -> p (t j)"),
             )
 
-        whole = slice(0, PART)
-        pieces = (slice(0, PIECE), slice(PIECE, PART))
-
-        def first(part, cols=whole):
+        def first_tier(part, cols):
             quantise(part, cols, rounded, q_code, q_scale, E4M3)
 
-        def second(part, cols=whole):
+        def second_tier(part, cols):
             quantise(part, cols, rest, r_code, r_scale, E5M2)
 
-        def back_shape(part, s):
-            if part in NARROW:
-                return pieces[s], range(PACK)
-            return whole, range(2 * s, 2 * s + 2)
-
-        def read_back(part, s):
-            cols, rows = back_shape(part, s)
-            a, t0 = part_place(part)
-            width = cols.stop - cols.start
-            span = slice(t0 + cols.start, t0 + cols.stop)
-            back = bank_tile(SUM_BANKS + s)
-            for place, j in enumerate(rows):
+        def read_back_and_subtract(part, s):
+            cols, rows = (pieces[s], range(PACK)) if part in NARROW else (whole, range(2 * s, 2 * s + 2))
+            a, width = place_of(part)[0], cols.stop - cols.start
+            back = bank_tile(WAVE + s)
+            for i, j in enumerate(rows):
                 nc.tensor.matmul_mx(
-                    out=back[:, place * width : (place + 1) * width],
+                    out=back[:, i * width : (i + 1) * width],
                     lhsT=eye_code[:, j * P : (j + 1) * P].bitcast(E4M3),
                     lhsT_scale=eye_scale[:, j * P : (j + 1) * P],
-                    rhs=q_code[a][:, span].bitcast(E4M3),
-                    rhs_scale=q_scale[a][:, span],
+                    rhs=q_code[a][:, columns(part, cols)].bitcast(E4M3),
+                    rhs_scale=q_scale[a][:, columns(part, cols)],
                     start=True,
                     stop=True,
                 )
-            return back
-
-        def subtract(back, part, s):
-            cols, rows = back_shape(part, s)
             target = rest[part][:, cols, :] if part in NARROW else unjoined[part][:, s, :, :]
             nc.vector.tensor_tensor(
                 out=target.rearrange("p (c i) j -> p c j i", i=RUN),
@@ -267,98 +264,97 @@ def tile_mix_tierx_none_kernel(tc, x, w4_words, w4_scales, out):
                 op=mybir.AluOpType.subtract,
             )
 
-        def join(part, copy, dtype):
-            source = unjoined[part][:].rearrange("p u t e -> p (u t e)").bitcast(dtype)
-            target = rest[part][:].rearrange("p t j -> p (t j)").bitcast(dtype)
-            copy(
-                out=target.rearrange("p (t u) -> p t u", u=2),
-                in_=source.rearrange("p (u t) -> p t u", u=2),
+        def join(part):
+            source = unjoined[part][:].rearrange("p u t e -> p (u t e)").bitcast(U32)
+            target = rest[part][:].rearrange("p t j -> p (t j)").bitcast(U32)
+            nc.scalar.copy(
+                out=target.rearrange("p (t u) -> p t u", u=2), in_=source.rearrange("p (u t) -> p t u", u=2)
             )
 
-        def share_rounding(part):
-            round_x(part, pieces[0], nc.vector.tensor_copy)
-            round_x(part, pieces[1], nc.scalar.copy)
+        def cuts(part):
+            return pieces if part <= 2 else [whole]
 
         def behind_subtraction(part, s):
-            back = 2 * part + s
-            for later in range(2, PARTS):
-                if back == 2 * later - 3:
-                    for cols in pieces if later == 2 else [whole]:
-                        round_x(later, cols, nc.scalar.copy)
-            if s == 0 and part and part - 1 not in NARROW:
-                join(part - 1, nc.scalar.copy, U32)
-            if back == 2 * PARTS - 1:
-                join(part, nc.scalar.copy, U32)
-            if back == 2:
-                first(2, pieces[0])
-                first(2, pieces[1])
-            elif s == 0 and 1 < part + 1 < PARTS and part + 1 != EARLY_PARTS - 1:
-                first(part + 1)
-            if s == 1 and part + 2 == EARLY_PARTS - 1:
-                first(part + 2)
-            if s == 1 and part and part - 1 not in AT_ONCE:
-                second(part - 1)
-            if s == 1 and part in AT_ONCE:
-                for cols in pieces if part < 3 else [whole]:
-                    second(part, cols)
+            last = part == PARTS - 1
+            if s == 0:
+                if part - 1 in wide:
+                    join(part - 1)
+                if part + 1 not in (1, HALF_PARTS - 1, PARTS):
+                    for cols in cuts(part + 1):
+                        first_tier(part + 1, cols)
+                return
+            if part + 2 < PARTS:
+                for cols in cuts(part + 2):
+                    round_x(part + 2, cols, nc.scalar.copy)
+            if last:
+                join(part)
+            if part + 2 == HALF_PARTS - 1:
+                first_tier(part + 2, whole)
+            if part - 1 in wide:
+                second_tier(part - 1, whole)
+            if part in NARROW or last:
+                for cols in cuts(part):
+                    second_tier(part, cols)
 
-        acc = {}
-        left = {}
         pairs = kept("pair", WAVE // 2, [P, 2, BANK], F32)
         results = [pairs[i // 2][:, i % 2, :] for i in range(WAVE)]
-        results.extend([tile[:] for tile in kept("result", 2 * N_TILES + 1 - WAVE, [P, BANK], F32)])
+        results.extend([tile[:] for tile in kept("result", HALVES * N_TILES + 1 - WAVE, [P, BANK], F32)])
 
         def group_of(half, n, side):
             return (half, n, side if (half, n) == (HALVES - 1, N_TILES - 1) else None)
 
-        for half, n, a, tier, side in pass_order():
-            left[group_of(half, n, side)] = left.get(group_of(half, n, side), 0) + 1
+        groups = [group_of(half, n, side) for half, n, a, tier, side in pass_order()]
+        left = {group: groups.count(group) for group in groups}
+        acc = {}
+
+        def side_columns(side):
+            return slice(0, BANK) if side is None else slice(side * PART, (side + 1) * PART)
 
         def main_pass(half, n, a, tier, side):
             group = group_of(half, n, side)
             opens = group not in acc
             if opens:
-                acc[group] = bank_tile(len(acc) % SUM_BANKS)
-            cols = slice(0, BANK) if side is None else slice(side * PART, (side + 1) * PART)
+                acc[group] = bank_tile(len(acc) % WAVE)
+            left[group] = left[group] - 1
+            cols = side_columns(side)
             span = slice(half * BANK + cols.start, half * BANK + cols.stop)
             code, scale, dtype = (r_code, r_scale, E5M2) if tier else (q_code, q_scale, E4M3)
-            left[group] = left[group] - 1
+            words, scales = weights(a, n)
             nc.tensor.matmul_mx(
                 out=acc[group][:, cols],
-                lhsT=weight_words(a, n).bitcast(E2M1),
-                lhsT_scale=weight_scales(a, n),
+                lhsT=words.bitcast(E2M1),
+                lhsT_scale=scales,
                 rhs=code[a][:, span].bitcast(dtype),
                 rhs_scale=scale[a][:, span],
                 start=opens,
                 stop=left[group] == 0,
             )
             if left[group] == 0:
-                index = list(acc).index(group)
-                copy = nc.vector.tensor_copy if index % 2 else nc.scalar.copy
-                if group[2] is None:
-                    cols, span = slice(0, BANK), slice(half * BANK, (half + 1) * BANK)
-                copy(out=results[index][:, cols], in_=acc[group][:, cols])
-                if index >= WAVE:
-                    nc.sync.dma_start(out=out[n * P : (n + 1) * P, span], in_=results[index][:, cols])
-                elif index % 2:
-                    rows = out[(n - 1) * P : (n + 1) * P, span].rearrange("(h p) t -> p h t", h=2)
-                    nc.sync.dma_start(out=rows, in_=pairs[index // 2][:])
+                empty(group)
 
-        share_rounding(0)
-        quantise_eye(1)
-        first(0, pieces[0])
-        first(0, pieces[1])
-        share_rounding(1)
-        first(1, pieces[0])
-        first(1, pieces[1])
+        def empty(group):
+            half, n, side = group
+            index = list(acc).index(group)
+            cols = side_columns(side)
+            span = slice(half * BANK + cols.start, half * BANK + cols.stop)
+            copy = nc.vector.tensor_copy if index % 2 else nc.scalar.copy
+            copy(out=results[index][:, cols], in_=acc[group][:, cols])
+            if index >= WAVE:
+                nc.sync.dma_start(out=out[n * P : (n + 1) * P, span], in_=results[index][:, cols])
+            elif index % 2:
+                rows = out[(n - 1) * P : (n + 1) * P, span].rearrange("(h p) t -> p h t", h=2)
+                nc.sync.dma_start(out=rows, in_=pairs[index // 2][:])
+
+        for part in range(2):
+            round_x(part, pieces[0], nc.vector.tensor_copy)
+            round_x(part, pieces[1], nc.scalar.copy)
+            if part == 0:
+                quantise_eye(1)
+            for cols in pieces:
+                first_tier(part, cols)
         for task in tensor_order():
             if task[0] == "back":
-                subtract(read_back(*task[1:]), *task[1:])
+                read_back_and_subtract(*task[1:])
                 behind_subtraction(*task[1:])
             else:
                 main_pass(*task[1:])
-
-
-ROUND_LEAD = 5
-AT_ONCE = (0, 1, 2, 5, PARTS - 1)
-SWEPT = 4

@@ -29,14 +29,14 @@ WAVE = 6
 ALIGN = 256
 RUN = 4
 ONE = (0x3F80, 0x3F800000)
-WARM_UP = 6
+WARM_UP = 5
 
-BY_SIDES = 4
-NARROW = (0, 1, 2, HALF_PARTS - 1)
-EARLY_GAP = 4
-LATE_GAP = 6
-SWEPT = 4
-LATE_BEHIND = 8
+SECOND_WAVE = WAVE - 1
+PACE = 3
+
+
+def is_narrow(part):
+    return part < HALF_PARTS or part == PARTS - 1
 
 
 def place_of(part):
@@ -53,53 +53,40 @@ def part_sweep(part, tier):
     return sweep(0, part // 2, tier, part % 2)
 
 
-def pass_order():
-    order = part_sweep(0, 0)
-    for part in range(1, BY_SIDES):
-        order.extend(part_sweep(part, 0) + part_sweep(part - 1, 1))
-    order.extend(sweep(0, PASSES - 1, 0) + part_sweep(BY_SIDES - 1, 1) + sweep(0, PASSES - 1, 1))
-    for n in range(WAVE, N_TILES):
-        order.extend([(0, n, a, tier, None) for a in range(PASSES) for tier in range(TIERS)])
-    stages = [(0, 0), (1, 0), (0, 1), (2, 0), (1, 1)]
-    for i, (a, tier) in enumerate(stages):
-        order.extend(sweep(1, a, tier, tiles=range(WAVE - 1 if i + 1 < len(stages) else SWEPT)))
-        if i:
-            order.extend(sweep(1, *stages[i - 1], tiles=[WAVE - 1]))
-    for n in range(N_TILES - 1):
-        todo = [(1, n, a, tier, None) for tier in range(TIERS) for a in range(PASSES)]
-        order.extend([work for work in todo if work not in order])
-    for side in range(2):
-        order.extend([(1, N_TILES - 1, a, tier, side) for a in range(PASSES) for tier in range(TIERS)])
-    return order
+def whole_tile(half, n, side=None):
+    return [(half, n, a, tier, side) for a in range(PASSES) for tier in range(TIERS)]
 
 
 def tensor_order():
-    order = pass_order()
-    start, done = {}, 0
-    for work in order:
-        start[work] = done
-        done = done + (2 if work[-1] is None else 1)
+    def passes(work):
+        return [("pass",) + step for step in work]
 
-    def place(part, s):
-        if part == 0:
-            return 0
-        if part == 1:
-            return start[part_sweep(1, 0)[0]] + (s + 1) * WAVE // 2
-        if part < HALF_PARTS:
-            if part < BY_SIDES:
-                return start[part_sweep(part, 0)[0]] + EARLY_GAP * s
-            behind = 2 * (part - BY_SIDES) + s - 1
-            return start[sweep(0, PASSES - 1, 0)[0]] + (EARLY_GAP * behind if behind >= 0 else -EARLY_GAP // 2)
-        if part == HALF_PARTS:
-            return start[sweep(0, PASSES - 1, 1)[0]]
-        return start[0, WAVE, 0, 0, None] + LATE_GAP * (2 * (part - HALF_PARTS) + s - 1)
-
-    backs = [(part, s) for part in range(PARTS) for s in range(2)]
     queue = []
-    for work in order:
-        queue.extend([("back",) + back for back in backs if place(*back) <= start[work]])
-        backs = [back for back in backs if place(*back) > start[work]]
-        queue.append(("pass",) + work)
+    for part in range(HALF_PARTS):
+        first, middle = passes(part_sweep(part, 0)), WAVE // 2 if part else 0
+        queue.extend([("back", part, 0)] + first[:middle] + [("back", part, 1)] + first[middle:])
+        if part:
+            queue.extend(passes(part_sweep(part - 1, 1)))
+    rest = part_sweep(HALF_PARTS - 1, 1)
+    for n in range(WAVE, N_TILES):
+        rest.extend(whole_tile(0, n))
+    for a in range(PASSES + 1):
+        if a < PASSES:
+            rest.extend(sweep(1, a, 0, tiles=range(SECOND_WAVE)))
+        if a:
+            rest.extend(sweep(1, a - 1, 1, tiles=range(SECOND_WAVE)))
+    for n in range(SECOND_WAVE, N_TILES - 1):
+        rest.extend(whole_tile(1, n))
+    for side in range(2):
+        rest.extend(whole_tile(1, N_TILES - 1, side))
+    backs = [("back", part, s) for part in range(HALF_PARTS, PARTS) for s in range(2)]
+    columns = 0
+    for step in rest:
+        if backs and columns % (PACE * BANK) == 0:
+            queue.append(backs[0])
+            backs = backs[1:]
+        queue.append(("pass",) + step)
+        columns = columns + (BANK if step[-1] is None else PART)
     return queue
 
 
@@ -164,13 +151,15 @@ def tile_mix_tierx_none_kernel(tc, x, w4_words, w4_scales, out):
 
         quantise_eye(0)
 
-        w_early = kept("w_early", 2 * (PASSES - 1), [P, early], U8)
-        w_last = keep.tile([P, 2 * early], U8, align_bytes=ALIGN)
+        w_early = kept("w_early", PASSES, [P, 2 * early], U8)
         w_late = keep.tile([P, PASSES, 2 * late], U8, align_bytes=ALIGN)
-        raw = kept("raw", PARTS, [P, PACK, PART], F32)
+        raw_parts = kept("raw_part", HALF_PARTS, [P, PACK, PART], F32)
+        raw_chunks = kept("raw_chunk", PASSES, [P, PACK, BANK], F32)
+        raw = [tile[:] for tile in raw_parts]
+        raw.extend([tile[:, :, side * PART : (side + 1) * PART] for tile in raw_chunks for side in range(2)])
         rounded = kept("rounded", PARTS, [P, PART, PACK], BF16)
         rest = kept("rest", PARTS, [P, PART, PACK], BF16)
-        wide = [part for part in range(PARTS) if part not in NARROW]
+        wide = [part for part in range(PARTS) if not is_narrow(part)]
         unjoined = dict(zip(wide, kept("unjoined", len(wide), [P, 2, PART, 2], BF16)))
         q_code = kept("q_code", PASSES, [P, T], U32)
         q_scale = kept("q_scale", PASSES, [P, T], U8)
@@ -179,30 +168,22 @@ def tile_mix_tierx_none_kernel(tc, x, w4_words, w4_scales, out):
 
         scale_rows = w4_scales.bitcast(I32).rearrange("a (q r) n -> r q a n", r=4)
 
-        def load_scales(a):
+        def load_x(target, a, t0, width):
+            rows = x[a * P * PACK : (a + 1) * P * PACK, t0 : t0 + width]
+            nc.sync.dma_start(out=target[:], in_=rows.rearrange("(p j) t -> p j t", j=PACK))
+
+        def load_weights(a):
             for r in range(4):
                 nc.sync.dma_start(out=early_scale[a].bitcast(I32)[r:P:32, :], in_=scale_rows[r, :, a, : early // 4])
+            nc.sync.dma_start(out=w_early[a][:].bitcast(I32), in_=w4_words[a, :, : 2 * early].bitcast(I32))
 
-        def load_words(target, a, first_byte, last_byte):
-            nc.sync.dma_start(out=target[:].bitcast(I32), in_=w4_words[a, :, first_byte:last_byte].bitcast(I32))
-
-        for part in range(PARTS):
-            a, t0 = place_of(part)
-            rows = x[a * P * PACK : (a + 1) * P * PACK, t0 : t0 + PART]
-            nc.sync.dma_start(out=raw[part][:], in_=rows.rearrange("(p j) t -> p j t", j=PACK))
-            if part == 1:
-                load_scales(0)
-                load_words(w_early[0], 0, 0, early)
-                load_words(w_early[1], 0, early, 2 * early)
-            if part == 2:
-                load_scales(1)
-                load_words(w_early[2], 1, 0, early)
-            if part == 3:
-                load_words(w_early[3], 1, early, 2 * early)
-            if part == HALF_PARTS - 1:
-                load_scales(2)
-                load_words(w_last, 2, 0, 2 * early)
-            if part == LATE_BEHIND:
+        for part in range(HALF_PARTS):
+            load_x(raw_parts[part], *place_of(part), PART)
+            if part == 1 or (part and part % 2 == 0):
+                load_weights(part // 2)
+        for a in range(PASSES):
+            load_x(raw_chunks[a], a, BANK, BANK)
+            if a == 1:
                 words = w4_words[:, :, 2 * early :].bitcast(I32).rearrange("a p n -> p a n")
                 nc.sync.dma_start(out=w_late[:].bitcast(I32), in_=words)
                 for r in range(4):
@@ -212,8 +193,7 @@ def tile_mix_tierx_none_kernel(tc, x, w4_words, w4_scales, out):
             if n >= WAVE:
                 m = n - WAVE
                 return w_late[:, a, 2 * m * P : 2 * (m + 1) * P], late_scale[:, a, m * P : (m + 1) * P]
-            tile, m = (w_last, n) if a == PASSES - 1 else (w_early[2 * a + 2 * n // WAVE], n % (WAVE // 2))
-            return tile[:, 2 * m * P : 2 * (m + 1) * P], early_scale[a][:, n * P : (n + 1) * P]
+            return w_early[a][:, 2 * n * P : 2 * (n + 1) * P], early_scale[a][:, n * P : (n + 1) * P]
 
         whole = slice(0, PART)
         pieces = (slice(0, PIECE), slice(PIECE, PART))
@@ -243,7 +223,7 @@ def tile_mix_tierx_none_kernel(tc, x, w4_words, w4_scales, out):
             quantise(part, cols, rest, r_code, r_scale, E5M2)
 
         def read_back_and_subtract(part, s):
-            cols, rows = (pieces[s], range(PACK)) if part in NARROW else (whole, range(2 * s, 2 * s + 2))
+            cols, rows = (pieces[s], range(PACK)) if is_narrow(part) else (whole, range(2 * s, 2 * s + 2))
             a, width = place_of(part)[0], cols.stop - cols.start
             back = bank_tile(WAVE + s)
             for i, j in enumerate(rows):
@@ -256,7 +236,7 @@ def tile_mix_tierx_none_kernel(tc, x, w4_words, w4_scales, out):
                     start=True,
                     stop=True,
                 )
-            target = rest[part][:, cols, :] if part in NARROW else unjoined[part][:, s, :, :]
+            target = rest[part][:, cols, :] if is_narrow(part) else unjoined[part][:, s, :, :]
             nc.vector.tensor_tensor(
                 out=target.rearrange("p (c i) j -> p c j i", i=RUN),
                 in0=raw[part][:, rows.start : rows.stop, cols].rearrange("p j (c i) -> p c j i", i=RUN),
@@ -265,45 +245,34 @@ def tile_mix_tierx_none_kernel(tc, x, w4_words, w4_scales, out):
             )
 
         def join(part):
-            source = unjoined[part][:].rearrange("p u t e -> p (u t e)").bitcast(U32)
-            target = rest[part][:].rearrange("p t j -> p (t j)").bitcast(U32)
-            nc.scalar.copy(
+            source = unjoined[part][:].rearrange("p u t e -> p (u t e)").bitcast(I32)
+            target = rest[part][:].rearrange("p t j -> p (t j)").bitcast(I32)
+            nc.vector.tensor_copy(
                 out=target.rearrange("p (t u) -> p t u", u=2), in_=source.rearrange("p (u t) -> p t u", u=2)
             )
 
-        def cuts(part):
-            return pieces if part <= 2 else [whole]
-
         def behind_subtraction(part, s):
-            last = part == PARTS - 1
             if s == 0:
+                if part + 2 < PARTS:
+                    round_x(part + 2, whole, nc.scalar.copy)
+                if part + 1 < PARTS:
+                    first_tier(part + 1, whole)
                 if part - 1 in wide:
                     join(part - 1)
-                if part + 1 not in (1, HALF_PARTS - 1, PARTS):
-                    for cols in cuts(part + 1):
-                        first_tier(part + 1, cols)
                 return
-            if part + 2 < PARTS:
-                for cols in cuts(part + 2):
-                    round_x(part + 2, cols, nc.scalar.copy)
-            if last:
-                join(part)
-            if part + 2 == HALF_PARTS - 1:
-                first_tier(part + 2, whole)
             if part - 1 in wide:
                 second_tier(part - 1, whole)
-            if part in NARROW or last:
-                for cols in cuts(part):
+            if is_narrow(part):
+                for cols in pieces:
                     second_tier(part, cols)
 
-        pairs = kept("pair", WAVE // 2, [P, 2, BANK], F32)
-        results = [pairs[i // 2][:, i % 2, :] for i in range(WAVE)]
-        results.extend([tile[:] for tile in kept("result", HALVES * N_TILES + 1 - WAVE, [P, BANK], F32)])
+        results = kept("result", HALVES * N_TILES + 1, [P, BANK], F32)
 
         def group_of(half, n, side):
             return (half, n, side if (half, n) == (HALVES - 1, N_TILES - 1) else None)
 
-        groups = [group_of(half, n, side) for half, n, a, tier, side in pass_order()]
+        queue = tensor_order()
+        groups = [group_of(task[1], task[2], task[-1]) for task in queue if task[0] == "pass"]
         left = {group: groups.count(group) for group in groups}
         acc = {}
 
@@ -337,22 +306,18 @@ def tile_mix_tierx_none_kernel(tc, x, w4_words, w4_scales, out):
             index = list(acc).index(group)
             cols = side_columns(side)
             span = slice(half * BANK + cols.start, half * BANK + cols.stop)
-            copy = nc.vector.tensor_copy if index % 2 else nc.scalar.copy
+            copy = nc.vector.tensor_copy if half and index % 2 else nc.scalar.copy
             copy(out=results[index][:, cols], in_=acc[group][:, cols])
-            if index >= WAVE:
-                nc.sync.dma_start(out=out[n * P : (n + 1) * P, span], in_=results[index][:, cols])
-            elif index % 2:
-                rows = out[(n - 1) * P : (n + 1) * P, span].rearrange("(h p) t -> p h t", h=2)
-                nc.sync.dma_start(out=rows, in_=pairs[index // 2][:])
+            nc.sync.dma_start(out=out[n * P : (n + 1) * P, span], in_=results[index][:, cols])
 
         for part in range(2):
             round_x(part, pieces[0], nc.vector.tensor_copy)
             round_x(part, pieces[1], nc.scalar.copy)
             if part == 0:
                 quantise_eye(1)
-            for cols in pieces:
-                first_tier(part, cols)
-        for task in tensor_order():
+                for cols in pieces:
+                    first_tier(part, cols)
+        for task in queue:
             if task[0] == "back":
                 read_back_and_subtract(*task[1:])
                 behind_subtraction(*task[1:])

@@ -32,11 +32,12 @@ ONE = (0x3F80, 0x3F800000)
 WARM_UP = 5
 
 SECOND_WAVE = WAVE - 1
-PACE = 3
+NARROW_PACE = 4
+WIDE_PACE = 6
 
 
 def is_narrow(part):
-    return part < HALF_PARTS or part == PARTS - 1
+    return part < HALF_PARTS
 
 
 def place_of(part):
@@ -49,10 +50,6 @@ def sweep(half, a, tier, side=None, tiles=range(WAVE)):
     return [(half, n, a, tier, side) for n in tiles]
 
 
-def part_sweep(part, tier):
-    return sweep(0, part // 2, tier, part % 2)
-
-
 def whole_tile(half, n, side=None):
     return [(half, n, a, tier, side) for a in range(PASSES) for tier in range(TIERS)]
 
@@ -61,13 +58,27 @@ def tensor_order():
     def passes(work):
         return [("pass",) + step for step in work]
 
-    queue = []
-    for part in range(HALF_PARTS):
-        first, middle = passes(part_sweep(part, 0)), WAVE // 2 if part else 0
-        queue.extend([("back", part, 0)] + first[:middle] + [("back", part, 1)] + first[middle:])
-        if part:
-            queue.extend(passes(part_sweep(part - 1, 1)))
-    rest = part_sweep(HALF_PARTS - 1, 1)
+    def woven(part, work, middle):
+        return [("back", part, 0)] + passes(work[:middle]) + [("back", part, 1)] + passes(work[middle:])
+
+    def paced(work, parts, first, pace):
+        backs = [("back", part, s) for part in parts for s in range(2)]
+        woven_work, done, due = [], 0, first
+        for step in work:
+            done = done + (2 if step[-1] is None else 1)
+            if backs and done > due:
+                woven_work.append(backs[0])
+                backs, due = backs[1:], due + pace
+            woven_work.append(("pass",) + step)
+        return woven_work
+
+    middle = WAVE // 2
+    queue = woven(0, sweep(0, 0, 0, 0), 0)
+    queue.extend(woven(1, sweep(0, 0, 0, 1) + sweep(0, 0, 1, 0), middle))
+    queue.extend(woven(2, sweep(0, 0, 1, 1), 0))
+    queue.extend(woven(3, sweep(0, 1, 0), 2))
+    queue.extend(paced(sweep(0, 1, 1, 0) + sweep(0, 1, 1, 1) + sweep(0, 2, 0), (4, 5), middle, NARROW_PACE))
+    rest = sweep(0, 2, 1)
     for n in range(WAVE, N_TILES):
         rest.extend(whole_tile(0, n))
     for a in range(PASSES + 1):
@@ -79,14 +90,7 @@ def tensor_order():
         rest.extend(whole_tile(1, n))
     for side in range(2):
         rest.extend(whole_tile(1, N_TILES - 1, side))
-    backs = [("back", part, s) for part in range(HALF_PARTS, PARTS) for s in range(2)]
-    columns = 0
-    for step in rest:
-        if backs and columns % (PACE * BANK) == 0:
-            queue.append(backs[0])
-            backs = backs[1:]
-        queue.append(("pass",) + step)
-        columns = columns + (BANK if step[-1] is None else PART)
+    queue.extend(paced(rest, range(HALF_PARTS, PARTS), 0, WIDE_PACE))
     return queue
 
 
@@ -175,11 +179,12 @@ def tile_mix_tierx_none_kernel(tc, x, w4_words, w4_scales, out):
         def load_weights(a):
             for r in range(4):
                 nc.sync.dma_start(out=early_scale[a].bitcast(I32)[r:P:32, :], in_=scale_rows[r, :, a, : early // 4])
-            nc.sync.dma_start(out=w_early[a][:].bitcast(I32), in_=w4_words[a, :, : 2 * early].bitcast(I32))
+            for cols in (slice(0, early), slice(early, 2 * early)) if a == 0 else (slice(0, 2 * early),):
+                nc.sync.dma_start(out=w_early[a][:, cols].bitcast(I32), in_=w4_words[a, :, cols].bitcast(I32))
 
         for part in range(HALF_PARTS):
             load_x(raw_parts[part], *place_of(part), PART)
-            if part == 1 or (part and part % 2 == 0):
+            if part % 2:
                 load_weights(part // 2)
         for a in range(PASSES):
             load_x(raw_chunks[a], a, BANK, BANK)
@@ -251,19 +256,27 @@ def tile_mix_tierx_none_kernel(tc, x, w4_words, w4_scales, out):
                 out=target.rearrange("p (t u) -> p t u", u=2), in_=source.rearrange("p (u t) -> p t u", u=2)
             )
 
+        def spans(part):
+            return pieces if part <= 3 else (whole,)
+
         def behind_subtraction(part, s):
+            if s == 0 and part + 2 < PARTS:
+                for cols in spans(part + 2):
+                    round_x(part + 2, cols, nc.scalar.copy)
+            if s == (is_narrow(part) and part % 2) and part + 1 < PARTS:
+                for cols in spans(part + 1):
+                    first_tier(part + 1, cols)
             if s == 0:
-                if part + 2 < PARTS:
-                    round_x(part + 2, whole, nc.scalar.copy)
-                if part + 1 < PARTS:
-                    first_tier(part + 1, whole)
                 if part - 1 in wide:
                     join(part - 1)
                 return
             if part - 1 in wide:
                 second_tier(part - 1, whole)
+            if part == PARTS - 1:
+                join(part)
+                second_tier(part, whole)
             if is_narrow(part):
-                for cols in pieces:
+                for cols in (whole,) if part % 2 else pieces:
                     second_tier(part, cols)
 
         results = kept("result", HALVES * N_TILES + 1, [P, BANK], F32)

@@ -28,6 +28,7 @@ PARTS = HALVES * HALF_PARTS
 WAVE = 6
 ALIGN = 256
 RUN = 4
+LINE = 8
 ONE = (0x3F80, 0x3F800000)
 WARM_UP = 5
 
@@ -242,10 +243,11 @@ def tile_mix_tierx_none_kernel(tc, x, w4_words, w4_scales, out):
                     stop=True,
                 )
             target = rest[part][:, cols, :] if is_narrow(part) else unjoined[part][:, s, :, :]
+            run = LINE // len(rows)
             nc.vector.tensor_tensor(
-                out=target.rearrange("p (c i) j -> p c j i", i=RUN),
-                in0=raw[part][:, rows.start : rows.stop, cols].rearrange("p j (c i) -> p c j i", i=RUN),
-                in1=back[:].rearrange("p (j c i) -> p c j i", j=len(rows), i=RUN),
+                out=target.rearrange("p (c i) j -> p c j i", i=run),
+                in0=raw[part][:, rows.start : rows.stop, cols].rearrange("p j (c i) -> p c j i", i=run),
+                in1=back[:].rearrange("p (j c i) -> p c j i", j=len(rows), i=run),
                 op=mybir.AluOpType.subtract,
             )
 

@@ -32,9 +32,9 @@ LINE = 8
 ONE = (0x3F80, 0x3F800000)
 WARM_UP = 5
 
-SECOND_WAVE = WAVE - 1
-NARROW_PACE = 4
-WIDE_PACE = 6
+GUEST = WAVE
+PACE = 3
+TURN = 5
 
 
 def is_narrow(part):
@@ -59,39 +59,31 @@ def tensor_order():
     def passes(work):
         return [("pass",) + step for step in work]
 
-    def woven(part, work, middle):
-        return [("back", part, 0)] + passes(work[:middle]) + [("back", part, 1)] + passes(work[middle:])
-
-    def paced(work, parts, first, pace):
-        backs = [("back", part, s) for part in parts for s in range(2)]
-        woven_work, done, due = [], 0, first
-        for step in work:
-            done = done + (2 if step[-1] is None else 1)
-            if backs and done > due:
-                woven_work.append(backs[0])
-                backs, due = backs[1:], due + pace
-            woven_work.append(("pass",) + step)
-        return woven_work
-
-    middle = WAVE // 2
-    queue = woven(0, sweep(0, 0, 0, 0), 0)
-    queue.extend(woven(1, sweep(0, 0, 0, 1) + sweep(0, 0, 1, 0), middle))
-    queue.extend(woven(2, sweep(0, 0, 1, 1), 0))
-    queue.extend(woven(3, sweep(0, 1, 0), 2))
-    queue.extend(paced(sweep(0, 1, 1, 0) + sweep(0, 1, 1, 1) + sweep(0, 2, 0), (4, 5), middle, NARROW_PACE))
-    rest = sweep(0, 2, 1)
-    for n in range(WAVE, N_TILES):
+    queue = []
+    for part in range(HALF_PARTS):
+        first, middle = passes(sweep(0, part // 2, 0, part % 2)), WAVE // 2 if part else 0
+        queue.extend([("back", part, 0)] + first[:middle] + [("back", part, 1)] + first[middle:])
+        if 0 < part < HALF_PARTS - 1:
+            queue.extend(passes(sweep(0, (part - 1) // 2, 1, (part - 1) % 2)))
+    rest = whole_tile(0, GUEST) + sweep(0, PASSES - 1, 1)
+    for n in range(GUEST + 1, N_TILES):
         rest.extend(whole_tile(0, n))
     for a in range(PASSES + 1):
         if a < PASSES:
-            rest.extend(sweep(1, a, 0, tiles=range(SECOND_WAVE)))
+            rest.extend(sweep(1, a, 0))
         if a:
-            rest.extend(sweep(1, a - 1, 1, tiles=range(SECOND_WAVE)))
-    for n in range(SECOND_WAVE, N_TILES - 1):
+            rest.extend(sweep(1, a - 1, 1))
+    for n in range(WAVE, N_TILES - 1):
         rest.extend(whole_tile(1, n))
     for side in range(2):
         rest.extend(whole_tile(1, N_TILES - 1, side))
-    queue.extend(paced(rest, range(HALF_PARTS, PARTS), 0, WIDE_PACE))
+    backs = [("back", part, s) for part in range(HALF_PARTS, PARTS) for s in range(2)]
+    start = PASSES * TIERS - 2
+    places = [start] + [start + TURN + PACE * i for i in range(len(backs) - 1)]
+    for i, step in enumerate(rest):
+        if i in places:
+            queue.append(backs[places.index(i)])
+        queue.append(("pass",) + step)
     return queue
 
 
@@ -185,11 +177,11 @@ def tile_mix_tierx_none_kernel(tc, x, w4_words, w4_scales, out):
 
         for part in range(HALF_PARTS):
             load_x(raw_parts[part], *place_of(part), PART)
-            if part % 2:
+            if part == 1 or (part and part % 2 == 0):
                 load_weights(part // 2)
         for a in range(PASSES):
             load_x(raw_chunks[a], a, BANK, BANK)
-            if a == 1:
+            if a == 0:
                 words = w4_words[:, :, 2 * early :].bitcast(I32).rearrange("a p n -> p a n")
                 nc.sync.dma_start(out=w_late[:].bitcast(I32), in_=words)
                 for r in range(4):
@@ -231,7 +223,7 @@ def tile_mix_tierx_none_kernel(tc, x, w4_words, w4_scales, out):
         def read_back_and_subtract(part, s):
             cols, rows = (pieces[s], range(PACK)) if is_narrow(part) else (whole, range(2 * s, 2 * s + 2))
             a, width = place_of(part)[0], cols.stop - cols.start
-            back = bank_tile(WAVE + s)
+            back = bank_tile(WAVE + 1 if part == HALF_PARTS else WAVE + s)
             for i, j in enumerate(rows):
                 nc.tensor.matmul_mx(
                     out=back[:, i * width : (i + 1) * width],
@@ -259,16 +251,16 @@ def tile_mix_tierx_none_kernel(tc, x, w4_words, w4_scales, out):
             )
 
         def spans(part):
-            return pieces if part <= 3 else (whole,)
+            return pieces if part <= 2 else (whole,)
 
         def behind_subtraction(part, s):
-            if s == 0 and part + 2 < PARTS:
+            if s == (part > HALF_PARTS) and part + 2 < PARTS:
                 for cols in spans(part + 2):
                     round_x(part + 2, cols, nc.scalar.copy)
-            if s == (is_narrow(part) and part % 2) and part + 1 < PARTS:
-                for cols in spans(part + 1):
-                    first_tier(part + 1, cols)
             if s == 0:
+                if part + 1 < PARTS:
+                    for cols in spans(part + 1):
+                        first_tier(part + 1, cols)
                 if part - 1 in wide:
                     join(part - 1)
                 return
@@ -278,7 +270,7 @@ def tile_mix_tierx_none_kernel(tc, x, w4_words, w4_scales, out):
                 join(part)
                 second_tier(part, whole)
             if is_narrow(part):
-                for cols in (whole,) if part % 2 else pieces:
+                for cols in pieces:
                     second_tier(part, cols)
 
         results = kept("result", HALVES * N_TILES + 1, [P, BANK], F32)
@@ -298,7 +290,8 @@ def tile_mix_tierx_none_kernel(tc, x, w4_words, w4_scales, out):
             group = group_of(half, n, side)
             opens = group not in acc
             if opens:
-                acc[group] = bank_tile(len(acc) % WAVE)
+                guest = (0, GUEST, None)
+                acc[group] = bank_tile(WAVE if group == guest else len(set(acc) - {guest}) % WAVE)
             left[group] = left[group] - 1
             cols = side_columns(side)
             span = slice(half * BANK + cols.start, half * BANK + cols.stop)

@@ -38,7 +38,7 @@ TURN = 5
 
 
 def is_narrow(part):
-    return part < HALF_PARTS
+    return part < HALF_PARTS or part == PARTS - 1
 
 
 def place_of(part):
@@ -266,9 +266,6 @@ def tile_mix_tierx_none_kernel(tc, x, w4_words, w4_scales, out):
                 return
             if part - 1 in wide:
                 second_tier(part - 1, whole)
-            if part == PARTS - 1:
-                join(part)
-                second_tier(part, whole)
             if is_narrow(part):
                 for cols in pieces:
                     second_tier(part, cols)
@@ -314,7 +311,8 @@ def tile_mix_tierx_none_kernel(tc, x, w4_words, w4_scales, out):
             index = list(acc).index(group)
             cols = side_columns(side)
             span = slice(half * BANK + cols.start, half * BANK + cols.stop)
-            copy = nc.vector.tensor_copy if half and index % 2 else nc.scalar.copy
+            on_vector = index % 2 if half else n < WAVE and n % PACE == 0
+            copy = nc.vector.tensor_copy if on_vector else nc.scalar.copy
             copy(out=results[index][:, cols], in_=acc[group][:, cols])
             nc.sync.dma_start(out=out[n * P : (n + 1) * P, span], in_=results[index][:, cols])
 

@@ -68,11 +68,15 @@ def tensor_order():
     rest = whole_tile(0, GUEST) + sweep(0, PASSES - 1, 1)
     for n in range(GUEST + 1, N_TILES):
         rest.extend(whole_tile(0, n))
-    for a in range(PASSES + 1):
-        if a < PASSES:
-            rest.extend(sweep(1, a, 0))
-        if a:
-            rest.extend(sweep(1, a - 1, 1))
+    for a in range(PASSES):
+        rest.extend(sweep(1, a, 0))
+        if a == 1:
+            rest.extend(sweep(1, 0, 1))
+    ahead, closing = sweep(1, PASSES - 2, 1), sweep(1, PASSES - 1, 1)
+    for i in range(WAVE + WAVE // 2):
+        rest.extend(ahead[i : i + 1])
+        if i >= WAVE // 2:
+            rest.append(closing[i - WAVE // 2])
     for n in range(WAVE, N_TILES - 1):
         rest.extend(whole_tile(1, n))
     for side in range(2):
@@ -165,20 +169,36 @@ def tile_mix_tierx_none_kernel(tc, x, w4_words, w4_scales, out):
 
         scale_rows = w4_scales.bitcast(I32).rearrange("a (q r) n -> r q a n", r=4)
 
+        whole = slice(0, PART)
+        pieces = (slice(0, PIECE), slice(PIECE, PART))
+
         def load_x(target, a, t0, width):
             rows = x[a * P * PACK : (a + 1) * P * PACK, t0 : t0 + width]
             nc.sync.dma_start(out=target[:], in_=rows.rearrange("(p j) t -> p j t", j=PACK))
 
-        def load_weights(a):
+        def load_scales(a):
             for r in range(4):
                 nc.sync.dma_start(out=early_scale[a].bitcast(I32)[r:P:32, :], in_=scale_rows[r, :, a, : early // 4])
-            for cols in (slice(0, early), slice(early, 2 * early)) if a == 0 else (slice(0, 2 * early),):
-                nc.sync.dma_start(out=w_early[a][:, cols].bitcast(I32), in_=w4_words[a, :, cols].bitcast(I32))
+
+        def load_words(a, first, last):
+            cols = slice(2 * first * P, 2 * last * P)
+            nc.sync.dma_start(out=w_early[a][:, cols].bitcast(I32), in_=w4_words[a, :, cols].bitcast(I32))
 
         for part in range(HALF_PARTS):
-            load_x(raw_parts[part], *place_of(part), PART)
-            if part == 1 or (part and part % 2 == 0):
-                load_weights(part // 2)
+            a, t0 = place_of(part)
+            for cols in pieces if part == 2 else (whole,):
+                load_x(raw_parts[part][:, :, cols], a, t0 + cols.start, cols.stop - cols.start)
+            if part == 1:
+                load_scales(0)
+                load_words(0, 0, WAVE)
+            if part == 2:
+                load_scales(1)
+                load_words(1, 0, WAVE // 2)
+            if part == 3:
+                load_words(1, WAVE // 2, WAVE)
+            if part == 4:
+                load_scales(2)
+                load_words(2, 0, WAVE)
         for a in range(PASSES):
             load_x(raw_chunks[a], a, BANK, BANK)
             if a == 0:
@@ -192,9 +212,6 @@ def tile_mix_tierx_none_kernel(tc, x, w4_words, w4_scales, out):
                 m = n - WAVE
                 return w_late[:, a, 2 * m * P : 2 * (m + 1) * P], late_scale[:, a, m * P : (m + 1) * P]
             return w_early[a][:, 2 * n * P : 2 * (n + 1) * P], early_scale[a][:, n * P : (n + 1) * P]
-
-        whole = slice(0, PART)
-        pieces = (slice(0, PIECE), slice(PIECE, PART))
 
         def columns(part, cols):
             t0 = place_of(part)[1]
@@ -251,7 +268,7 @@ def tile_mix_tierx_none_kernel(tc, x, w4_words, w4_scales, out):
             )
 
         def spans(part):
-            return pieces if part <= 2 else (whole,)
+            return pieces if part <= 3 else (whole,)
 
         def behind_subtraction(part, s):
             if s == (part > HALF_PARTS) and part + 2 < PARTS:

@@ -34,11 +34,16 @@ WARM_UP = 5
 
 GUEST = WAVE
 PACE = 3
+SHARE = 80
 TURN = 5
 
 
 def is_narrow(part):
-    return part < HALF_PARTS or part == PARTS - 1
+    return (part < HALF_PARTS and part != HALF_PARTS - 2) or part == PARTS - 1
+
+
+def scalar_joins(part):
+    return part < HALF_PARTS or part >= HALF_PARTS + 2
 
 
 def place_of(part):
@@ -65,6 +70,9 @@ def tensor_order():
         queue.extend([("back", part, 0)] + first[:middle] + [("back", part, 1)] + first[middle:])
         if 0 < part < HALF_PARTS - 1:
             queue.extend(passes(sweep(0, (part - 1) // 2, 1, (part - 1) % 2)))
+    for s in range(2):
+        at = queue.index(("back", HALF_PARTS - 1, s))
+        queue = queue[: at - 1] + [queue[at], queue[at - 1]] + queue[at + 1 :]
     rest = whole_tile(0, GUEST) + sweep(0, PASSES - 1, 1)
     for n in range(GUEST + 1, N_TILES):
         rest.extend(whole_tile(0, n))
@@ -150,7 +158,8 @@ def tile_mix_tierx_none_kernel(tc, x, w4_words, w4_scales, out):
                 in_=eye_rows[u][:].rearrange("p e w -> p (e w)").bitcast(BF16),
             )
 
-        quantise_eye(0)
+        for u in range(2):
+            quantise_eye(u)
 
         w_early = kept("w_early", PASSES, [P, 2 * early], U8)
         w_late = keep.tile([P, PASSES, 2 * late], U8, align_bytes=ALIGN)
@@ -185,12 +194,11 @@ def tile_mix_tierx_none_kernel(tc, x, w4_words, w4_scales, out):
             nc.sync.dma_start(out=w_early[a][:, cols].bitcast(I32), in_=w4_words[a, :, cols].bitcast(I32))
 
         for part in range(HALF_PARTS):
-            a, t0 = place_of(part)
-            for cols in pieces if part == 2 else (whole,):
-                load_x(raw_parts[part][:, :, cols], a, t0 + cols.start, cols.stop - cols.start)
+            load_x(raw_parts[part], *place_of(part), PART)
             if part == 1:
                 load_scales(0)
-                load_words(0, 0, WAVE)
+                load_words(0, 0, WAVE // 2)
+                load_words(0, WAVE // 2, WAVE)
             if part == 2:
                 load_scales(1)
                 load_words(1, 0, WAVE // 2)
@@ -260,12 +268,10 @@ def tile_mix_tierx_none_kernel(tc, x, w4_words, w4_scales, out):
                 op=mybir.AluOpType.subtract,
             )
 
-        def join(part):
-            source = unjoined[part][:].rearrange("p u t e -> p (u t e)").bitcast(I32)
-            target = rest[part][:].rearrange("p t j -> p (t j)").bitcast(I32)
-            nc.vector.tensor_copy(
-                out=target.rearrange("p (t u) -> p t u", u=2), in_=source.rearrange("p (u t) -> p t u", u=2)
-            )
+        def join(part, copy):
+            source = unjoined[part][:].rearrange("p u t e -> p (u t e)").bitcast(U32)
+            target = rest[part][:].rearrange("p t j -> p (t j)").bitcast(U32)
+            copy(out=target.rearrange("p (t u) -> p t u", u=2), in_=source.rearrange("p (u t) -> p t u", u=2))
 
         def spans(part):
             return pieces if part <= 3 else (whole,)
@@ -273,16 +279,22 @@ def tile_mix_tierx_none_kernel(tc, x, w4_words, w4_scales, out):
         def behind_subtraction(part, s):
             if s == (part > HALF_PARTS) and part + 2 < PARTS:
                 for cols in spans(part + 2):
+                    if part == 0 and cols == pieces[1]:
+                        cols = slice(PART - PIECE // 2, PART)
                     round_x(part + 2, cols, nc.scalar.copy)
             if s == 0:
+                if part == 1:
+                    round_x(2, slice(PIECE, PART - PIECE // 2), nc.vector.tensor_copy)
                 if part + 1 < PARTS:
                     for cols in spans(part + 1):
                         first_tier(part + 1, cols)
-                if part - 1 in wide:
-                    join(part - 1)
+                if part - 1 in wide and not scalar_joins(part - 1):
+                    join(part - 1, nc.vector.tensor_copy)
                 return
             if part - 1 in wide:
                 second_tier(part - 1, whole)
+            if part in wide and scalar_joins(part):
+                join(part, nc.scalar.copy)
             if is_narrow(part):
                 for cols in pieces:
                     second_tier(part, cols)
@@ -333,13 +345,13 @@ def tile_mix_tierx_none_kernel(tc, x, w4_words, w4_scales, out):
             copy(out=results[index][:, cols], in_=acc[group][:, cols])
             nc.sync.dma_start(out=out[n * P : (n + 1) * P, span], in_=results[index][:, cols])
 
-        for part in range(2):
-            round_x(part, pieces[0], nc.vector.tensor_copy)
-            round_x(part, pieces[1], nc.scalar.copy)
-            if part == 0:
-                quantise_eye(1)
-                for cols in pieces:
-                    first_tier(part, cols)
+        for cols in pieces:
+            round_x(0, slice(cols.start, cols.start + SHARE), nc.vector.tensor_copy)
+            round_x(0, slice(cols.start + SHARE, cols.stop), nc.scalar.copy)
+        for cols in pieces:
+            first_tier(0, cols)
+        round_x(1, pieces[0], nc.vector.tensor_copy)
+        round_x(1, pieces[1], nc.scalar.copy)
         for task in queue:
             if task[0] == "back":
                 read_back_and_subtract(*task[1:])

@@ -34,7 +34,9 @@ WARM_UP = 5
 
 GUEST = WAVE
 PACE = 3
-SHARE = 80
+SHARE = 88
+SECOND = 4
+SKEW = 4
 TURN = 5
 
 
@@ -66,7 +68,7 @@ def tensor_order():
 
     queue = []
     for part in range(HALF_PARTS):
-        first, middle = passes(sweep(0, part // 2, 0, part % 2)), WAVE // 2 if part else 0
+        first, middle = passes(sweep(0, part // 2, 0, part % 2)), SECOND if part else 0
         queue.extend([("back", part, 0)] + first[:middle] + [("back", part, 1)] + first[middle:])
         if 0 < part < HALF_PARTS - 1:
             queue.extend(passes(sweep(0, (part - 1) // 2, 1, (part - 1) % 2)))
@@ -81,10 +83,10 @@ def tensor_order():
         if a == 1:
             rest.extend(sweep(1, 0, 1))
     ahead, closing = sweep(1, PASSES - 2, 1), sweep(1, PASSES - 1, 1)
-    for i in range(WAVE + WAVE // 2):
+    for i in range(WAVE + SKEW):
         rest.extend(ahead[i : i + 1])
-        if i >= WAVE // 2:
-            rest.append(closing[i - WAVE // 2])
+        if i >= SKEW:
+            rest.append(closing[i - SKEW])
     for n in range(WAVE, N_TILES - 1):
         rest.extend(whole_tile(1, n))
     for side in range(2):
@@ -136,13 +138,13 @@ def tile_mix_tierx_none_kernel(tc, x, w4_words, w4_scales, out):
         nc.gpsimd.iota(
             ramp[:], pattern=[[1, 2 * P]], base=0, channel_multiplier=-2, allow_small_or_imprecise_dtypes=True
         )
-        eye_rows = kept("eye_rows", 2, [P, 2, 2 * P], I32)
+        eye_rows = keep.tile([P, PACK, 2 * P], I32, align_bytes=ALIGN)
         eye_code = keep.tile([P, PACK * P], U32, align_bytes=ALIGN)
         eye_scale = keep.tile([P, PACK * P], U8, align_bytes=ALIGN)
         for u in range(2):
             for e in range(2):
                 nc.vector.tensor_scalar(
-                    out=eye_rows[u][:, e, :],
+                    out=eye_rows[:, 2 * u + e, :],
                     in0=ramp[:],
                     scalar1=float(u),
                     scalar2=float(ONE[e]),
@@ -150,16 +152,11 @@ def tile_mix_tierx_none_kernel(tc, x, w4_words, w4_scales, out):
                     op1=mybir.AluOpType.mult,
                 )
 
-        def quantise_eye(u):
-            blocks = slice(u * 2 * P, (u + 1) * 2 * P)
-            nc.vector.quantize_mx(
-                out=eye_code[:, blocks].bitcast(E4M3),
-                scales=eye_scale[:, blocks],
-                in_=eye_rows[u][:].rearrange("p e w -> p (e w)").bitcast(BF16),
-            )
-
-        for u in range(2):
-            quantise_eye(u)
+        nc.vector.quantize_mx(
+            out=eye_code[:].bitcast(E4M3),
+            scales=eye_scale[:],
+            in_=eye_rows[:].rearrange("p j w -> p (j w)").bitcast(BF16),
+        )
 
         w_early = kept("w_early", PASSES, [P, 2 * early], U8)
         w_late = keep.tile([P, PASSES, 2 * late], U8, align_bytes=ALIGN)
@@ -350,7 +347,8 @@ def tile_mix_tierx_none_kernel(tc, x, w4_words, w4_scales, out):
             round_x(0, slice(cols.start + SHARE, cols.stop), nc.scalar.copy)
         for cols in pieces:
             first_tier(0, cols)
-        round_x(1, pieces[0], nc.vector.tensor_copy)
+        round_x(1, slice(0, SHARE), nc.vector.tensor_copy)
+        round_x(1, slice(SHARE, PIECE), nc.scalar.copy)
         round_x(1, pieces[1], nc.scalar.copy)
         for task in queue:
             if task[0] == "back":

from contextlib import ExitStack

import concourse.mybir as mybir

K, N, T = 1536, 1024, 1024
FLOPS = 2 * 2 * K * N * T

F32 = mybir.dt.float32
BF16 = mybir.dt.bfloat16
I32 = mybir.dt.int32
U32 = mybir.dt.uint32
U8 = mybir.dt.uint8
E4M3 = mybir.dt.float8_e4m3fn_x4
E5M2 = mybir.dt.float8_e5m2_x4
E2M1 = mybir.dt.float4_e2m1fn_x4

P = 128
PACK = 4
PASSES = K // (P * PACK)
TIERS = 2
N_TILES = N // P
BANK = 512
PART = BANK // 2
PIECE = PART // 2
HALVES = T // BANK
HALF_PARTS = 2 * PASSES
PARTS = HALVES * HALF_PARTS
WAVE = 6
ALIGN = 256
RUN = 4
LINE = 8
ONE = (0x3F80, 0x3F800000)
WARM_UP = 5

GUEST = WAVE
PACE = 3
SHARE = 88
SECOND = 4
SKEW = 4
TURN = 5


def is_narrow(part):
    return (part < HALF_PARTS and part != HALF_PARTS - 2) or part == PARTS - 1


def scalar_joins(part):
    return part < HALF_PARTS or part >= HALF_PARTS + 2


def place_of(part):
    chunk, side = divmod(part, 2)
    half, a = divmod(chunk, PASSES)
    return a, half * BANK + side * PART


def sweep(half, a, tier, side=None, tiles=range(WAVE)):
    return [(half, n, a, tier, side) for n in tiles]


def whole_tile(half, n, side=None):
    return [(half, n, a, tier, side) for a in range(PASSES) for tier in range(TIERS)]


def tensor_order():
    def passes(work):
        return [("pass",) + step for step in work]

    queue = []
    for part in range(HALF_PARTS):
        first, middle = passes(sweep(0, part // 2, 0, part % 2)), SECOND if part else 0
        queue.extend([("back", part, 0)] + first[:middle] + [("back", part, 1)] + first[middle:])
        if 0 < part < HALF_PARTS - 1:
            queue.extend(passes(sweep(0, (part - 1) // 2, 1, (part - 1) % 2)))
    for s in range(2):
        at = queue.index(("back", HALF_PARTS - 1, s))
        queue = queue[: at - 1] + [queue[at], queue[at - 1]] + queue[at + 1 :]
    rest = whole_tile(0, GUEST) + sweep(0, PASSES - 1, 1)
    for n in range(GUEST + 1, N_TILES):
        rest.extend(whole_tile(0, n))
    for a in range(PASSES):
        rest.extend(sweep(1, a, 0))
        if a == 1:
            rest.extend(sweep(1, 0, 1))
    ahead, closing = sweep(1, PASSES - 2, 1), sweep(1, PASSES - 1, 1)
    for i in range(WAVE + SKEW):
        rest.extend(ahead[i : i + 1])
        if i >= SKEW:
            rest.append(closing[i - SKEW])
    for n in range(WAVE, N_TILES - 1):
        rest.extend(whole_tile(1, n))
    for side in range(2):
        rest.extend(whole_tile(1, N_TILES - 1, side))
    backs = [("back", part, s) for part in range(HALF_PARTS, PARTS) for s in range(2)]
    start = PASSES * TIERS - 2
    places = [start] + [start + TURN + PACE * i for i in range(len(backs) - 1)]
    for i, step in enumerate(rest):
        if i in places:
            queue.append(backs[places.index(i)])
        queue.append(("pass",) + step)
    return queue


def tile_mix_tierx_none_kernel(tc, x, w4_words, w4_scales, out):
    nc = tc.nc
    with ExitStack() as ctx:
        keep = ctx.enter_context(tc.tile_pool(name="keep", bufs=1))
        psum = ctx.enter_context(tc.psum_pool(name="psum", bufs=1))
        ctx.enter_context(tc.manual_schedule())

        def bank_tile(bank):
            return psum.tile([P, BANK], F32, name="bank%d" % bank)

        def kept(name, count, shape, dtype):
            return [keep.tile(shape, dtype, align_bytes=ALIGN, name="%s%d" % (name, i)) for i in range(count)]

        early, late = WAVE * P, (N_TILES - WAVE) * P
        planes = kept("planes", PASSES - 1, [P, early], U8)
        last_planes = keep.tile([P, early + PASSES * late], U8, align_bytes=ALIGN)
        for plane in [last_planes] + planes:
            nc.vector.memset(plane[:].bitcast(U32), 0)
        early_scale = [plane[:] for plane in planes] + [last_planes[:, :early]]
        late_scale = last_planes[:, early:].rearrange("p (a n) -> p a n", a=PASSES)

        unread = bank_tile(0)
        for turn in range(WARM_UP):
            nc.tensor.matmul_mx(
                out=unread[:],
                lhsT=last_planes[:, : PACK * P].bitcast(E4M3),
                lhsT_scale=last_planes[:, :P],
                rhs=last_planes[:, : 2 * BANK].bitcast(E2M1),
                rhs_scale=last_planes[:, :BANK],
                start=True,
                stop=True,
            )

        ramp = keep.tile([P, 2 * P], F32, align_bytes=ALIGN)
        nc.gpsimd.iota(
            ramp[:], pattern=[[1, 2 * P]], base=0, channel_multiplier=-2, allow_small_or_imprecise_dtypes=True
        )
        eye_rows = keep.tile([P, PACK, 2 * P], I32, align_bytes=ALIGN)
        eye_code = keep.tile([P, PACK * P], U32, align_bytes=ALIGN)
        eye_scale = keep.tile([P, PACK * P], U8, align_bytes=ALIGN)
        for u in range(2):
            for e in range(2):
                nc.vector.tensor_scalar(
                    out=eye_rows[:, 2 * u + e, :],
                    in0=ramp[:],
                    scalar1=float(u),
                    scalar2=float(ONE[e]),
                    op0=mybir.AluOpType.is_equal,
                    op1=mybir.AluOpType.mult,
                )

        nc.vector.quantize_mx(
            out=eye_code[:].bitcast(E4M3),
            scales=eye_scale[:],
            in_=eye_rows[:].rearrange("p j w -> p (j w)").bitcast(BF16),
        )

        w_early = kept("w_early", PASSES, [P, 2 * early], U8)
        w_late = keep.tile([P, PASSES, 2 * late], U8, align_bytes=ALIGN)
        raw_parts = kept("raw_part", HALF_PARTS, [P, PACK, PART], F32)
        raw_chunks = kept("raw_chunk", PASSES, [P, PACK, BANK], F32)
        raw = [tile[:] for tile in raw_parts]
        raw.extend([tile[:, :, side * PART : (side + 1) * PART] for tile in raw_chunks for side in range(2)])
        rounded = kept("rounded", PARTS, [P, PART, PACK], BF16)
        rest = kept("rest", PARTS, [P, PART, PACK], BF16)
        wide = [part for part in range(PARTS) if not is_narrow(part)]
        unjoined = dict(zip(wide, kept("unjoined", len(wide), [P, 2, PART, 2], BF16)))
        q_code = kept("q_code", PASSES, [P, T], U32)
        q_scale = kept("q_scale", PASSES, [P, T], U8)
        r_code = kept("r_code", PASSES, [P, T], U32)
        r_scale = kept("r_scale", PASSES, [P, T], U8)

        scale_rows = w4_scales.bitcast(I32).rearrange("a (q r) n -> r q a n", r=4)

        whole = slice(0, PART)
        pieces = (slice(0, PIECE), slice(PIECE, PART))

        def load_x(target, a, t0, width):
            rows = x[a * P * PACK : (a + 1) * P * PACK, t0 : t0 + width]
            nc.sync.dma_start(out=target[:], in_=rows.rearrange("(p j) t -> p j t", j=PACK))

        def load_scales(a):
            for r in range(4):
                nc.sync.dma_start(out=early_scale[a].bitcast(I32)[r:P:32, :], in_=scale_rows[r, :, a, : early // 4])

        def load_words(a, first, last):
            cols = slice(2 * first * P, 2 * last * P)
            nc.sync.dma_start(out=w_early[a][:, cols].bitcast(I32), in_=w4_words[a, :, cols].bitcast(I32))

        for part in range(HALF_PARTS):
            load_x(raw_parts[part], *place_of(part), PART)
            if part == 1:
                load_scales(0)
                load_words(0, 0, WAVE // 2)
                load_words(0, WAVE // 2, WAVE)
            if part == 2:
                load_scales(1)
                load_words(1, 0, WAVE // 2)
            if part == 3:
                load_words(1, WAVE // 2, WAVE)
            if part == 4:
                load_scales(2)
                load_words(2, 0, WAVE)
        for a in range(PASSES):
            load_x(raw_chunks[a], a, BANK, BANK)
            if a == 0:
                words = w4_words[:, :, 2 * early :].bitcast(I32).rearrange("a p n -> p a n")
                nc.sync.dma_start(out=w_late[:].bitcast(I32), in_=words)
                for r in range(4):
                    nc.sync.dma_start(out=late_scale.bitcast(I32)[r:P:32], in_=scale_rows[r, :, :, early // 4 :])

        def weights(a, n):
            if n >= WAVE:
                m = n - WAVE
                return w_late[:, a, 2 * m * P : 2 * (m + 1) * P], late_scale[:, a, m * P : (m + 1) * P]
            return w_early[a][:, 2 * n * P : 2 * (n + 1) * P], early_scale[a][:, n * P : (n + 1) * P]

        def columns(part, cols):
            t0 = place_of(part)[1]
            return slice(t0 + cols.start, t0 + cols.stop)

        def round_x(part, cols, copy):
            copy(
                out=rounded[part][:, cols, :].rearrange("p (c i) j -> p c j i", i=RUN),
                in_=raw[part][:, :, cols].rearrange("p j (c i) -> p c j i", i=RUN),
            )

        def quantise(part, cols, source, code, scale, dtype):
            a = place_of(part)[0]
            nc.vector.quantize_mx(
                out=code[a][:, columns(part, cols)].bitcast(dtype),
                scales=scale[a][:, columns(part, cols)],
                in_=source[part][:, cols, :].rearrange("p t j -> p (t j)"),
            )

        def first_tier(part, cols):
            quantise(part, cols, rounded, q_code, q_scale, E4M3)

        def second_tier(part, cols):
            quantise(part, cols, rest, r_code, r_scale, E5M2)

        def read_back_and_subtract(part, s):
            cols, rows = (pieces[s], range(PACK)) if is_narrow(part) else (whole, range(2 * s, 2 * s + 2))
            a, width = place_of(part)[0], cols.stop - cols.start
            back = bank_tile(WAVE + 1 if part == HALF_PARTS else WAVE + s)
            for i, j in enumerate(rows):
                nc.tensor.matmul_mx(
                    out=back[:, i * width : (i + 1) * width],
                    lhsT=eye_code[:, j * P : (j + 1) * P].bitcast(E4M3),
                    lhsT_scale=eye_scale[:, j * P : (j + 1) * P],
                    rhs=q_code[a][:, columns(part, cols)].bitcast(E4M3),
                    rhs_scale=q_scale[a][:, columns(part, cols)],
                    start=True,
                    stop=True,
                )
            target = rest[part][:, cols, :] if is_narrow(part) else unjoined[part][:, s, :, :]
            run = LINE // len(rows)
            nc.vector.tensor_tensor(
                out=target.rearrange("p (c i) j -> p c j i", i=run),
                in0=raw[part][:, rows.start : rows.stop, cols].rearrange("p j (c i) -> p c j i", i=run),
                in1=back[:].rearrange("p (j c i) -> p c j i", j=len(rows), i=run),
                op=mybir.AluOpType.subtract,
            )

        def join(part, copy):
            source = unjoined[part][:].rearrange("p u t e -> p (u t e)").bitcast(U32)
            target = rest[part][:].rearrange("p t j -> p (t j)").bitcast(U32)
            copy(out=target.rearrange("p (t u) -> p t u", u=2), in_=source.rearrange("p (u t) -> p t u", u=2))

        def spans(part):
            return pieces if part <= 3 else (whole,)

        def behind_subtraction(part, s):
            if s == (part > HALF_PARTS) and part + 2 < PARTS:
                for cols in spans(part + 2):
                    if part == 0 and cols == pieces[1]:
                        cols = slice(PART - PIECE // 2, PART)
                    round_x(part + 2, cols, nc.scalar.copy)
            if s == 0:
                if part == 1:
                    round_x(2, slice(PIECE, PART - PIECE // 2), nc.vector.tensor_copy)
                if part + 1 < PARTS:
                    for cols in spans(part + 1):
                        first_tier(part + 1, cols)
                if part - 1 in wide and not scalar_joins(part - 1):
                    join(part - 1, nc.vector.tensor_copy)
                return
            if part - 1 in wide:
                second_tier(part - 1, whole)
            if part in wide and scalar_joins(part):
                join(part, nc.scalar.copy)
            if is_narrow(part):
                for cols in pieces:
                    second_tier(part, cols)

        results = kept("result", HALVES * N_TILES + 1, [P, BANK], F32)

        def group_of(half, n, side):
            return (half, n, side if (half, n) == (HALVES - 1, N_TILES - 1) else None)

        queue = tensor_order()
        groups = [group_of(task[1], task[2], task[-1]) for task in queue if task[0] == "pass"]
        left = {group: groups.count(group) for group in groups}
        acc = {}

        def side_columns(side):
            return slice(0, BANK) if side is None else slice(side * PART, (side + 1) * PART)

        def main_pass(half, n, a, tier, side):
            group = group_of(half, n, side)
            opens = group not in acc
            if opens:
                guest = (0, GUEST, None)
                acc[group] = bank_tile(WAVE if group == guest else len(set(acc) - {guest}) % WAVE)
            left[group] = left[group] - 1
            cols = side_columns(side)
            span = slice(half * BANK + cols.start, half * BANK + cols.stop)
            code, scale, dtype = (r_code, r_scale, E5M2) if tier else (q_code, q_scale, E4M3)
            words, scales = weights(a, n)
            nc.tensor.matmul_mx(
                out=acc[group][:, cols],
                lhsT=words.bitcast(E2M1),
                lhsT_scale=scales,
                rhs=code[a][:, span].bitcast(dtype),
                rhs_scale=scale[a][:, span],
                start=opens,
                stop=left[group] == 0,
            )
            if left[group] == 0:
                empty(group)

        def empty(group):
            half, n, side = group
            index = list(acc).index(group)
            cols = side_columns(side)
            span = slice(half * BANK + cols.start, half * BANK + cols.stop)
            on_vector = index % 2 if half else n < WAVE and n % PACE == 0
            copy = nc.vector.tensor_copy if on_vector else nc.scalar.copy
            copy(out=results[index][:, cols], in_=acc[group][:, cols])
            nc.sync.dma_start(out=out[n * P : (n + 1) * P, span], in_=results[index][:, cols])

        for cols in pieces:
            round_x(0, slice(cols.start, cols.start + SHARE), nc.vector.tensor_copy)
            round_x(0, slice(cols.start + SHARE, cols.stop), nc.scalar.copy)
        for cols in pieces:
            first_tier(0, cols)
        round_x(1, slice(0, SHARE), nc.vector.tensor_copy)
        round_x(1, slice(SHARE, PIECE), nc.scalar.copy)
        round_x(1, pieces[1], nc.scalar.copy)
        for task in queue:
            if task[0] == "back":
                read_back_and_subtract(*task[1:])
                behind_subtraction(*task[1:])
            else:
                main_pass(*task[1:])
